import numpy as np
import ml_dtypes


def mxq(x, axis, fmt="e4m3"):
    dtype, down = {"e4m3": (ml_dtypes.float8_e4m3fn, 7), "e5m2": (ml_dtypes.float8_e5m2, 14)}[fmt]
    v = np.moveaxis(np.asarray(x, np.float32).astype(ml_dtypes.bfloat16).astype(np.float64), axis, -1)
    blocks = v.reshape(v.shape[:-1] + (-1, 32))
    amax = np.abs(blocks).max(-1, keepdims=True)
    byte = np.maximum(np.where(amax > 0, np.frexp(amax)[1] - 1 + 127, 0) - down, 1)
    scale = np.exp2(byte - 127.0)
    codes = (blocks / scale).astype(np.float32).astype(dtype).astype(np.float64)
    return np.moveaxis((codes * scale).reshape(v.shape), -1, axis)


WIDE = False


def mx_kscale(k):
    if not WIDE:
        return np.ones(k)
    levels = np.array([24, -24, 12, -12, 0])
    if k % 512:
        return np.exp2(np.random.permutation(np.resize(levels, k // 32))).repeat(32)
    a = np.empty((k // 512, 16))
    for p in range(k // 512):
        a[p, :8] = np.random.permutation(np.resize(levels, 8))
        for g in range(8):
            far = levels[np.abs(levels - a[p, g]) >= 10]
            a[p, g + 8] = far[np.random.randint(len(far))]
    return np.exp2(a.ravel()).repeat(32)


def f64(x):
    return np.asarray(x).astype(np.float64)


def striped(idx):
    return np.tile(idx.reshape(-1, 16).T, (8, 1)).astype(np.uint16)


def unstriped(offs):
    return offs[:16].T.reshape(-1).astype(np.int64)


E2M1 = np.array([0.0, 0.5, 1.0, 1.5, 2.0, 3.0, 4.0, 6.0, -0.0, -0.5, -1.0, -1.5, -2.0, -3.0, -4.0, -6.0])


def pack_weight(w, fmt):
    k, n = w.shape
    w = f64(np.asarray(w, np.float32).astype(ml_dtypes.bfloat16)).reshape(k // 32, 32, n)
    amax = np.abs(w).max(1)
    if fmt == "e4m3":
        byte = np.frexp(amax)[1] - 1 + 127 - 7
    else:
        mant, ex = np.frexp(amax / 6.0)
        byte = np.where(mant > 0.5, ex, ex - 1) + 127
    byte = np.clip(np.where(amax > 0, byte, 1), 1, 254)
    scaled = (w * np.exp2(127.0 - byte)[:, None, :]).reshape(k, n).astype(np.float32)
    by_word = np.ascontiguousarray(scaled.reshape(k // 512, 128, 4, n).transpose(0, 1, 3, 2))
    if fmt == "e4m3":
        words = by_word.astype(ml_dtypes.float8_e4m3fn).view(np.uint8)
    else:
        c = by_word.astype(ml_dtypes.float4_e2m1fn).view(np.uint8) & 0xF
        words = (c[..., 0::2] | (c[..., 1::2] << 4)).reshape(k // 512, 128, 2 * n)
    return np.ascontiguousarray(words), np.ascontiguousarray(byte.astype(np.uint8).reshape(k // 512, 16, n))


def unpack_weight(words, scales, fmt):
    g, _, n = scales.shape
    words = np.ascontiguousarray(words).reshape(g, 128, n, -1)
    if fmt == "e4m3":
        vals = words.view(ml_dtypes.float8_e4m3fn).astype(np.float64)
    else:
        nib = np.empty((g, 128, n, 4), np.uint8)
        nib[..., 0::2] = words & 0xF
        nib[..., 1::2] = words >> 4
        vals = E2M1[nib]
    vals = vals * np.repeat(np.exp2(scales.astype(np.float64) - 127.0), 8, axis=1)[..., None]
    return vals.transpose(0, 1, 3, 2).reshape(g * 512, n)


def pack_table4(v):
    words, scales = pack_weight(v, "e2m1")
    g, t = words.shape[0] // 2, v.shape[1]
    return np.ascontiguousarray(words.reshape(g, 2, 128, t, 2).transpose(0, 2, 3, 1, 4).reshape(g, 128, t, 4)), scales


def unpack_table4(words, scales):
    g, _, t, _ = words.shape
    return unpack_weight(words.reshape(g, 128, t, 2, 2).transpose(0, 3, 1, 2, 4).reshape(2 * g, 128, 2 * t), scales, "e2m1")


def gelu(f):
    return 0.5 * f * (1.0 + np.tanh(np.sqrt(2.0 / np.pi) * (f + 0.044715 * f**3)))


K, R, N, T, J = 1024, 512, 512, 2048, 1024


def setup_inputs():
    n = np.random.standard_normal
    s = mx_kscale(K)[:, None]
    u = mx_kscale(R)[:, None]
    wd = n((R, N)) / np.sqrt(R) / u
    wd4 = pack_weight(wd, "e2m1")
    wdrest = wd - unpack_weight(*wd4, "e2m1")
    p_tab = pack_table4(n((K, T)) * s)
    p_wd8 = pack_weight(wdrest, "e4m3")
    return {
        "tab_words": p_tab[0],
        "tab_scales": p_tab[1],
        "ws": (n((K, R)) / np.sqrt(2 * K) / s).astype(np.float32),
        "wt": (n((K, R)) / np.sqrt(2 * K) / s).astype(np.float32),
        "sm": (np.random.uniform(0.5, 2.0, R) * u[:, 0]).astype(np.float32),
        "wd4_words": wd4[0],
        "wd4_scales": wd4[1],
        "wd8_words": p_wd8[0],
        "wd8_scales": p_wd8[1],
        "rT": (n((N, T))).astype(np.float32),
        "wgo": np.tile(np.random.uniform(0.5, 2.0, J), (128, 1)).astype(np.float32),
        "offs": striped(np.random.permutation(T)[:J]),
        "offs2": striped(np.random.permutation(T)[:J]),
    }


def reference(tab_words, tab_scales, ws, wt, sm, wd4_words, wd4_scales, wd8_words, wd8_scales, rT, wgo, offs, offs2):
    idx = unstriped(offs)
    idx2 = unstriped(offs2)
    tab_ = unpack_table4(tab_words, tab_scales)[:, idx]
    tabb_ = unpack_table4(tab_words, tab_scales)[:, idx2]
    ws_ = mxq(f64(ws), 0, "e4m3")
    wt_ = mxq(f64(wt), 0, "e4m3")
    a = ws_.T @ tab_ + wt_.T @ tabb_
    h = f64(sm)[:, None] * gelu(a)
    h_ = mxq(h, 0, "e4m3")
    wd4_ = unpack_weight(wd4_words, wd4_scales, "e2m1")
    wd8_ = unpack_weight(wd8_words, wd8_scales, "e4m3")
    y = wd4_.T @ h_ + wd8_.T @ h_
    out = np.zeros((N, T))
    out[:, idx2] = f64(wgo)[0] * (y + f64(rT)[:, idx2])
    return out

@@ -1,0 +1,220 @@
+from contextlib import ExitStack
+
+import concourse.mybir as mybir
+from concourse.masks import make_identity
+
+K, R, N, T, J = 1024, 512, 512, 2048, 1024
+FLOPS = 2 * J * (2 * K * R + 2 * R * N)
+
+F32 = mybir.dt.float32
+BF16 = mybir.dt.bfloat16
+I32 = mybir.dt.int32
+U32 = mybir.dt.uint32
+U16 = mybir.dt.uint16
+U8 = mybir.dt.uint8
+FP8X4 = mybir.dt.float8_e4m3fn_x4
+FP4X4 = mybir.dt.float4_e2m1fn_x4
+GELU = mybir.ActivationFunctionType.Gelu_apprx_tanh
+COPY = mybir.ActivationFunctionType.Copy
+MULT = mybir.AluOpType.mult
+
+P = 128
+PACK = 4
+K_PASS = P * PACK
+PASSES = K // K_PASS
+QUADS = 4
+CHUNKS = J // P
+N_TILES = N // P
+HALF = J // 2
+HALF_CHUNKS = CHUNKS // 2
+WINDOWS = 3
+
+
+def tile_list_msg_gelu_res_resL_kernel(
+    tc, tab_words, tab_scales, ws, wt, sm, wd4_words, wd4_scales, wd8_words, wd8_scales, rT, wgo, offs, offs2, out
+):
+    nc = tc.nc
+    with ExitStack() as ctx:
+        lists = ctx.enter_context(tc.tile_pool(name="lists", bufs=1))
+        keep = ctx.enter_context(tc.tile_pool(name="keep", bufs=1))
+        ring2 = ctx.enter_context(tc.tile_pool(name="ring2", bufs=2))
+        ring3 = ctx.enter_context(tc.tile_pool(name="ring3", bufs=3))
+        psum = ctx.enter_context(tc.psum_pool(name="psum", bufs=2))
+
+        src_list = lists.tile([P, J // 16], U16, name="src_list")
+        dst_list = lists.tile([P, J // 16], U16, name="dst_list")
+        both = (src_list, dst_list)
+
+        tab_w = keep.tile([P, T], I32, name="tab_w", align_bytes=64)
+        tab_s = keep.tile([P, T], U8, name="tab_s", tag="tables", align_bytes=64)
+        wd_s = keep.tile([P, 2, N], U8, name="wd_s", align_bytes=64)
+        plane1 = keep.tile([P, 2 * J], U8, name="plane1", align_bytes=64)
+        nc.vector.memset(plane1[:].bitcast(I32), 0)
+        windows = [keep.tile([P, T], F32, name="window%d" % i) for i in range(WINDOWS)]
+        for i in range(WINDOWS):
+            nc.vector.memset(windows[i][:], 0.0)
+
+        warm_in = keep.tile([P, 1], F32, name="warm_in")
+        warm_out = keep.tile([P, 1], F32, name="warm_out")
+        nc.gpsimd.memset(warm_in[:], 0.0)
+        nc.scalar.activation(warm_out[:], warm_in[:], GELU)
+
+        nc.sync.dma_start(src_list[:], offs)
+        scale_rows = tab_scales.rearrange("a q t -> (a q) t").bitcast(I32)
+        nc.sync.dma_start(
+            out=tab_s[0:112, :].bitcast(I32), in_=scale_rows[0:28, :].unsqueeze(0).broadcast_to([4, 28, T // 4])
+        )
+        nc.sync.dma_start(
+            out=tab_s[112:P, :].bitcast(I32), in_=scale_rows[28:32, :].unsqueeze(0).broadcast_to([4, 4, T // 4])
+        )
+        nc.sync.dma_start(dst_list[:], offs2)
+        w_raw = []
+        for i, w in enumerate((ws, wt)):
+            for a in range(PASSES):
+                raw = keep.tile([P, PACK, R], F32, name="w_raw%d%d" % (i, a))
+                nc.sync.dma_start(
+                    out=raw[:], in_=w[a * K_PASS : (a + 1) * K_PASS, :].rearrange("(p i) r -> p i r", i=PACK)
+                )
+                w_raw.append(raw)
+                if len(w_raw) == 1:
+                    nc.sync.dma_start(out=tab_w[:], in_=tab_words[0].rearrange("p t b -> p (t b)").bitcast(I32))
+        wd4 = keep.tile([P, 2 * N], U8, name="wd4", align_bytes=64)
+        wd8 = keep.tile([P, N], I32, name="wd8", align_bytes=64)
+        nc.sync.dma_start(out=wd4[:].bitcast(I32), in_=wd4_words[0].bitcast(I32))
+        nc.sync.dma_start(out=wd8[:], in_=wd8_words[0].rearrange("p n b -> p (n b)").bitcast(I32))
+
+        ident = keep.tile([P, P], F32, name="ident")
+        make_identity(nc, ident[:])
+        sm_t = keep.tile([P, PACK], F32, name="sm_t")
+        nc.gpsimd.dma_start(out=sm_t[:], in_=sm.rearrange("(p t) -> p t", t=PACK))
+        wgo_rows = keep.tile([P, P], F32, name="wgo_rows")
+        nc.gpsimd.dma_start(
+            out=wgo_rows[:], in_=wgo[0 : P // CHUNKS, :].rearrange("g (c p) -> (g c) p", p=P)
+        )
+
+        plane0 = keep.tile([P, 2 * J], U8, name="plane0", align_bytes=64)
+        for i in range(2):
+            nc.vector.tensor_copy(plane0[:, i * J : (i + 1) * J], tab_s[:].indirect(both[i][:]))
+        nc.sync.dma_start(out=plane1[0 : P - 16, :].bitcast(I32), in_=plane0[16:P, :].bitcast(I32))
+        res = keep.tile([P, N_TILES, T], F32, name="res", tag="tables", align_bytes=64)
+        for nt in range(N_TILES):
+            nc.sync.dma_start(out=res[:, nt, :], in_=rT[nt * P : (nt + 1) * P, :])
+        planes = (plane0, plane1)
+        for i, scales in enumerate((wd4_scales, wd8_scales)):
+            rows = scales[0].bitcast(I32)
+            nc.gpsimd.dma_start(
+                out=wd_s[0:98, i, :].bitcast(I32), in_=rows[0:14, :].unsqueeze(0).broadcast_to([7, 14, N // 4])
+            )
+            nc.gpsimd.dma_start(
+                out=wd_s[98:P, i, :].bitcast(I32), in_=rows[14:16, :].unsqueeze(0).broadcast_to([15, 2, N // 4])
+            )
+
+        picked = [keep.tile([P, J], U32, name="picked%d" % i) for i in range(2)]
+        parted = [keep.tile([P, PASSES * 2 * J], U8, name="parted%d" % i, align_bytes=64) for i in range(2)]
+        for i in range(2):
+            nc.vector.tensor_copy(picked[i][:], tab_w[:].bitcast(U32).indirect(both[i][:]))
+        for i in range(2):
+            nc.vector.tensor_copy(
+                parted[i][:].bitcast(U16).rearrange("p (d j) -> p d j", d=PASSES),
+                picked[i][:].bitcast(U16).rearrange("p (j d) -> p d j", d=PASSES),
+            )
+
+        wgo_ps = psum.tile([P, P], F32, name="wgo_ps", tag="z")
+        nc.tensor.transpose(wgo_ps[:], wgo_rows[:], ident[:])
+        wgo_col = keep.tile([P, CHUNKS], F32, name="wgo_col")
+        nc.scalar.copy(wgo_col[:], wgo_ps[:, 0:CHUNKS])
+
+        w_codes = keep.tile([P, 2 * PASSES, R], U32, name="w_codes", align_bytes=64)
+        w_scales = keep.tile([P, 2 * PASSES, R], U8, name="w_scales", align_bytes=64)
+        for u in range(2 * PASSES):
+            grouped = ring2.tile([P, R * PACK], BF16, name="grouped", align_bytes=64)
+            nc.scalar.copy(
+                grouped[:].rearrange("p (t m i) -> p m i t", t=PACK, i=PACK),
+                w_raw[u][:].rearrange("p i (m t) -> p m i t", t=PACK),
+            )
+            nc.vector.quantize_mx(out=w_codes[:, u, :].bitcast(FP8X4), scales=w_scales[:, u, :], in_=grouped[:])
+
+        h_codes = keep.tile([P, J], U32, name="h_codes", align_bytes=64)
+        h_scales = keep.tile([P, J], U8, name="h_scales", align_bytes=64)
+        msg_t = [keep.tile([P, N], F32, name="msg_t%d" % c) for c in range(CHUNKS)]
+        res_t = [keep.tile([P, N], F32, name="res_t%d" % c) for c in range(CHUNKS)]
+        g = [keep.tile([P, J], F32, name="g%d" % nt) for nt in range(N_TILES)]
+
+        def message(c):
+            cols = slice(c * P, (c + 1) * P)
+            a_ps = psum.tile([P, PACK, P], F32, name="a_ps", tag="a")
+            for t in range(PACK):
+                for u in range(2 * PASSES):
+                    i, a = divmod(u, PASSES)
+                    start = (a * J + c * P) * 2
+                    nc.tensor.matmul_mx(
+                        out=a_ps[:, t, :],
+                        lhsT=w_codes[:, u, t * P : (t + 1) * P].bitcast(FP8X4),
+                        lhsT_scale=w_scales[:, u, t * P : (t + 1) * P],
+                        rhs=parted[i][:, start : start + 2 * P].bitcast(FP4X4),
+                        rhs_scale=planes[a][:, i * J + c * P : i * J + (c + 1) * P],
+                        start=(u == 0),
+                        stop=(u == 2 * PASSES - 1),
+                    )
+            act = ring3.tile([P, P, PACK], F32, name="act")
+            nc.scalar.activation(act[:], a_ps[:].rearrange("p t j -> p j t"), GELU)
+            h = ring3.tile([P, P, PACK], BF16, name="h", align_bytes=64)
+            nc.vector.tensor_tensor(h[:], act[:], sm_t[:].unsqueeze(1).to_broadcast([P, P, PACK]), MULT)
+            nc.vector.quantize_mx(
+                out=h_codes[:, cols].bitcast(FP8X4), scales=h_scales[:, cols], in_=h[:].rearrange("p j t -> p (j t)")
+            )
+            y_ps = psum.tile([P, N], F32, name="y_ps", tag="y")
+            nc.tensor.matmul_mx(
+                out=y_ps[:], lhsT=h_codes[:, cols].bitcast(FP8X4), lhsT_scale=h_scales[:, cols],
+                rhs=wd4[:].bitcast(FP4X4), rhs_scale=wd_s[:, 0, :], start=True, stop=False,
+            )
+            nc.tensor.matmul_mx(
+                out=y_ps[:], lhsT=h_codes[:, cols].bitcast(FP8X4), lhsT_scale=h_scales[:, cols],
+                rhs=wd8[:].bitcast(FP8X4), rhs_scale=wd_s[:, 1, :], start=False, stop=True,
+            )
+            nc.scalar.activation(msg_t[c][:], y_ps[:], COPY, scale=wgo_col[:, c : c + 1])
+
+        def residual(half):
+            for nt in range(N_TILES):
+                nc.vector.tensor_copy(
+                    g[nt][:, half * HALF : (half + 1) * HALF],
+                    res[:, nt, :].indirect(dst_list[:, half * HALF // 16 : (half + 1) * HALF // 16]),
+                )
+            for c in range(half * HALF_CHUNKS, (half + 1) * HALF_CHUNKS):
+                g_ps = psum.tile([P, N], F32, name="g_ps", tag="g")
+                for nt in range(N_TILES):
+                    nc.tensor.transpose(g_ps[:, nt * P : (nt + 1) * P], g[nt][:, c * P : (c + 1) * P], ident[:])
+                nc.scalar.activation(res_t[c][:], g_ps[:], COPY, scale=wgo_col[:, c : c + 1])
+
+        z = {}
+
+        def total(nt, half):
+            z_ps = psum.tile([P, HALF], F32, name="z_ps", tag="z")
+            rows = slice(nt * P, (nt + 1) * P)
+            for s in range(HALF_CHUNKS):
+                c = half * HALF_CHUNKS + s
+                nc.tensor.matmul(z_ps[:, s * P : (s + 1) * P], lhsT=res_t[c][:, rows], rhs=ident[:],
+                                 start=True, stop=False, is_transpose=True)
+                nc.tensor.matmul(z_ps[:, s * P : (s + 1) * P], lhsT=msg_t[c][:, rows], rhs=ident[:],
+                                 start=False, stop=True, is_transpose=True)
+            z[nt, half] = keep.tile([P, HALF], F32, name="z%d%d" % (nt, half))
+            nc.scalar.copy(z[nt, half][:], z_ps[:])
+
+        def place(nt, half):
+            nc.vector.tensor_copy(
+                windows[nt % WINDOWS][:].indirect(dst_list[:, half * HALF // 16 : (half + 1) * HALF // 16]), z[nt, half][:]
+            )
+
+        for c in range(HALF_CHUNKS):
+            message(c)
+        residual(0)
+        for c in range(HALF_CHUNKS, CHUNKS):
+            total(c - HALF_CHUNKS, 0)
+            message(c)
+        residual(1)
+        for nt in range(N_TILES):
+            total(nt, 1)
+        for nt in range(N_TILES):
+            place(nt, 0)
+            place(nt, 1)
+            nc.sync.dma_start(out=out[nt * P : (nt + 1) * P, :], in_=windows[nt % WINDOWS][:])

@@ -1,7 +1,6 @@
 from contextlib import ExitStack
 
 import concourse.mybir as mybir
-from concourse.masks import make_identity
 
 K, R, N, T, J = 1024, 512, 512, 2048, 1024
 FLOPS = 2 * J * (2 * K * R + 2 * R * N)
@@ -17,6 +16,7 @@ FP4X4 = mybir.dt.float4_e2m1fn_x4
 GELU = mybir.ActivationFunctionType.Gelu_apprx_tanh
 COPY = mybir.ActivationFunctionType.Copy
 MULT = mybir.AluOpType.mult
+ADD = mybir.AluOpType.add
 
 P = 128
 PACK = 4
@@ -28,6 +28,7 @@ N_TILES = N // P
 HALF = J // 2
 HALF_CHUNKS = CHUNKS // 2
 WINDOWS = 3
+QUARTER = HALF // 2
 
 
 def tile_list_msg_gelu_res_resL_kernel(
@@ -39,13 +40,13 @@ def tile_list_msg_gelu_res_resL_kernel(
         keep = ctx.enter_context(tc.tile_pool(name="keep", bufs=1))
         ring2 = ctx.enter_context(tc.tile_pool(name="ring2", bufs=2))
         ring3 = ctx.enter_context(tc.tile_pool(name="ring3", bufs=3))
-        psum = ctx.enter_context(tc.psum_pool(name="psum", bufs=2))
+        psum = ctx.enter_context(tc.psum_pool(name="psum", bufs=4))
 
         src_list = lists.tile([P, J // 16], U16, name="src_list")
         dst_list = lists.tile([P, J // 16], U16, name="dst_list")
         both = (src_list, dst_list)
 
-        tab_w = keep.tile([P, T], I32, name="tab_w", align_bytes=64)
+        tab_w = keep.tile([P, T], I32, name="tab_w", tag="tab_w", align_bytes=64)
         tab_s = keep.tile([P, T], U8, name="tab_s", tag="tables", align_bytes=64)
         wd_s = keep.tile([P, 2, N], U8, name="wd_s", align_bytes=64)
         plane1 = keep.tile([P, 2 * J], U8, name="plane1", align_bytes=64)
@@ -71,26 +72,16 @@ def tile_list_msg_gelu_res_resL_kernel(
         w_raw = []
         for i, w in enumerate((ws, wt)):
             for a in range(PASSES):
-                raw = keep.tile([P, PACK, R], F32, name="w_raw%d%d" % (i, a))
+                raw = keep.tile([P, PACK, R], F32, name="w_raw", tag="w_raw%d%d" % (i, a), align_bytes=64)
                 nc.sync.dma_start(
                     out=raw[:], in_=w[a * K_PASS : (a + 1) * K_PASS, :].rearrange("(p i) r -> p i r", i=PACK)
                 )
                 w_raw.append(raw)
                 if len(w_raw) == 1:
                     nc.sync.dma_start(out=tab_w[:], in_=tab_words[0].rearrange("p t b -> p (t b)").bitcast(I32))
-        wd4 = keep.tile([P, 2 * N], U8, name="wd4", align_bytes=64)
-        wd8 = keep.tile([P, N], I32, name="wd8", align_bytes=64)
-        nc.sync.dma_start(out=wd4[:].bitcast(I32), in_=wd4_words[0].bitcast(I32))
-        nc.sync.dma_start(out=wd8[:], in_=wd8_words[0].rearrange("p n b -> p (n b)").bitcast(I32))
 
-        ident = keep.tile([P, P], F32, name="ident")
-        make_identity(nc, ident[:])
         sm_t = keep.tile([P, PACK], F32, name="sm_t")
         nc.gpsimd.dma_start(out=sm_t[:], in_=sm.rearrange("(p t) -> p t", t=PACK))
-        wgo_rows = keep.tile([P, P], F32, name="wgo_rows")
-        nc.gpsimd.dma_start(
-            out=wgo_rows[:], in_=wgo[0 : P // CHUNKS, :].rearrange("g (c p) -> (g c) p", p=P)
-        )
 
         plane0 = keep.tile([P, 2 * J], U8, name="plane0", align_bytes=64)
         for i in range(2):
@@ -119,11 +110,6 @@ def tile_list_msg_gelu_res_resL_kernel(
                 picked[i][:].bitcast(U16).rearrange("p (j d) -> p d j", d=PASSES),
             )
 
-        wgo_ps = psum.tile([P, P], F32, name="wgo_ps", tag="z")
-        nc.tensor.transpose(wgo_ps[:], wgo_rows[:], ident[:])
-        wgo_col = keep.tile([P, CHUNKS], F32, name="wgo_col")
-        nc.scalar.copy(wgo_col[:], wgo_ps[:, 0:CHUNKS])
-
         w_codes = keep.tile([P, 2 * PASSES, R], U32, name="w_codes", align_bytes=64)
         w_scales = keep.tile([P, 2 * PASSES, R], U8, name="w_scales", align_bytes=64)
         for u in range(2 * PASSES):
@@ -134,86 +120,79 @@ def tile_list_msg_gelu_res_resL_kernel(
             )
             nc.vector.quantize_mx(out=w_codes[:, u, :].bitcast(FP8X4), scales=w_scales[:, u, :], in_=grouped[:])
 
+        wd4 = keep.tile([P, 2 * N], U8, name="wd4", tag="w_raw00", align_bytes=64)
+        wd8 = keep.tile([P, N], I32, name="wd8", tag="w_raw01", align_bytes=64)
+        nc.sync.dma_start(out=wd4[:].bitcast(I32), in_=wd4_words[0].bitcast(I32))
+        nc.sync.dma_start(out=wd8[:], in_=wd8_words[0].rearrange("p n b -> p (n b)").bitcast(I32))
+        edge_w = keep.tile([P, J], F32, name="edge_w", tag="tab_w", align_bytes=64)
+        nc.sync.dma_start(out=edge_w[:], in_=wgo)
+
         h_codes = keep.tile([P, J], U32, name="h_codes", align_bytes=64)
         h_scales = keep.tile([P, J], U8, name="h_scales", align_bytes=64)
-        msg_t = [keep.tile([P, N], F32, name="msg_t%d" % c) for c in range(CHUNKS)]
-        res_t = [keep.tile([P, N], F32, name="res_t%d" % c) for c in range(CHUNKS)]
         g = [keep.tile([P, J], F32, name="g%d" % nt) for nt in range(N_TILES)]
 
-        def message(c):
-            cols = slice(c * P, (c + 1) * P)
-            a_ps = psum.tile([P, PACK, P], F32, name="a_ps", tag="a")
+        def hidden(half):
+            first = half * HALF
+            planar = ring2.tile([P, PACK, HALF], BF16, name="planar")
             for t in range(PACK):
+                a_ps = psum.tile([P, HALF], F32, name="a_ps")
                 for u in range(2 * PASSES):
                     i, a = divmod(u, PASSES)
-                    start = (a * J + c * P) * 2
+                    start = (a * J + first) * 2
                     nc.tensor.matmul_mx(
-                        out=a_ps[:, t, :],
+                        out=a_ps[:],
                         lhsT=w_codes[:, u, t * P : (t + 1) * P].bitcast(FP8X4),
                         lhsT_scale=w_scales[:, u, t * P : (t + 1) * P],
-                        rhs=parted[i][:, start : start + 2 * P].bitcast(FP4X4),
-                        rhs_scale=planes[a][:, i * J + c * P : i * J + (c + 1) * P],
+                        rhs=parted[i][:, start : start + 2 * HALF].bitcast(FP4X4),
+                        rhs_scale=planes[a][:, i * J + first : i * J + first + HALF],
                         start=(u == 0),
                         stop=(u == 2 * PASSES - 1),
                     )
-            act = ring3.tile([P, P, PACK], F32, name="act")
-            nc.scalar.activation(act[:], a_ps[:].rearrange("p t j -> p j t"), GELU)
-            h = ring3.tile([P, P, PACK], BF16, name="h", align_bytes=64)
-            nc.vector.tensor_tensor(h[:], act[:], sm_t[:].unsqueeze(1).to_broadcast([P, P, PACK]), MULT)
-            nc.vector.quantize_mx(
-                out=h_codes[:, cols].bitcast(FP8X4), scales=h_scales[:, cols], in_=h[:].rearrange("p j t -> p (j t)")
+                act = ring2.tile([P, HALF], F32, name="act")
+                nc.scalar.activation(act[:], a_ps[:], GELU)
+                nc.scalar.activation(planar[:, t, :], act[:], COPY, scale=sm_t[:, t : t + 1])
+            h = ring2.tile([P, HALF * PACK], BF16, name="h", align_bytes=64)
+            nc.scalar.copy(
+                h[:].rearrange("p (c i t) -> p c t i", i=4, t=PACK),
+                planar[:].rearrange("p t (c i) -> p c t i", i=4),
             )
-            y_ps = psum.tile([P, N], F32, name="y_ps", tag="y")
-            nc.tensor.matmul_mx(
-                out=y_ps[:], lhsT=h_codes[:, cols].bitcast(FP8X4), lhsT_scale=h_scales[:, cols],
-                rhs=wd4[:].bitcast(FP4X4), rhs_scale=wd_s[:, 0, :], start=True, stop=False,
-            )
-            nc.tensor.matmul_mx(
-                out=y_ps[:], lhsT=h_codes[:, cols].bitcast(FP8X4), lhsT_scale=h_scales[:, cols],
-                rhs=wd8[:].bitcast(FP8X4), rhs_scale=wd_s[:, 1, :], start=False, stop=True,
-            )
-            nc.scalar.activation(msg_t[c][:], y_ps[:], COPY, scale=wgo_col[:, c : c + 1])
-
-        def residual(half):
-            for nt in range(N_TILES):
-                nc.vector.tensor_copy(
-                    g[nt][:, half * HALF : (half + 1) * HALF],
-                    res[:, nt, :].indirect(dst_list[:, half * HALF // 16 : (half + 1) * HALF // 16]),
-                )
-            for c in range(half * HALF_CHUNKS, (half + 1) * HALF_CHUNKS):
-                g_ps = psum.tile([P, N], F32, name="g_ps", tag="g")
-                for nt in range(N_TILES):
-                    nc.tensor.transpose(g_ps[:, nt * P : (nt + 1) * P], g[nt][:, c * P : (c + 1) * P], ident[:])
-                nc.scalar.activation(res_t[c][:], g_ps[:], COPY, scale=wgo_col[:, c : c + 1])
+            cols = slice(first, first + HALF)
+            nc.vector.quantize_mx(out=h_codes[:, cols].bitcast(FP8X4), scales=h_scales[:, cols], in_=h[:])
 
         z = {}
 
         def total(nt, half):
-            z_ps = psum.tile([P, HALF], F32, name="z_ps", tag="z")
-            rows = slice(nt * P, (nt + 1) * P)
-            for s in range(HALF_CHUNKS):
-                c = half * HALF_CHUNKS + s
-                nc.tensor.matmul(z_ps[:, s * P : (s + 1) * P], lhsT=res_t[c][:, rows], rhs=ident[:],
-                                 start=True, stop=False, is_transpose=True)
-                nc.tensor.matmul(z_ps[:, s * P : (s + 1) * P], lhsT=msg_t[c][:, rows], rhs=ident[:],
-                                 start=False, stop=True, is_transpose=True)
+            cols = slice(half * HALF, (half + 1) * HALF)
+            y_ps = psum.tile([P, HALF], F32, name="y_ps")
+            nc.tensor.matmul_mx(
+                out=y_ps[:], lhsT=wd4[:, 2 * nt * P : 2 * (nt + 1) * P].bitcast(FP4X4),
+                lhsT_scale=wd_s[:, 0, nt * P : (nt + 1) * P],
+                rhs=h_codes[:, cols].bitcast(FP8X4), rhs_scale=h_scales[:, cols], start=True, stop=False,
+            )
+            nc.tensor.matmul_mx(
+                out=y_ps[:], lhsT=wd8[:, nt * P : (nt + 1) * P].bitcast(FP8X4),
+                lhsT_scale=wd_s[:, 1, nt * P : (nt + 1) * P],
+                rhs=h_codes[:, cols].bitcast(FP8X4), rhs_scale=h_scales[:, cols], start=False, stop=True,
+            )
             z[nt, half] = keep.tile([P, HALF], F32, name="z%d%d" % (nt, half))
-            nc.scalar.copy(z[nt, half][:], z_ps[:])
+            nc.vector.tensor_tensor(z[nt, half][:], y_ps[:], g[nt][:, cols], ADD)
 
         def place(nt, half):
-            nc.vector.tensor_copy(
-                windows[nt % WINDOWS][:].indirect(dst_list[:, half * HALF // 16 : (half + 1) * HALF // 16]), z[nt, half][:]
+            cols = slice(half * HALF, (half + 1) * HALF)
+            nc.vector.tensor_tensor(
+                windows[nt % WINDOWS][:].indirect(dst_list[:, half * HALF // 16 : (half + 1) * HALF // 16]),
+                z[nt, half][:],
+                edge_w[:, cols],
+                MULT,
             )
 
-        for c in range(HALF_CHUNKS):
-            message(c)
-        residual(0)
-        for c in range(HALF_CHUNKS, CHUNKS):
-            total(c - HALF_CHUNKS, 0)
-            message(c)
-        residual(1)
+        for half in range(2):
+            hidden(half)
         for nt in range(N_TILES):
-            total(nt, 1)
+            nc.vector.tensor_copy(g[nt][:], res[:, nt, :].indirect(dst_list[:]))
+        for half in range(2):
+            for nt in range(N_TILES):
+                total(nt, half)
         for nt in range(N_TILES):
             place(nt, 0)
             place(nt, 1)

@@ -27,8 +27,7 @@ CHUNKS = J // P
 N_TILES = N // P
 HALF = J // 2
 HALF_CHUNKS = CHUNKS // 2
-WINDOWS = 3
-QUARTER = HALF // 2
+WINDOWS = 4
 
 
 def tile_list_msg_gelu_res_resL_kernel(
@@ -40,7 +39,8 @@ def tile_list_msg_gelu_res_resL_kernel(
         keep = ctx.enter_context(tc.tile_pool(name="keep", bufs=1))
         ring2 = ctx.enter_context(tc.tile_pool(name="ring2", bufs=2))
         ring3 = ctx.enter_context(tc.tile_pool(name="ring3", bufs=3))
-        psum = ctx.enter_context(tc.psum_pool(name="psum", bufs=4))
+        psum_a = ctx.enter_context(tc.psum_pool(name="psum_a", bufs=6))
+        psum_y = ctx.enter_context(tc.psum_pool(name="psum_y", bufs=2))
 
         src_list = lists.tile([P, J // 16], U16, name="src_list")
         dst_list = lists.tile([P, J // 16], U16, name="dst_list")
@@ -50,34 +50,37 @@ def tile_list_msg_gelu_res_resL_kernel(
         tab_s = keep.tile([P, T], U8, name="tab_s", tag="tables", align_bytes=64)
         wd_s = keep.tile([P, 2, N], U8, name="wd_s", align_bytes=64)
         plane1 = keep.tile([P, 2 * J], U8, name="plane1", align_bytes=64)
+        nc.vector.memset(tab_s[:].bitcast(I32), 0)
+        warm_in = keep.tile([P, 1], F32, name="warm_in")
+        nc.vector.memset(warm_in[:], 0.0)
         nc.vector.memset(plane1[:].bitcast(I32), 0)
         windows = [keep.tile([P, T], F32, name="window%d" % i) for i in range(WINDOWS)]
-        for i in range(WINDOWS):
+        for i in range(WINDOWS - 1):
             nc.vector.memset(windows[i][:], 0.0)
 
-        warm_in = keep.tile([P, 1], F32, name="warm_in")
-        warm_out = keep.tile([P, 1], F32, name="warm_out")
-        nc.gpsimd.memset(warm_in[:], 0.0)
-        nc.scalar.activation(warm_out[:], warm_in[:], GELU)
-
         nc.sync.dma_start(src_list[:], offs)
-        scale_rows = tab_scales.rearrange("a q t -> (a q) t").bitcast(I32)
-        nc.sync.dma_start(
-            out=tab_s[0:112, :].bitcast(I32), in_=scale_rows[0:28, :].unsqueeze(0).broadcast_to([4, 28, T // 4])
-        )
-        nc.sync.dma_start(
-            out=tab_s[112:P, :].bitcast(I32), in_=scale_rows[28:32, :].unsqueeze(0).broadcast_to([4, 4, T // 4])
-        )
         nc.sync.dma_start(dst_list[:], offs2)
-        w_raw = []
-        for i, w in enumerate((ws, wt)):
+        for q in range(QUADS):
+            nc.scalar.dma_start(
+                out=tab_s[32 * q : 32 * q + 8, :].bitcast(I32),
+                in_=tab_scales[:, 4 * q : 4 * q + 4, :].bitcast(I32),
+            )
+        warm_out = keep.tile([P, 1], F32, name="warm_out")
+        nc.scalar.activation(warm_out[:], warm_in[:], GELU)
+        grouped = []
+        for w in (ws, wt):
             for a in range(PASSES):
-                raw = keep.tile([P, PACK, R], F32, name="w_raw", tag="w_raw%d%d" % (i, a), align_bytes=64)
+                raw = ring3.tile([P, PACK, R], F32, name="raw")
                 nc.sync.dma_start(
                     out=raw[:], in_=w[a * K_PASS : (a + 1) * K_PASS, :].rearrange("(p i) r -> p i r", i=PACK)
                 )
-                w_raw.append(raw)
-                if len(w_raw) == 1:
+                rounded = keep.tile([P, R * PACK], BF16, name="rounded%d" % len(grouped), align_bytes=64)
+                nc.scalar.copy(
+                    rounded[:].rearrange("p (t m i) -> p m i t", t=PACK, i=PACK),
+                    raw[:].rearrange("p i (m t) -> p m i t", t=PACK),
+                )
+                grouped.append(rounded)
+                if len(grouped) == 1:
                     nc.sync.dma_start(out=tab_w[:], in_=tab_words[0].rearrange("p t b -> p (t b)").bitcast(I32))
 
         sm_t = keep.tile([P, PACK], F32, name="sm_t")
@@ -86,7 +89,7 @@ def tile_list_msg_gelu_res_resL_kernel(
         plane0 = keep.tile([P, 2 * J], U8, name="plane0", align_bytes=64)
         for i in range(2):
             nc.vector.tensor_copy(plane0[:, i * J : (i + 1) * J], tab_s[:].indirect(both[i][:]))
-        nc.sync.dma_start(out=plane1[0 : P - 16, :].bitcast(I32), in_=plane0[16:P, :].bitcast(I32))
+        nc.sync.dma_start(out=plane1[0:112, :].bitcast(I32), in_=plane0[4:116, :].bitcast(I32))
         res = keep.tile([P, N_TILES, T], F32, name="res", tag="tables", align_bytes=64)
         for nt in range(N_TILES):
             nc.sync.dma_start(out=res[:, nt, :], in_=rT[nt * P : (nt + 1) * P, :])
@@ -99,8 +102,9 @@ def tile_list_msg_gelu_res_resL_kernel(
             nc.gpsimd.dma_start(
                 out=wd_s[98:P, i, :].bitcast(I32), in_=rows[14:16, :].unsqueeze(0).broadcast_to([15, 2, N // 4])
             )
+        nc.gpsimd.memset(windows[WINDOWS - 1][:], 0.0)
 
-        picked = [keep.tile([P, J], U32, name="picked%d" % i) for i in range(2)]
+        picked = [keep.tile([P, J], U32, name="picked", tag="picked%d" % i, align_bytes=64) for i in range(2)]
         parted = [keep.tile([P, PASSES * 2 * J], U8, name="parted%d" % i, align_bytes=64) for i in range(2)]
         for i in range(2):
             nc.vector.tensor_copy(picked[i][:], tab_w[:].bitcast(U32).indirect(both[i][:]))
@@ -113,15 +117,10 @@ def tile_list_msg_gelu_res_resL_kernel(
         w_codes = keep.tile([P, 2 * PASSES, R], U32, name="w_codes", align_bytes=64)
         w_scales = keep.tile([P, 2 * PASSES, R], U8, name="w_scales", align_bytes=64)
         for u in range(2 * PASSES):
-            grouped = ring2.tile([P, R * PACK], BF16, name="grouped", align_bytes=64)
-            nc.scalar.copy(
-                grouped[:].rearrange("p (t m i) -> p m i t", t=PACK, i=PACK),
-                w_raw[u][:].rearrange("p i (m t) -> p m i t", t=PACK),
-            )
-            nc.vector.quantize_mx(out=w_codes[:, u, :].bitcast(FP8X4), scales=w_scales[:, u, :], in_=grouped[:])
+            nc.vector.quantize_mx(out=w_codes[:, u, :].bitcast(FP8X4), scales=w_scales[:, u, :], in_=grouped[u][:])
 
-        wd4 = keep.tile([P, 2 * N], U8, name="wd4", tag="w_raw00", align_bytes=64)
-        wd8 = keep.tile([P, N], I32, name="wd8", tag="w_raw01", align_bytes=64)
+        wd4 = keep.tile([P, 2 * N], U8, name="wd4", tag="picked0", align_bytes=64)
+        wd8 = keep.tile([P, N], I32, name="wd8", tag="picked1", align_bytes=64)
         nc.sync.dma_start(out=wd4[:].bitcast(I32), in_=wd4_words[0].bitcast(I32))
         nc.sync.dma_start(out=wd8[:], in_=wd8_words[0].rearrange("p n b -> p (n b)").bitcast(I32))
         edge_w = keep.tile([P, J], F32, name="edge_w", tag="tab_w", align_bytes=64)
@@ -131,23 +130,42 @@ def tile_list_msg_gelu_res_resL_kernel(
         h_scales = keep.tile([P, J], U8, name="h_scales", align_bytes=64)
         g = [keep.tile([P, J], F32, name="g%d" % nt) for nt in range(N_TILES)]
 
+        def project(a_ps, t, first, width):
+            for u in range(2 * PASSES):
+                i, a = divmod(u, PASSES)
+                start = (a * J + first) * 2
+                nc.tensor.matmul_mx(
+                    out=a_ps,
+                    lhsT=w_codes[:, u, t * P : (t + 1) * P].bitcast(FP8X4),
+                    lhsT_scale=w_scales[:, u, t * P : (t + 1) * P],
+                    rhs=parted[i][:, start : start + 2 * width].bitcast(FP4X4),
+                    rhs_scale=planes[a][:, i * J + first : i * J + first + width],
+                    start=(u == 0),
+                    stop=(u == 2 * PASSES - 1),
+                )
+
+        def hidden_first():
+            h = ring2.tile([P, HALF * PACK], BF16, name="h", align_bytes=64)
+            for c in range(HALF_CHUNKS):
+                a_ps = psum_a.tile([P, PACK, P], F32, name="a_ps")
+                for t in range(PACK):
+                    project(a_ps[:, t, :], t, c * P, P)
+                act = ring3.tile([P, P, PACK], F32, name="act4")
+                nc.scalar.activation(act[:], a_ps[:].rearrange("p t j -> p j t"), GELU)
+                nc.gpsimd.tensor_tensor(
+                    h[:, c * P * PACK : (c + 1) * P * PACK].rearrange("p (j t) -> p j t", t=PACK),
+                    act[:],
+                    sm_t[:].unsqueeze(1).to_broadcast([P, P, PACK]),
+                    MULT,
+                )
+            nc.vector.quantize_mx(out=h_codes[:, 0:HALF].bitcast(FP8X4), scales=h_scales[:, 0:HALF], in_=h[:])
+
         def hidden(half):
             first = half * HALF
             planar = ring2.tile([P, PACK, HALF], BF16, name="planar")
             for t in range(PACK):
-                a_ps = psum.tile([P, HALF], F32, name="a_ps")
-                for u in range(2 * PASSES):
-                    i, a = divmod(u, PASSES)
-                    start = (a * J + first) * 2
-                    nc.tensor.matmul_mx(
-                        out=a_ps[:],
-                        lhsT=w_codes[:, u, t * P : (t + 1) * P].bitcast(FP8X4),
-                        lhsT_scale=w_scales[:, u, t * P : (t + 1) * P],
-                        rhs=parted[i][:, start : start + 2 * HALF].bitcast(FP4X4),
-                        rhs_scale=planes[a][:, i * J + first : i * J + first + HALF],
-                        start=(u == 0),
-                        stop=(u == 2 * PASSES - 1),
-                    )
+                a_ps = psum_a.tile([P, HALF], F32, name="a_ps")
+                project(a_ps[:], t, first, HALF)
                 act = ring2.tile([P, HALF], F32, name="act")
                 nc.scalar.activation(act[:], a_ps[:], GELU)
                 nc.scalar.activation(planar[:, t, :], act[:], COPY, scale=sm_t[:, t : t + 1])
@@ -163,7 +181,7 @@ def tile_list_msg_gelu_res_resL_kernel(
 
         def total(nt, half):
             cols = slice(half * HALF, (half + 1) * HALF)
-            y_ps = psum.tile([P, HALF], F32, name="y_ps")
+            y_ps = psum_y.tile([P, HALF], F32, name="y_ps")
             nc.tensor.matmul_mx(
                 out=y_ps[:], lhsT=wd4[:, 2 * nt * P : 2 * (nt + 1) * P].bitcast(FP4X4),
                 lhsT_scale=wd_s[:, 0, nt * P : (nt + 1) * P],
@@ -175,24 +193,30 @@ def tile_list_msg_gelu_res_resL_kernel(
                 rhs=h_codes[:, cols].bitcast(FP8X4), rhs_scale=h_scales[:, cols], start=False, stop=True,
             )
             z[nt, half] = keep.tile([P, HALF], F32, name="z%d%d" % (nt, half))
-            nc.vector.tensor_tensor(z[nt, half][:], y_ps[:], g[nt][:, cols], ADD)
+            summed = ring2.tile([P, HALF], F32, name="summed")
+            if (nt, half) == (0, 0):
+                nc.vector.tensor_tensor(summed[:], y_ps[:], g[nt][:, cols], ADD)
+                nc.vector.tensor_tensor(z[nt, half][:], summed[:], edge_w[:, cols], MULT)
+            else:
+                y = ring3.tile([P, HALF], F32, name="y")
+                nc.scalar.copy(y[:], y_ps[:])
+                nc.gpsimd.tensor_tensor(summed[:], y[:], g[nt][:, cols], ADD)
+                nc.gpsimd.tensor_tensor(z[nt, half][:], summed[:], edge_w[:, cols], MULT)
 
         def place(nt, half):
-            cols = slice(half * HALF, (half + 1) * HALF)
-            nc.vector.tensor_tensor(
+            nc.vector.tensor_copy(
                 windows[nt % WINDOWS][:].indirect(dst_list[:, half * HALF // 16 : (half + 1) * HALF // 16]),
                 z[nt, half][:],
-                edge_w[:, cols],
-                MULT,
             )
 
-        for half in range(2):
-            hidden(half)
+        hidden_first()
         for nt in range(N_TILES):
             nc.vector.tensor_copy(g[nt][:], res[:, nt, :].indirect(dst_list[:]))
-        for half in range(2):
-            for nt in range(N_TILES):
-                total(nt, half)
+        for nt in range(N_TILES):
+            total(nt, 0)
+        hidden(1)
+        for nt in range(N_TILES):
+            total(nt, 1)
         for nt in range(N_TILES):
             place(nt, 0)
             place(nt, 1)

@@ -50,21 +50,21 @@ def tile_list_msg_gelu_res_resL_kernel(
         tab_s = keep.tile([P, T], U8, name="tab_s", tag="tables", align_bytes=64)
         wd_s = keep.tile([P, 2, N], U8, name="wd_s", align_bytes=64)
         plane1 = keep.tile([P, 2 * J], U8, name="plane1", align_bytes=64)
-        nc.vector.memset(tab_s[:].bitcast(I32), 0)
         warm_in = keep.tile([P, 1], F32, name="warm_in")
         nc.vector.memset(warm_in[:], 0.0)
         nc.vector.memset(plane1[:].bitcast(I32), 0)
         windows = [keep.tile([P, T], F32, name="window%d" % i) for i in range(WINDOWS)]
-        for i in range(WINDOWS - 1):
+        for i in range(WINDOWS - 2):
             nc.vector.memset(windows[i][:], 0.0)
 
         nc.sync.dma_start(src_list[:], offs)
-        nc.sync.dma_start(dst_list[:], offs2)
-        for q in range(QUADS):
-            nc.scalar.dma_start(
-                out=tab_s[32 * q : 32 * q + 8, :].bitcast(I32),
-                in_=tab_scales[:, 4 * q : 4 * q + 4, :].bitcast(I32),
+        scale_rows = tab_scales.rearrange("a q t -> (a q) t").bitcast(I32)
+        for e in range(2 * QUADS):
+            first_row = 4 * ((e + 1) // 2)
+            nc.sync.dma_start(
+                out=tab_s[16 * e : 16 * (e + 1), :].bitcast(I32), in_=scale_rows[first_row : first_row + 16, :]
             )
+        nc.sync.dma_start(dst_list[:], offs2)
         warm_out = keep.tile([P, 1], F32, name="warm_out")
         nc.scalar.activation(warm_out[:], warm_in[:], GELU)
         grouped = []
@@ -76,8 +76,8 @@ def tile_list_msg_gelu_res_resL_kernel(
                 )
                 rounded = keep.tile([P, R * PACK], BF16, name="rounded%d" % len(grouped), align_bytes=64)
                 nc.scalar.copy(
-                    rounded[:].rearrange("p (t m i) -> p m i t", t=PACK, i=PACK),
-                    raw[:].rearrange("p i (m t) -> p m i t", t=PACK),
+                    rounded[:].rearrange("p (t m i) -> p m t i", t=PACK, i=PACK),
+                    raw[:].rearrange("p i (m t) -> p m t i", t=PACK),
                 )
                 grouped.append(rounded)
                 if len(grouped) == 1:
@@ -89,7 +89,7 @@ def tile_list_msg_gelu_res_resL_kernel(
         plane0 = keep.tile([P, 2 * J], U8, name="plane0", align_bytes=64)
         for i in range(2):
             nc.vector.tensor_copy(plane0[:, i * J : (i + 1) * J], tab_s[:].indirect(both[i][:]))
-        nc.sync.dma_start(out=plane1[0:112, :].bitcast(I32), in_=plane0[4:116, :].bitcast(I32))
+        nc.sync.dma_start(out=plane1[0:100, :].bitcast(I32), in_=plane0[28:P, :].bitcast(I32))
         res = keep.tile([P, N_TILES, T], F32, name="res", tag="tables", align_bytes=64)
         for nt in range(N_TILES):
             nc.sync.dma_start(out=res[:, nt, :], in_=rT[nt * P : (nt + 1) * P, :])
@@ -102,7 +102,8 @@ def tile_list_msg_gelu_res_resL_kernel(
             nc.gpsimd.dma_start(
                 out=wd_s[98:P, i, :].bitcast(I32), in_=rows[14:16, :].unsqueeze(0).broadcast_to([15, 2, N // 4])
             )
-        nc.gpsimd.memset(windows[WINDOWS - 1][:], 0.0)
+        for i in range(WINDOWS - 2, WINDOWS):
+            nc.gpsimd.memset(windows[i][:], 0.0)
 
         picked = [keep.tile([P, J], U32, name="picked", tag="picked%d" % i, align_bytes=64) for i in range(2)]
         parted = [keep.tile([P, PASSES * 2 * J], U8, name="parted%d" % i, align_bytes=64) for i in range(2)]

@@ -22,12 +22,11 @@ P = 128
 PACK = 4
 K_PASS = P * PACK
 PASSES = K // K_PASS
-QUADS = 4
-CHUNKS = J // P
 N_TILES = N // P
 HALF = J // 2
-HALF_CHUNKS = CHUNKS // 2
-WINDOWS = 4
+WINDOWS = 2
+SHIFT = 16
+SCALE_LOADS = ((0, 32, 0), (32, 16, 4), (48, 8, 20), (56, 32, 0), (88, 16, 4), (104, 8, 20))
 
 
 def tile_list_msg_gelu_res_resL_kernel(
@@ -37,150 +36,170 @@ def tile_list_msg_gelu_res_resL_kernel(
     with ExitStack() as ctx:
         lists = ctx.enter_context(tc.tile_pool(name="lists", bufs=1))
         keep = ctx.enter_context(tc.tile_pool(name="keep", bufs=1))
-        ring2 = ctx.enter_context(tc.tile_pool(name="ring2", bufs=2))
-        ring3 = ctx.enter_context(tc.tile_pool(name="ring3", bufs=3))
-        psum_a = ctx.enter_context(tc.psum_pool(name="psum_a", bufs=6))
-        psum_y = ctx.enter_context(tc.psum_pool(name="psum_y", bufs=2))
+        ring = ctx.enter_context(tc.tile_pool(name="ring", bufs=3))
+        psum_a = ctx.enter_context(tc.psum_pool(name="psum_a", bufs=4))
+        psum_y = ctx.enter_context(tc.psum_pool(name="psum_y", bufs=4))
 
         src_list = lists.tile([P, J // 16], U16, name="src_list")
         dst_list = lists.tile([P, J // 16], U16, name="dst_list")
         both = (src_list, dst_list)
 
-        tab_w = keep.tile([P, T], I32, name="tab_w", tag="tab_w", align_bytes=64)
-        tab_s = keep.tile([P, T], U8, name="tab_s", tag="tables", align_bytes=64)
+        def part_of(one_list, half):
+            return one_list[:, half * HALF // 16 : (half + 1) * HALF // 16]
+
+        tab_w = keep.tile([P, T], I32, name="tab_w", align_bytes=64)
+        tab_s = keep.tile([P, T], U8, name="tab_s", align_bytes=64)
         wd_s = keep.tile([P, 2, N], U8, name="wd_s", align_bytes=64)
+        plane0 = keep.tile([P, 2 * J], U8, name="plane0", align_bytes=64)
         plane1 = keep.tile([P, 2 * J], U8, name="plane1", align_bytes=64)
+        planes = (plane0, plane1)
         warm_in = keep.tile([P, 1], F32, name="warm_in")
+        warm_out = keep.tile([P, 1], F32, name="warm_out")
         nc.vector.memset(warm_in[:], 0.0)
-        nc.vector.memset(plane1[:].bitcast(I32), 0)
+        nc.scalar.activation(warm_out[:], warm_in[:], GELU)
         windows = [keep.tile([P, T], F32, name="window%d" % i) for i in range(WINDOWS)]
-        for i in range(WINDOWS - 2):
+        for i in range(WINDOWS):
             nc.vector.memset(windows[i][:], 0.0)
+        nc.vector.memset(plane1[:].bitcast(I32), 0)
 
         nc.sync.dma_start(src_list[:], offs)
         scale_rows = tab_scales.rearrange("a q t -> (a q) t").bitcast(I32)
-        for e in range(2 * QUADS):
-            first_row = 4 * ((e + 1) // 2)
-            nc.sync.dma_start(
-                out=tab_s[16 * e : 16 * (e + 1), :].bitcast(I32), in_=scale_rows[first_row : first_row + 16, :]
-            )
+        for first, count, row in SCALE_LOADS:
+            nc.sync.dma_start(out=tab_s[first : first + count, :].bitcast(I32), in_=scale_rows[row : row + count, :])
+        nc.sync.dma_start(
+            out=tab_s[112:P, :].bitcast(I32), in_=scale_rows[28:32, :].unsqueeze(0).broadcast_to([4, 4, T // 4])
+        )
         nc.sync.dma_start(dst_list[:], offs2)
-        warm_out = keep.tile([P, 1], F32, name="warm_out")
-        nc.scalar.activation(warm_out[:], warm_in[:], GELU)
-        grouped = []
-        for w in (ws, wt):
-            for a in range(PASSES):
-                raw = ring3.tile([P, PACK, R], F32, name="raw")
-                nc.sync.dma_start(
-                    out=raw[:], in_=w[a * K_PASS : (a + 1) * K_PASS, :].rearrange("(p i) r -> p i r", i=PACK)
-                )
-                rounded = keep.tile([P, R * PACK], BF16, name="rounded%d" % len(grouped), align_bytes=64)
-                nc.scalar.copy(
-                    rounded[:].rearrange("p (t m i) -> p m t i", t=PACK, i=PACK),
-                    raw[:].rearrange("p i (m t) -> p m t i", t=PACK),
-                )
-                grouped.append(rounded)
-                if len(grouped) == 1:
-                    nc.sync.dma_start(out=tab_w[:], in_=tab_words[0].rearrange("p t b -> p (t b)").bitcast(I32))
 
-        sm_t = keep.tile([P, PACK], F32, name="sm_t")
-        nc.gpsimd.dma_start(out=sm_t[:], in_=sm.rearrange("(p t) -> p t", t=PACK))
+        rounded = [
+            keep.tile([P, R * PACK], BF16, name="rounded", tag="rounded%d" % u, align_bytes=64) for u in range(2 * PASSES)
+        ]
 
-        plane0 = keep.tile([P, 2 * J], U8, name="plane0", align_bytes=64)
+        def load_weight(u, first, width):
+            w = (ws, wt)[u // PASSES]
+            a = u % PASSES
+            raw = keep.tile([P, PACK, width], F32, name="raw%d_%d" % (u, first))
+            nc.sync.dma_start(
+                out=raw[:],
+                in_=w[a * K_PASS : (a + 1) * K_PASS, first : first + width].rearrange("(p i) r -> p i r", i=PACK),
+            )
+            nc.scalar.copy(
+                rounded[u][:].rearrange("p (t m i) -> p m t i", t=PACK, i=PACK)[
+                    :, first // PACK : (first + width) // PACK, :, :
+                ],
+                raw[:].rearrange("p i (m t) -> p m t i", t=PACK),
+            )
+
+        load_weight(0, 0, R)
+        load_weight(1, 0, R // 2)
+        nc.sync.dma_start(out=tab_w[:], in_=tab_words[0].rearrange("p t b -> p (t b)").bitcast(I32))
+        load_weight(1, R // 2, R // 2)
+        load_weight(2, 0, R // 2)
+        load_weight(2, R // 2, R // 2)
         for i in range(2):
             nc.vector.tensor_copy(plane0[:, i * J : (i + 1) * J], tab_s[:].indirect(both[i][:]))
-        nc.sync.dma_start(out=plane1[0:100, :].bitcast(I32), in_=plane0[28:P, :].bitcast(I32))
-        res = keep.tile([P, N_TILES, T], F32, name="res", tag="tables", align_bytes=64)
-        for nt in range(N_TILES):
-            nc.sync.dma_start(out=res[:, nt, :], in_=rT[nt * P : (nt + 1) * P, :])
-        planes = (plane0, plane1)
+        nc.sync.dma_start(out=plane1[0 : P - SHIFT, :].bitcast(I32), in_=plane0[SHIFT:P, :].bitcast(I32))
+
+        load_weight(3, 0, R // 2)
+        load_weight(3, R // 2, R // 2)
+        sm_t = keep.tile([P, PACK], F32, name="sm_t")
+        nc.sync.dma_start(out=sm_t[:], in_=sm.rearrange("(p t) -> p t", t=PACK))
+
+        res = [keep.tile([P, T], F32, name="res%d" % nt) for nt in range(N_TILES)]
+        wd4 = keep.tile([P, 2 * N], U8, name="wd4", align_bytes=64)
+        wd8 = keep.tile([P, N], I32, name="wd8", align_bytes=64)
+        edge_w = keep.tile([P, J], F32, name="edge_w")
+        for nt in range(N_TILES - 1):
+            nc.sync.dma_start(out=res[nt][:], in_=rT[nt * P : (nt + 1) * P, :])
+        nc.sync.dma_start(out=wd4[:].bitcast(I32), in_=wd4_words[0].bitcast(I32))
+        nc.sync.dma_start(out=wd8[:], in_=wd8_words[0].rearrange("p n b -> p (n b)").bitcast(I32))
         for i, scales in enumerate((wd4_scales, wd8_scales)):
             rows = scales[0].bitcast(I32)
-            nc.gpsimd.dma_start(
+            nc.sync.dma_start(
                 out=wd_s[0:98, i, :].bitcast(I32), in_=rows[0:14, :].unsqueeze(0).broadcast_to([7, 14, N // 4])
             )
-            nc.gpsimd.dma_start(
+            nc.sync.dma_start(
                 out=wd_s[98:P, i, :].bitcast(I32), in_=rows[14:16, :].unsqueeze(0).broadcast_to([15, 2, N // 4])
             )
-        for i in range(WINDOWS - 2, WINDOWS):
-            nc.gpsimd.memset(windows[i][:], 0.0)
-
-        picked = [keep.tile([P, J], U32, name="picked", tag="picked%d" % i, align_bytes=64) for i in range(2)]
-        parted = [keep.tile([P, PASSES * 2 * J], U8, name="parted%d" % i, align_bytes=64) for i in range(2)]
-        for i in range(2):
-            nc.vector.tensor_copy(picked[i][:], tab_w[:].bitcast(U32).indirect(both[i][:]))
-        for i in range(2):
-            nc.vector.tensor_copy(
-                parted[i][:].bitcast(U16).rearrange("p (d j) -> p d j", d=PASSES),
-                picked[i][:].bitcast(U16).rearrange("p (j d) -> p d j", d=PASSES),
-            )
+        nc.sync.dma_start(out=res[N_TILES - 1][:], in_=rT[(N_TILES - 1) * P : N_TILES * P, :])
+        nc.sync.dma_start(out=edge_w[:], in_=wgo)
 
         w_codes = keep.tile([P, 2 * PASSES, R], U32, name="w_codes", align_bytes=64)
         w_scales = keep.tile([P, 2 * PASSES, R], U8, name="w_scales", align_bytes=64)
-        for u in range(2 * PASSES):
-            nc.vector.quantize_mx(out=w_codes[:, u, :].bitcast(FP8X4), scales=w_scales[:, u, :], in_=grouped[u][:])
 
-        wd4 = keep.tile([P, 2 * N], U8, name="wd4", tag="picked0", align_bytes=64)
-        wd8 = keep.tile([P, N], I32, name="wd8", tag="picked1", align_bytes=64)
-        nc.sync.dma_start(out=wd4[:].bitcast(I32), in_=wd4_words[0].bitcast(I32))
-        nc.sync.dma_start(out=wd8[:], in_=wd8_words[0].rearrange("p n b -> p (n b)").bitcast(I32))
-        edge_w = keep.tile([P, J], F32, name="edge_w", tag="tab_w", align_bytes=64)
-        nc.sync.dma_start(out=edge_w[:], in_=wgo)
+        def quantise_weight(u):
+            nc.vector.quantize_mx(out=w_codes[:, u, :].bitcast(FP8X4), scales=w_scales[:, u, :], in_=rounded[u][:])
+
+        picked = {}
+        parted = {}
+
+        def pick(i, half, tag):
+            picked[i, half] = keep.tile([P, HALF], U32, name="picked", tag=tag, align_bytes=64)
+            nc.vector.tensor_copy(picked[i, half][:], tab_w[:].bitcast(U32).indirect(part_of(both[i], half)))
+
+        def part(i, half, tag):
+            parted[i, half] = keep.tile([P, PASSES * 2 * HALF], U8, name="parted", tag=tag, align_bytes=64)
+            nc.vector.tensor_copy(
+                parted[i, half][:].bitcast(U16).rearrange("p (d j) -> p d j", d=PASSES),
+                picked[i, half][:].bitcast(U16).rearrange("p (j d) -> p d j", d=PASSES),
+            )
+
+        quantise_weight(0)
+        for i in range(2):
+            pick(i, 0, "picked%d" % i)
+        for i in range(2):
+            part(i, 0, "parted%d" % i)
+        quantise_weight(1)
+        pick(0, 1, "picked2")
+        quantise_weight(2)
+        pick(1, 1, "rounded2")
+        part(0, 1, "parted2")
+        quantise_weight(3)
+        part(1, 1, "rounded3")
 
         h_codes = keep.tile([P, J], U32, name="h_codes", align_bytes=64)
         h_scales = keep.tile([P, J], U8, name="h_scales", align_bytes=64)
-        g = [keep.tile([P, J], F32, name="g%d" % nt) for nt in range(N_TILES)]
 
-        def project(a_ps, t, first, width):
+        def project(half):
+            banks = [psum_a.tile([P, HALF], F32, name="a_ps") for t in range(PACK)]
+            first = half * HALF
             for u in range(2 * PASSES):
                 i, a = divmod(u, PASSES)
-                start = (a * J + first) * 2
-                nc.tensor.matmul_mx(
-                    out=a_ps,
-                    lhsT=w_codes[:, u, t * P : (t + 1) * P].bitcast(FP8X4),
-                    lhsT_scale=w_scales[:, u, t * P : (t + 1) * P],
-                    rhs=parted[i][:, start : start + 2 * width].bitcast(FP4X4),
-                    rhs_scale=planes[a][:, i * J + first : i * J + first + width],
-                    start=(u == 0),
-                    stop=(u == 2 * PASSES - 1),
-                )
-
-        def hidden_first():
-            h = ring2.tile([P, HALF * PACK], BF16, name="h", align_bytes=64)
-            for c in range(HALF_CHUNKS):
-                a_ps = psum_a.tile([P, PACK, P], F32, name="a_ps")
+                start = a * HALF * 2
                 for t in range(PACK):
-                    project(a_ps[:, t, :], t, c * P, P)
-                act = ring3.tile([P, P, PACK], F32, name="act4")
-                nc.scalar.activation(act[:], a_ps[:].rearrange("p t j -> p j t"), GELU)
-                nc.gpsimd.tensor_tensor(
-                    h[:, c * P * PACK : (c + 1) * P * PACK].rearrange("p (j t) -> p j t", t=PACK),
-                    act[:],
-                    sm_t[:].unsqueeze(1).to_broadcast([P, P, PACK]),
-                    MULT,
-                )
-            nc.vector.quantize_mx(out=h_codes[:, 0:HALF].bitcast(FP8X4), scales=h_scales[:, 0:HALF], in_=h[:])
+                    nc.tensor.matmul_mx(
+                        out=banks[t][:],
+                        lhsT=w_codes[:, u, t * P : (t + 1) * P].bitcast(FP8X4),
+                        lhsT_scale=w_scales[:, u, t * P : (t + 1) * P],
+                        rhs=parted[i, half][:, start : start + 2 * HALF].bitcast(FP4X4),
+                        rhs_scale=planes[a][:, i * J + first : i * J + first + HALF],
+                        start=(u == 0),
+                        stop=(u == 2 * PASSES - 1),
+                    )
+            return banks
 
-        def hidden(half):
-            first = half * HALF
-            planar = ring2.tile([P, PACK, HALF], BF16, name="planar")
-            for t in range(PACK):
-                a_ps = psum_a.tile([P, HALF], F32, name="a_ps")
-                project(a_ps[:], t, first, HALF)
-                act = ring2.tile([P, HALF], F32, name="act")
-                nc.scalar.activation(act[:], a_ps[:], GELU)
-                nc.scalar.activation(planar[:, t, :], act[:], COPY, scale=sm_t[:, t : t + 1])
-            h = ring2.tile([P, HALF * PACK], BF16, name="h", align_bytes=64)
+        def hidden(half, banks):
+            planar = keep.tile([P, PACK, HALF], BF16, name="planar%d" % half)
+            acts = []
+            for t in range(PACK + 1):
+                if t < PACK:
+                    act = ring.tile([P, HALF], F32, name="act")
+                    nc.scalar.activation(act[:], banks[t][:], GELU)
+                    acts.append(act)
+                if t > 0:
+                    nc.scalar.activation(planar[:, t - 1, :], acts[t - 1][:], COPY, scale=sm_t[:, t - 1 : t])
+            h = keep.tile([P, HALF * PACK], BF16, name="h", tag="h%d" % half, align_bytes=64)
             nc.scalar.copy(
                 h[:].rearrange("p (c i t) -> p c t i", i=4, t=PACK),
                 planar[:].rearrange("p t (c i) -> p c t i", i=4),
             )
-            cols = slice(first, first + HALF)
+            return h
+
+        def quantise_hidden(half, h):
+            cols = slice(half * HALF, (half + 1) * HALF)
             nc.vector.quantize_mx(out=h_codes[:, cols].bitcast(FP8X4), scales=h_scales[:, cols], in_=h[:])
 
-        z = {}
-
-        def total(nt, half):
+        def message(nt, half):
             cols = slice(half * HALF, (half + 1) * HALF)
             y_ps = psum_y.tile([P, HALF], F32, name="y_ps")
             nc.tensor.matmul_mx(
@@ -193,32 +212,63 @@ def tile_list_msg_gelu_res_resL_kernel(
                 lhsT_scale=wd_s[:, 1, nt * P : (nt + 1) * P],
                 rhs=h_codes[:, cols].bitcast(FP8X4), rhs_scale=h_scales[:, cols], start=False, stop=True,
             )
-            z[nt, half] = keep.tile([P, HALF], F32, name="z%d%d" % (nt, half))
-            summed = ring2.tile([P, HALF], F32, name="summed")
-            if (nt, half) == (0, 0):
-                nc.vector.tensor_tensor(summed[:], y_ps[:], g[nt][:, cols], ADD)
-                nc.vector.tensor_tensor(z[nt, half][:], summed[:], edge_w[:, cols], MULT)
-            else:
-                y = ring3.tile([P, HALF], F32, name="y")
-                nc.scalar.copy(y[:], y_ps[:])
-                nc.gpsimd.tensor_tensor(summed[:], y[:], g[nt][:, cols], ADD)
-                nc.gpsimd.tensor_tensor(z[nt, half][:], summed[:], edge_w[:, cols], MULT)
+            return y_ps
+
+        h_first = hidden(0, project(0))
+        second_banks = project(1)
+
+        own = {}
+        first_tile = keep.tile([P, J], F32, name="own0", tag="rounded2", align_bytes=64)
+        for nt in range(N_TILES - 1):
+            whole = first_tile if nt == 0 else keep.tile([P, J], F32, name="own%d" % nt)
+            nc.vector.tensor_copy(whole[:], res[nt][:].indirect(dst_list[:]))
+            for half in range(2):
+                own[nt, half] = whole[:, half * HALF : (half + 1) * HALF]
+        last = N_TILES - 1
+        last_first = keep.tile([P, HALF], F32, name="last_first")
+        nc.vector.tensor_copy(last_first[:], res[last][:].indirect(part_of(dst_list, 0)))
+        own[last, 0] = last_first[:]
+        quantise_hidden(0, h_first)
+        last_second = keep.tile([P, HALF], F32, name="last_second", tag="h0", align_bytes=64)
+        nc.vector.tensor_copy(last_second[:], res[last][:].indirect(part_of(dst_list, 1)))
+        own[last, 1] = last_second[:]
+
+        summed = {}
+
+        def total(nt, half, into):
+            nc.vector.tensor_tensor(into, message(nt, half)[:], own[nt, half], ADD)
+            summed[nt, half] = into
 
         def place(nt, half):
-            nc.vector.tensor_copy(
-                windows[nt % WINDOWS][:].indirect(dst_list[:, half * HALF // 16 : (half + 1) * HALF // 16]),
-                z[nt, half][:],
+            nc.vector.tensor_tensor(
+                windows[nt % WINDOWS][:].indirect(part_of(dst_list, half)),
+                summed[nt, half],
+                edge_w[:, half * HALF : (half + 1) * HALF],
+                MULT,
             )
 
-        hidden_first()
-        for nt in range(N_TILES):
-            nc.vector.tensor_copy(g[nt][:], res[:, nt, :].indirect(dst_list[:]))
-        for nt in range(N_TILES):
-            total(nt, 0)
-        hidden(1)
-        for nt in range(N_TILES):
-            total(nt, 1)
-        for nt in range(N_TILES):
+        def fresh(tag):
+            return keep.tile([P, HALF], F32, name="summed", tag=tag)[:]
+
+        def store(nt):
+            nc.sync.dma_start(out=out[nt * P : (nt + 1) * P, :], in_=windows[nt % WINDOWS][:])
+
+        h_second = hidden(1, second_banks)
+        for nt in range(WINDOWS):
+            total(nt, 0, fresh("summed%d" % nt))
+        for nt in range(WINDOWS):
+            place(nt, 0)
+        quantise_hidden(1, h_second)
+        late = keep.tile([P, N_TILES - WINDOWS, HALF], F32, name="late", tag="h1", align_bytes=64)
+        for nt in range(WINDOWS, N_TILES):
+            total(nt, 0, late[:, nt - WINDOWS, :])
+        for nt in range(WINDOWS):
+            total(nt, 1, fresh("summed%d" % nt))
+        for nt in range(WINDOWS):
+            place(nt, 1)
+            store(nt)
+            total(nt + WINDOWS, 1, fresh("summed%d" % nt))
+        for nt in range(WINDOWS, N_TILES):
             place(nt, 0)
             place(nt, 1)
-            nc.sync.dma_start(out=out[nt * P : (nt + 1) * P, :], in_=windows[nt % WINDOWS][:])
+            store(nt)

@@ -24,7 +24,7 @@ K_PASS = P * PACK
 PASSES = K // K_PASS
 N_TILES = N // P
 HALF = J // 2
-WINDOWS = 2
+WINDOWS = 4
 SHIFT = 16
 SCALE_LOADS = ((0, 32, 0), (32, 16, 4), (48, 8, 20), (56, 32, 0), (88, 16, 4), (104, 8, 20))
 
@@ -53,13 +53,13 @@ def tile_list_msg_gelu_res_resL_kernel(
         plane0 = keep.tile([P, 2 * J], U8, name="plane0", align_bytes=64)
         plane1 = keep.tile([P, 2 * J], U8, name="plane1", align_bytes=64)
         planes = (plane0, plane1)
-        warm_in = keep.tile([P, 1], F32, name="warm_in")
-        warm_out = keep.tile([P, 1], F32, name="warm_out")
+        warm_in = keep.tile([P, 1], F32, name="warm_in", tag="window2")
+        warm_out = keep.tile([P, 1], F32, name="warm_out", tag="window3")
         nc.vector.memset(warm_in[:], 0.0)
         nc.scalar.activation(warm_out[:], warm_in[:], GELU)
         windows = [keep.tile([P, T], F32, name="window%d" % i) for i in range(WINDOWS)]
         for i in range(WINDOWS):
-            nc.vector.memset(windows[i][:], 0.0)
+            (nc.vector if i < 2 else nc.gpsimd).memset(windows[i][:], 0.0)
         nc.vector.memset(plane1[:].bitcast(I32), 0)
 
         nc.sync.dma_start(src_list[:], offs)
@@ -179,7 +179,7 @@ def tile_list_msg_gelu_res_resL_kernel(
             return banks
 
         def hidden(half, banks):
-            planar = keep.tile([P, PACK, HALF], BF16, name="planar%d" % half)
+            planar = keep.tile([P, PACK, HALF], BF16, name="planar", tag="planar%d" % half)
             acts = []
             for t in range(PACK + 1):
                 if t < PACK:
@@ -233,42 +233,40 @@ def tile_list_msg_gelu_res_resL_kernel(
         nc.vector.tensor_copy(last_second[:], res[last][:].indirect(part_of(dst_list, 1)))
         own[last, 1] = last_second[:]
 
-        summed = {}
+        weighted = {}
 
-        def total(nt, half, into):
-            nc.vector.tensor_tensor(into, message(nt, half)[:], own[nt, half], ADD)
-            summed[nt, half] = into
+        def finish(nt, half):
+            cols = slice(half * HALF, (half + 1) * HALF)
+            y_ps = message(nt, half)
+            summed = ring.tile([P, HALF], F32, name="summed")
+            weighted[nt, half] = keep.tile([P, HALF], F32, name="weighted%d%d" % (nt, half))
+            if (nt, half) == (0, 0):
+                nc.vector.tensor_tensor(summed[:], y_ps[:], own[nt, half], ADD)
+                nc.vector.tensor_tensor(weighted[nt, half][:], summed[:], edge_w[:, cols], MULT)
+            else:
+                if (nt, half) == (2, 0):
+                    y = keep.tile([P, HALF], F32, name="y", tag="planar1")
+                else:
+                    y = ring.tile([P, HALF], F32, name="y")
+                nc.scalar.copy(y[:], y_ps[:])
+                nc.gpsimd.tensor_tensor(summed[:], y[:], own[nt, half], ADD)
+                nc.gpsimd.tensor_tensor(weighted[nt, half][:], summed[:], edge_w[:, cols], MULT)
 
         def place(nt, half):
-            nc.vector.tensor_tensor(
-                windows[nt % WINDOWS][:].indirect(part_of(dst_list, half)),
-                summed[nt, half],
-                edge_w[:, half * HALF : (half + 1) * HALF],
-                MULT,
-            )
+            nc.vector.tensor_copy(windows[nt][:].indirect(part_of(dst_list, half)), weighted[nt, half][:])
 
-        def fresh(tag):
-            return keep.tile([P, HALF], F32, name="summed", tag=tag)[:]
-
-        def store(nt):
-            nc.sync.dma_start(out=out[nt * P : (nt + 1) * P, :], in_=windows[nt % WINDOWS][:])
-
+        finish(0, 0)
+        finish(1, 0)
         h_second = hidden(1, second_banks)
-        for nt in range(WINDOWS):
-            total(nt, 0, fresh("summed%d" % nt))
-        for nt in range(WINDOWS):
-            place(nt, 0)
+        finish(2, 0)
+        finish(3, 0)
+        place(0, 0)
+        place(1, 0)
         quantise_hidden(1, h_second)
-        late = keep.tile([P, N_TILES - WINDOWS, HALF], F32, name="late", tag="h1", align_bytes=64)
-        for nt in range(WINDOWS, N_TILES):
-            total(nt, 0, late[:, nt - WINDOWS, :])
-        for nt in range(WINDOWS):
-            total(nt, 1, fresh("summed%d" % nt))
-        for nt in range(WINDOWS):
+        place(2, 0)
+        place(3, 0)
+        for nt in range(N_TILES):
+            finish(nt, 1)
+        for nt in range(N_TILES):
             place(nt, 1)
-            store(nt)
-            total(nt + WINDOWS, 1, fresh("summed%d" % nt))
-        for nt in range(WINDOWS, N_TILES):
-            place(nt, 0)
-            place(nt, 1)
-            store(nt)
+            nc.sync.dma_start(out=out[nt * P : (nt + 1) * P, :], in_=windows[nt][:])

@@ -24,9 +24,9 @@ K_PASS = P * PACK
 PASSES = K // K_PASS
 N_TILES = N // P
 HALF = J // 2
+QUARTER = J // 4
 WINDOWS = 4
 SHIFT = 16
-SCALE_LOADS = ((0, 32, 0), (32, 16, 4), (48, 8, 20), (56, 32, 0), (88, 16, 4), (104, 8, 20))
 
 
 def tile_list_msg_gelu_res_resL_kernel(
@@ -55,6 +55,10 @@ def tile_list_msg_gelu_res_resL_kernel(
         planes = (plane0, plane1)
         warm_in = keep.tile([P, 1], F32, name="warm_in", tag="window2")
         warm_out = keep.tile([P, 1], F32, name="warm_out", tag="window3")
+        nc.vector.memset(tab_s[:].bitcast(I32), 0)
+        scale_rows = tab_scales.bitcast(I32).rearrange("a (q r) t -> r q a t", r=PACK)
+        for r in range(PACK):
+            nc.scalar.dma_start(out=tab_s[r:P:SHIFT, :].bitcast(I32), in_=scale_rows[r])
         nc.vector.memset(warm_in[:], 0.0)
         nc.scalar.activation(warm_out[:], warm_in[:], GELU)
         windows = [keep.tile([P, T], F32, name="window%d" % i) for i in range(WINDOWS)]
@@ -63,12 +67,6 @@ def tile_list_msg_gelu_res_resL_kernel(
         nc.vector.memset(plane1[:].bitcast(I32), 0)
 
         nc.sync.dma_start(src_list[:], offs)
-        scale_rows = tab_scales.rearrange("a q t -> (a q) t").bitcast(I32)
-        for first, count, row in SCALE_LOADS:
-            nc.sync.dma_start(out=tab_s[first : first + count, :].bitcast(I32), in_=scale_rows[row : row + count, :])
-        nc.sync.dma_start(
-            out=tab_s[112:P, :].bitcast(I32), in_=scale_rows[28:32, :].unsqueeze(0).broadcast_to([4, 4, T // 4])
-        )
         nc.sync.dma_start(dst_list[:], offs2)
 
         rounded = [
@@ -109,7 +107,7 @@ def tile_list_msg_gelu_res_resL_kernel(
         wd4 = keep.tile([P, 2 * N], U8, name="wd4", align_bytes=64)
         wd8 = keep.tile([P, N], I32, name="wd8", align_bytes=64)
         edge_w = keep.tile([P, J], F32, name="edge_w")
-        for nt in range(N_TILES - 1):
+        for nt in range(2):
             nc.sync.dma_start(out=res[nt][:], in_=rT[nt * P : (nt + 1) * P, :])
         nc.sync.dma_start(out=wd4[:].bitcast(I32), in_=wd4_words[0].bitcast(I32))
         nc.sync.dma_start(out=wd8[:], in_=wd8_words[0].rearrange("p n b -> p (n b)").bitcast(I32))
@@ -121,8 +119,9 @@ def tile_list_msg_gelu_res_resL_kernel(
             nc.sync.dma_start(
                 out=wd_s[98:P, i, :].bitcast(I32), in_=rows[14:16, :].unsqueeze(0).broadcast_to([15, 2, N // 4])
             )
-        nc.sync.dma_start(out=res[N_TILES - 1][:], in_=rT[(N_TILES - 1) * P : N_TILES * P, :])
         nc.sync.dma_start(out=edge_w[:], in_=wgo)
+        for nt in range(2, N_TILES):
+            nc.sync.dma_start(out=res[nt][:], in_=rT[nt * P : (nt + 1) * P, :])
 
         w_codes = keep.tile([P, 2 * PASSES, R], U32, name="w_codes", align_bytes=64)
         w_scales = keep.tile([P, 2 * PASSES, R], U8, name="w_scales", align_bytes=64)
@@ -137,25 +136,27 @@ def tile_list_msg_gelu_res_resL_kernel(
             picked[i, half] = keep.tile([P, HALF], U32, name="picked", tag=tag, align_bytes=64)
             nc.vector.tensor_copy(picked[i, half][:], tab_w[:].bitcast(U32).indirect(part_of(both[i], half)))
 
-        def part(i, half, tag):
-            parted[i, half] = keep.tile([P, PASSES * 2 * HALF], U8, name="parted", tag=tag, align_bytes=64)
+        def part(i, half, into):
+            parted[i, half] = into[:, i * PASSES * 2 * HALF : (i + 1) * PASSES * 2 * HALF]
             nc.vector.tensor_copy(
-                parted[i, half][:].bitcast(U16).rearrange("p (d j) -> p d j", d=PASSES),
+                parted[i, half].bitcast(U16).rearrange("p (d j) -> p d j", d=PASSES),
                 picked[i, half][:].bitcast(U16).rearrange("p (j d) -> p d j", d=PASSES),
             )
 
         quantise_weight(0)
         for i in range(2):
             pick(i, 0, "picked%d" % i)
+        parted_first = keep.tile([P, 2 * PASSES * 2 * HALF], U8, name="parted_first", align_bytes=64)
         for i in range(2):
-            part(i, 0, "parted%d" % i)
+            part(i, 0, parted_first)
         quantise_weight(1)
         pick(0, 1, "picked2")
         quantise_weight(2)
         pick(1, 1, "rounded2")
-        part(0, 1, "parted2")
         quantise_weight(3)
-        part(1, 1, "rounded3")
+        parted_second = keep.tile([P, 2 * PASSES * 2 * HALF], U8, name="parted_second", tag="rounded3", align_bytes=64)
+        for i in range(2):
+            part(i, 1, parted_second)
 
         h_codes = keep.tile([P, J], U32, name="h_codes", align_bytes=64)
         h_scales = keep.tile([P, J], U8, name="h_scales", align_bytes=64)
@@ -163,110 +164,112 @@ def tile_list_msg_gelu_res_resL_kernel(
         def project(half):
             banks = [psum_a.tile([P, HALF], F32, name="a_ps") for t in range(PACK)]
             first = half * HALF
-            for u in range(2 * PASSES):
+            steps = [(u, t) for u in range(2 * PASSES) for t in range(PACK)]
+            if half == 1:
+                steps = [(u, t) for t in range(PACK) for u in range(2 * PASSES)]
+            for u, t in steps:
                 i, a = divmod(u, PASSES)
                 start = a * HALF * 2
-                for t in range(PACK):
-                    nc.tensor.matmul_mx(
-                        out=banks[t][:],
-                        lhsT=w_codes[:, u, t * P : (t + 1) * P].bitcast(FP8X4),
-                        lhsT_scale=w_scales[:, u, t * P : (t + 1) * P],
-                        rhs=parted[i, half][:, start : start + 2 * HALF].bitcast(FP4X4),
-                        rhs_scale=planes[a][:, i * J + first : i * J + first + HALF],
-                        start=(u == 0),
-                        stop=(u == 2 * PASSES - 1),
-                    )
+                nc.tensor.matmul_mx(
+                    out=banks[t][:],
+                    lhsT=w_codes[:, u, t * P : (t + 1) * P].bitcast(FP8X4),
+                    lhsT_scale=w_scales[:, u, t * P : (t + 1) * P],
+                    rhs=parted[i, half][:, start : start + 2 * HALF].bitcast(FP4X4),
+                    rhs_scale=planes[a][:, i * J + first : i * J + first + HALF],
+                    start=(u == 0),
+                    stop=(u == 2 * PASSES - 1),
+                )
             return banks
 
-        def hidden(half, banks):
-            planar = keep.tile([P, PACK, HALF], BF16, name="planar", tag="planar%d" % half)
+        def hidden(banks, first, width, label):
+            planar = keep.tile([P, PACK, width], BF16, name="planar", tag="planar" + label)
             acts = []
             for t in range(PACK + 1):
                 if t < PACK:
-                    act = ring.tile([P, HALF], F32, name="act")
-                    nc.scalar.activation(act[:], banks[t][:], GELU)
+                    act = ring.tile([P, width], F32, name="act")
+                    nc.scalar.activation(act[:], banks[t][:, first : first + width], GELU)
                     acts.append(act)
                 if t > 0:
                     nc.scalar.activation(planar[:, t - 1, :], acts[t - 1][:], COPY, scale=sm_t[:, t - 1 : t])
-            h = keep.tile([P, HALF * PACK], BF16, name="h", tag="h%d" % half, align_bytes=64)
+            h = keep.tile([P, width * PACK], BF16, name="h", tag="h" + label, align_bytes=64)
             nc.scalar.copy(
                 h[:].rearrange("p (c i t) -> p c t i", i=4, t=PACK),
                 planar[:].rearrange("p t (c i) -> p c t i", i=4),
             )
             return h
 
-        def quantise_hidden(half, h):
-            cols = slice(half * HALF, (half + 1) * HALF)
+        def quantise_hidden(first, width, h):
+            cols = slice(first, first + width)
             nc.vector.quantize_mx(out=h_codes[:, cols].bitcast(FP8X4), scales=h_scales[:, cols], in_=h[:])
 
-        def message(nt, half):
-            cols = slice(half * HALF, (half + 1) * HALF)
-            y_ps = psum_y.tile([P, HALF], F32, name="y_ps")
-            nc.tensor.matmul_mx(
-                out=y_ps[:], lhsT=wd4[:, 2 * nt * P : 2 * (nt + 1) * P].bitcast(FP4X4),
-                lhsT_scale=wd_s[:, 0, nt * P : (nt + 1) * P],
-                rhs=h_codes[:, cols].bitcast(FP8X4), rhs_scale=h_scales[:, cols], start=True, stop=False,
-            )
-            nc.tensor.matmul_mx(
-                out=y_ps[:], lhsT=wd8[:, nt * P : (nt + 1) * P].bitcast(FP8X4),
-                lhsT_scale=wd_s[:, 1, nt * P : (nt + 1) * P],
-                rhs=h_codes[:, cols].bitcast(FP8X4), rhs_scale=h_scales[:, cols], start=False, stop=True,
-            )
+        def message(nt, first, width, step):
+            y_ps = psum_y.tile([P, width], F32, name="y_ps")
+            for c in range(0, width, step):
+                cols = slice(first + c, first + c + step)
+                nc.tensor.matmul_mx(
+                    out=y_ps[:, c : c + step], lhsT=wd4[:, 2 * nt * P : 2 * (nt + 1) * P].bitcast(FP4X4),
+                    lhsT_scale=wd_s[:, 0, nt * P : (nt + 1) * P],
+                    rhs=h_codes[:, cols].bitcast(FP8X4), rhs_scale=h_scales[:, cols], start=True, stop=False,
+                )
+                nc.tensor.matmul_mx(
+                    out=y_ps[:, c : c + step], lhsT=wd8[:, nt * P : (nt + 1) * P].bitcast(FP8X4),
+                    lhsT_scale=wd_s[:, 1, nt * P : (nt + 1) * P],
+                    rhs=h_codes[:, cols].bitcast(FP8X4), rhs_scale=h_scales[:, cols], start=False, stop=True,
+                )
             return y_ps
 
-        h_first = hidden(0, project(0))
-        second_banks = project(1)
+        def entries(first, width):
+            return dst_list[:, first // 16 : (first + width) // 16]
 
         own = {}
-        first_tile = keep.tile([P, J], F32, name="own0", tag="rounded2", align_bytes=64)
-        for nt in range(N_TILES - 1):
-            whole = first_tile if nt == 0 else keep.tile([P, J], F32, name="own%d" % nt)
-            nc.vector.tensor_copy(whole[:], res[nt][:].indirect(dst_list[:]))
-            for half in range(2):
-                own[nt, half] = whole[:, half * HALF : (half + 1) * HALF]
-        last = N_TILES - 1
-        last_first = keep.tile([P, HALF], F32, name="last_first")
-        nc.vector.tensor_copy(last_first[:], res[last][:].indirect(part_of(dst_list, 0)))
-        own[last, 0] = last_first[:]
-        quantise_hidden(0, h_first)
-        last_second = keep.tile([P, HALF], F32, name="last_second", tag="h0", align_bytes=64)
-        nc.vector.tensor_copy(last_second[:], res[last][:].indirect(part_of(dst_list, 1)))
-        own[last, 1] = last_second[:]
 
-        weighted = {}
+        def residual(nt, first, width, tag):
+            picked_r = keep.tile([P, width], F32, name="own", tag=tag, align_bytes=64)
+            nc.vector.tensor_copy(picked_r[:], res[nt][:].indirect(entries(first, width)))
+            for c in range(0, width, QUARTER):
+                own[nt, first + c] = picked_r[:, c:]
 
-        def finish(nt, half):
-            cols = slice(half * HALF, (half + 1) * HALF)
-            y_ps = message(nt, half)
-            summed = ring.tile([P, HALF], F32, name="summed")
-            weighted[nt, half] = keep.tile([P, HALF], F32, name="weighted%d%d" % (nt, half))
-            if (nt, half) == (0, 0):
-                nc.vector.tensor_tensor(summed[:], y_ps[:], own[nt, half], ADD)
-                nc.vector.tensor_tensor(weighted[nt, half][:], summed[:], edge_w[:, cols], MULT)
-            else:
-                if (nt, half) == (2, 0):
-                    y = keep.tile([P, HALF], F32, name="y", tag="planar1")
-                else:
-                    y = ring.tile([P, HALF], F32, name="y")
-                nc.scalar.copy(y[:], y_ps[:])
-                nc.gpsimd.tensor_tensor(summed[:], y[:], own[nt, half], ADD)
-                nc.gpsimd.tensor_tensor(weighted[nt, half][:], summed[:], edge_w[:, cols], MULT)
+        def on_vector(first):
+            y_ps = message(0, first, QUARTER, P)
+            summed = ring.tile([P, QUARTER], F32, name="early_sum")
+            weighted = keep.tile([P, QUARTER], F32, name="early", tag="early%d" % first, align_bytes=64)
+            nc.vector.tensor_tensor(summed[:], y_ps[:], own[0, first][:, 0:QUARTER], ADD)
+            nc.vector.tensor_tensor(weighted[:], summed[:], edge_w[:, first : first + QUARTER], MULT)
+            nc.vector.tensor_copy(windows[0][:].indirect(entries(first, QUARTER)), weighted[:])
 
-        def place(nt, half):
-            nc.vector.tensor_copy(windows[nt][:].indirect(part_of(dst_list, half)), weighted[nt, half][:])
+        def copy_out(nt, half):
+            y = ring.tile([P, HALF], F32, name="y")
+            nc.scalar.copy(y[:], message(nt, half * HALF, HALF, HALF)[:])
+            return y
 
-        finish(0, 0)
-        finish(1, 0)
-        h_second = hidden(1, second_banks)
-        finish(2, 0)
-        finish(3, 0)
-        place(0, 0)
-        place(1, 0)
-        quantise_hidden(1, h_second)
-        place(2, 0)
-        place(3, 0)
+        def combine(nt, half, y, tag):
+            first = half * HALF
+            summed = keep.tile([P, HALF], F32, name="summed")
+            weighted = keep.tile([P, HALF], F32, name="weighted", tag=tag)
+            nc.gpsimd.tensor_tensor(summed[:], y[:], own[nt, first][:, 0:HALF], ADD)
+            nc.gpsimd.tensor_tensor(weighted[:], summed[:], edge_w[:, first : first + HALF], MULT)
+            return weighted
+
+        def place(nt, half, weighted):
+            nc.vector.tensor_copy(windows[nt][:].indirect(part_of(dst_list, half)), weighted[:])
+
+        first_banks = project(0)
+        h_quarters = [hidden(first_banks, q * QUARTER, QUARTER, "q%d" % q) for q in range(2)]
+        second_banks = project(1)
+        residual(0, 0, J, "rounded2")
+        residual(1, 0, J, "own1")
+        for q in range(2):
+            quantise_hidden(q * QUARTER, QUARTER, h_quarters[q])
+            residual(2, q * HALF, HALF, "hq%d" % q)
+            on_vector(q * QUARTER)
+        residual(3, 0, J, "early%d" % QUARTER)
+        second_piece = combine(1, 0, copy_out(1, 0), "weighted10")
+        third_y = copy_out(2, 0)
+        h_second = hidden(second_banks, 0, HALF, "second")
+        place(1, 0, second_piece)
+        quantise_hidden(HALF, HALF, h_second)
+        place(2, 0, combine(2, 0, third_y, "planarsecond"))
+        place(3, 0, combine(3, 0, copy_out(3, 0), "weighted30"))
         for nt in range(N_TILES):
-            finish(nt, 1)
-        for nt in range(N_TILES):
-            place(nt, 1)
+            place(nt, 1, combine(nt, 1, copy_out(nt, 1), "weighted%d1" % nt))
             nc.sync.dma_start(out=out[nt * P : (nt + 1) * P, :], in_=windows[nt][:])

@@ -36,7 +36,6 @@ def tile_list_msg_gelu_res_resL_kernel(
     with ExitStack() as ctx:
         lists = ctx.enter_context(tc.tile_pool(name="lists", bufs=1))
         keep = ctx.enter_context(tc.tile_pool(name="keep", bufs=1))
-        ring = ctx.enter_context(tc.tile_pool(name="ring", bufs=3))
         psum_a = ctx.enter_context(tc.psum_pool(name="psum_a", bufs=4))
         psum_y = ctx.enter_context(tc.psum_pool(name="psum_y", bufs=4))
 
@@ -76,7 +75,7 @@ def tile_list_msg_gelu_res_resL_kernel(
         def load_weight(u, first, width):
             w = (ws, wt)[u // PASSES]
             a = u % PASSES
-            raw = keep.tile([P, PACK, width], F32, name="raw%d_%d" % (u, first))
+            raw = keep.tile([P, PACK, width], F32, name="raw", tag="raw%d_%d" % (u, first), align_bytes=64)
             nc.sync.dma_start(
                 out=raw[:],
                 in_=w[a * K_PASS : (a + 1) * K_PASS, first : first + width].rearrange("(p i) r -> p i r", i=PACK),
@@ -103,7 +102,7 @@ def tile_list_msg_gelu_res_resL_kernel(
         sm_t = keep.tile([P, PACK], F32, name="sm_t")
         nc.sync.dma_start(out=sm_t[:], in_=sm.rearrange("(p t) -> p t", t=PACK))
 
-        res = [keep.tile([P, T], F32, name="res%d" % nt) for nt in range(N_TILES)]
+        res = [keep.tile([P, T], F32, name="res", tag="res%d" % nt, align_bytes=64) for nt in range(N_TILES)]
         wd4 = keep.tile([P, 2 * N], U8, name="wd4", align_bytes=64)
         wd8 = keep.tile([P, N], I32, name="wd8", align_bytes=64)
         edge_w = keep.tile([P, J], F32, name="edge_w")
@@ -150,15 +149,14 @@ def tile_list_msg_gelu_res_resL_kernel(
         for i in range(2):
             part(i, 0, parted_first)
         quantise_weight(1)
-        pick(0, 1, "picked2")
+        pick(0, 1, "raw1_%d" % (R // 2))
         quantise_weight(2)
-        pick(1, 1, "rounded2")
+        pick(1, 1, "raw2_%d" % (R // 2))
         quantise_weight(3)
-        parted_second = keep.tile([P, 2 * PASSES * 2 * HALF], U8, name="parted_second", tag="rounded3", align_bytes=64)
+        parted_second = keep.tile([P, 2 * PASSES * 2 * HALF], U8, name="parted_second", tag="raw3_%d" % (R // 2), align_bytes=64)
         for i in range(2):
             part(i, 1, parted_second)
 
-        h_codes = keep.tile([P, J], U32, name="h_codes", align_bytes=64)
         h_scales = keep.tile([P, J], U8, name="h_scales", align_bytes=64)
 
         def project(half):
@@ -182,11 +180,11 @@ def tile_list_msg_gelu_res_resL_kernel(
             return banks
 
         def hidden(banks, first, width, label):
-            planar = keep.tile([P, PACK, width], BF16, name="planar", tag="planar" + label)
+            planar = keep.tile([P, PACK, width], BF16, name="planar", tag="planar" + label, align_bytes=64)
             acts = []
             for t in range(PACK + 1):
                 if t < PACK:
-                    act = ring.tile([P, width], F32, name="act")
+                    act = keep.tile([P, width], F32, name="act", tag="act%d" % t, align_bytes=64)
                     nc.scalar.activation(act[:], banks[t][:, first : first + width], GELU)
                     acts.append(act)
                 if t > 0:
@@ -202,74 +200,78 @@ def tile_list_msg_gelu_res_resL_kernel(
             cols = slice(first, first + width)
             nc.vector.quantize_mx(out=h_codes[:, cols].bitcast(FP8X4), scales=h_scales[:, cols], in_=h[:])
 
-        def message(nt, first, width, step):
-            y_ps = psum_y.tile([P, width], F32, name="y_ps")
-            for c in range(0, width, step):
-                cols = slice(first + c, first + c + step)
-                nc.tensor.matmul_mx(
-                    out=y_ps[:, c : c + step], lhsT=wd4[:, 2 * nt * P : 2 * (nt + 1) * P].bitcast(FP4X4),
-                    lhsT_scale=wd_s[:, 0, nt * P : (nt + 1) * P],
-                    rhs=h_codes[:, cols].bitcast(FP8X4), rhs_scale=h_scales[:, cols], start=True, stop=False,
-                )
-                nc.tensor.matmul_mx(
-                    out=y_ps[:, c : c + step], lhsT=wd8[:, nt * P : (nt + 1) * P].bitcast(FP8X4),
-                    lhsT_scale=wd_s[:, 1, nt * P : (nt + 1) * P],
-                    rhs=h_codes[:, cols].bitcast(FP8X4), rhs_scale=h_scales[:, cols], start=False, stop=True,
-                )
-            return y_ps
+        def message(into, nt, cols):
+            nc.tensor.matmul_mx(
+                out=into, lhsT=wd4[:, 2 * nt * P : 2 * (nt + 1) * P].bitcast(FP4X4),
+                lhsT_scale=wd_s[:, 0, nt * P : (nt + 1) * P],
+                rhs=h_codes[:, cols].bitcast(FP8X4), rhs_scale=h_scales[:, cols], start=True, stop=False,
+            )
+            nc.tensor.matmul_mx(
+                out=into, lhsT=wd8[:, nt * P : (nt + 1) * P].bitcast(FP8X4),
+                lhsT_scale=wd_s[:, 1, nt * P : (nt + 1) * P],
+                rhs=h_codes[:, cols].bitcast(FP8X4), rhs_scale=h_scales[:, cols], start=False, stop=True,
+            )
 
         def entries(first, width):
             return dst_list[:, first // 16 : (first + width) // 16]
 
         own = {}
 
-        def residual(nt, first, width, tag):
-            picked_r = keep.tile([P, width], F32, name="own", tag=tag, align_bytes=64)
-            nc.vector.tensor_copy(picked_r[:], res[nt][:].indirect(entries(first, width)))
-            for c in range(0, width, QUARTER):
-                own[nt, first + c] = picked_r[:, c:]
+        def residuals(parts, tag):
+            held = keep.tile([P, len(parts), HALF], F32, name="own", tag=tag, align_bytes=64)
+            for slot, (nt, half) in enumerate(parts):
+                nc.vector.tensor_copy(held[:, slot, :], res[nt][:].indirect(part_of(dst_list, half)))
+                own[nt, half] = held[:, slot, :]
+            return held
 
-        def on_vector(first):
-            y_ps = message(0, first, QUARTER, P)
-            summed = ring.tile([P, QUARTER], F32, name="early_sum")
-            weighted = keep.tile([P, QUARTER], F32, name="early", tag="early%d" % first, align_bytes=64)
-            nc.vector.tensor_tensor(summed[:], y_ps[:], own[0, first][:, 0:QUARTER], ADD)
-            nc.vector.tensor_tensor(weighted[:], summed[:], edge_w[:, first : first + QUARTER], MULT)
-            nc.vector.tensor_copy(windows[0][:].indirect(entries(first, QUARTER)), weighted[:])
-
-        def copy_out(nt, half):
-            y = ring.tile([P, HALF], F32, name="y")
-            nc.scalar.copy(y[:], message(nt, half * HALF, HALF, HALF)[:])
+        def copy_out(nt, half, tag):
+            y_ps = psum_y.tile([P, HALF], F32, name="y_ps")
+            message(y_ps[:], nt, slice(half * HALF, (half + 1) * HALF))
+            y = keep.tile([P, HALF], F32, name="y", tag=tag, align_bytes=64)
+            nc.scalar.copy(y[:], y_ps[:])
             return y
 
-        def combine(nt, half, y, tag):
-            first = half * HALF
-            summed = keep.tile([P, HALF], F32, name="summed")
-            weighted = keep.tile([P, HALF], F32, name="weighted", tag=tag)
-            nc.gpsimd.tensor_tensor(summed[:], y[:], own[nt, first][:, 0:HALF], ADD)
-            nc.gpsimd.tensor_tensor(weighted[:], summed[:], edge_w[:, first : first + HALF], MULT)
+        def combine(y, state, weight, tag):
+            summed = keep.tile(list(y.shape), F32, name="summed")
+            weighted = keep.tile(list(y.shape), F32, name="weighted", tag=tag, align_bytes=64)
+            nc.gpsimd.tensor_tensor(summed[:], y, state, ADD)
+            nc.gpsimd.tensor_tensor(weighted[:], summed[:], weight, MULT)
             return weighted
 
-        def place(nt, half, weighted):
-            nc.vector.tensor_copy(windows[nt][:].indirect(part_of(dst_list, half)), weighted[:])
+        def place(nt, first, width, weighted):
+            nc.vector.tensor_copy(windows[nt][:].indirect(entries(first, width)), weighted)
+
+        def early_quarter(q):
+            first = q * QUARTER
+            y_ps = psum_y.tile([P, QUARTER], F32, name="y_ps")
+            for c in range(0, QUARTER, P):
+                message(y_ps[:, c : c + P], 0, slice(first + c, first + c + P))
+            summed = keep.tile([P, QUARTER], F32, name="early", tag="early%d" % q, align_bytes=64)
+            nc.vector.tensor_tensor(summed[:], y_ps[:], own[0, 0][:, first : first + QUARTER], ADD)
+            nc.vector.tensor_tensor(
+                windows[0][:].indirect(entries(first, QUARTER)), summed[:], edge_w[:, first : first + QUARTER], MULT
+            )
+
+        def piece(nt, half, y, tag):
+            weighted = combine(y[:], own[nt, half], edge_w[:, half * HALF : (half + 1) * HALF], tag)
+            place(nt, half * HALF, HALF, weighted[:])
 
         first_banks = project(0)
         h_quarters = [hidden(first_banks, q * QUARTER, QUARTER, "q%d" % q) for q in range(2)]
         second_banks = project(1)
-        residual(0, 0, J, "rounded2")
-        residual(1, 0, J, "own1")
+        residuals([(0, 0), (0, 1), (1, 0), (1, 1)], "own_first")
+        h_codes = keep.tile([P, J], U32, name="h_codes", tag="res1", align_bytes=64)
         for q in range(2):
             quantise_hidden(q * QUARTER, QUARTER, h_quarters[q])
-            residual(2, q * HALF, HALF, "hq%d" % q)
-            on_vector(q * QUARTER)
-        residual(3, 0, J, "early%d" % QUARTER)
-        second_piece = combine(1, 0, copy_out(1, 0), "weighted10")
-        third_y = copy_out(2, 0)
+            residuals([(2, q)], "planarq%d" % q)
+            early_quarter(q)
+        residuals([(3, 0), (3, 1)], "early1")
+        piece(1, 0, copy_out(1, 0, "y1"), "weighted10")
+        third_y = copy_out(2, 0, "y0")
         h_second = hidden(second_banks, 0, HALF, "second")
-        place(1, 0, second_piece)
         quantise_hidden(HALF, HALF, h_second)
-        place(2, 0, combine(2, 0, third_y, "planarsecond"))
-        place(3, 0, combine(3, 0, copy_out(3, 0), "weighted30"))
+        piece(2, 0, third_y, "planarsecond")
+        piece(3, 0, copy_out(3, 0, "act%d" % (PACK - 1)), "weighted30")
         for nt in range(N_TILES):
-            place(nt, 1, combine(nt, 1, copy_out(nt, 1), "weighted%d1" % nt))
+            piece(nt, 1, copy_out(nt, 1, "y%d" % (nt % 2)), "weighted%d1" % nt)
             nc.sync.dma_start(out=out[nt * P : (nt + 1) * P, :], in_=windows[nt][:])

@@ -27,6 +27,7 @@ HALF = J // 2
 QUARTER = J // 4
 WINDOWS = 4
 SHIFT = 16
+SCALE_LOADS = ((0, 32, 0), (32, 16, 4), (48, 8, 20), (56, 32, 0), (88, 16, 4), (104, 8, 20))
 
 
 def tile_list_msg_gelu_res_resL_kernel(
@@ -54,10 +55,6 @@ def tile_list_msg_gelu_res_resL_kernel(
         planes = (plane0, plane1)
         warm_in = keep.tile([P, 1], F32, name="warm_in", tag="window2")
         warm_out = keep.tile([P, 1], F32, name="warm_out", tag="window3")
-        nc.vector.memset(tab_s[:].bitcast(I32), 0)
-        scale_rows = tab_scales.bitcast(I32).rearrange("a (q r) t -> r q a t", r=PACK)
-        for r in range(PACK):
-            nc.scalar.dma_start(out=tab_s[r:P:SHIFT, :].bitcast(I32), in_=scale_rows[r])
         nc.vector.memset(warm_in[:], 0.0)
         nc.scalar.activation(warm_out[:], warm_in[:], GELU)
         windows = [keep.tile([P, T], F32, name="window%d" % i) for i in range(WINDOWS)]
@@ -66,6 +63,12 @@ def tile_list_msg_gelu_res_resL_kernel(
         nc.vector.memset(plane1[:].bitcast(I32), 0)
 
         nc.sync.dma_start(src_list[:], offs)
+        scale_rows = tab_scales.rearrange("a q t -> (a q) t").bitcast(I32)
+        for first, count, row in SCALE_LOADS:
+            nc.sync.dma_start(out=tab_s[first : first + count, :].bitcast(I32), in_=scale_rows[row : row + count, :])
+        nc.sync.dma_start(
+            out=tab_s[112:P, :].bitcast(I32), in_=scale_rows[28:32, :].unsqueeze(0).broadcast_to([4, 4, T // 4])
+        )
         nc.sync.dma_start(dst_list[:], offs2)
 
         rounded = [

@@ -27,7 +27,6 @@ HALF = J // 2
 QUARTER = J // 4
 WINDOWS = 4
 SHIFT = 16
-SCALE_LOADS = ((0, 32, 0), (32, 16, 4), (48, 8, 20), (56, 32, 0), (88, 16, 4), (104, 8, 20))
 
 
 def tile_list_msg_gelu_res_resL_kernel(
@@ -37,8 +36,8 @@ def tile_list_msg_gelu_res_resL_kernel(
     with ExitStack() as ctx:
         lists = ctx.enter_context(tc.tile_pool(name="lists", bufs=1))
         keep = ctx.enter_context(tc.tile_pool(name="keep", bufs=1))
-        psum_a = ctx.enter_context(tc.psum_pool(name="psum_a", bufs=4))
-        psum_y = ctx.enter_context(tc.psum_pool(name="psum_y", bufs=4))
+        shared = ctx.enter_context(tc.tile_pool(name="shared", bufs=1))
+        psum = ctx.enter_context(tc.psum_pool(name="psum", bufs=8))
 
         src_list = lists.tile([P, J // 16], U16, name="src_list")
         dst_list = lists.tile([P, J // 16], U16, name="dst_list")
@@ -53,77 +52,79 @@ def tile_list_msg_gelu_res_resL_kernel(
         plane0 = keep.tile([P, 2 * J], U8, name="plane0", align_bytes=64)
         plane1 = keep.tile([P, 2 * J], U8, name="plane1", align_bytes=64)
         planes = (plane0, plane1)
-        warm_in = keep.tile([P, 1], F32, name="warm_in", tag="window2")
-        warm_out = keep.tile([P, 1], F32, name="warm_out", tag="window3")
-        nc.vector.memset(warm_in[:], 0.0)
-        nc.scalar.activation(warm_out[:], warm_in[:], GELU)
         windows = [keep.tile([P, T], F32, name="window%d" % i) for i in range(WINDOWS)]
+        for plane in (tab_s[:], plane1[:], wd_s[:].rearrange("p i n -> p (i n)")):
+            nc.gpsimd.memset(plane.bitcast(I32), 0)
         for i in range(WINDOWS):
             (nc.vector if i < 2 else nc.gpsimd).memset(windows[i][:], 0.0)
-        nc.vector.memset(plane1[:].bitcast(I32), 0)
+        warm_out = keep.tile([P, 1], F32, name="warm_out")
+        nc.scalar.activation(warm_out[:], windows[0][:, 0:1], GELU)
 
         nc.sync.dma_start(src_list[:], offs)
-        scale_rows = tab_scales.rearrange("a q t -> (a q) t").bitcast(I32)
-        for first, count, row in SCALE_LOADS:
-            nc.sync.dma_start(out=tab_s[first : first + count, :].bitcast(I32), in_=scale_rows[row : row + count, :])
-        nc.sync.dma_start(
-            out=tab_s[112:P, :].bitcast(I32), in_=scale_rows[28:32, :].unsqueeze(0).broadcast_to([4, 4, T // 4])
-        )
+        nc.sync.dma_start(out=tab_w[:], in_=tab_words[0].rearrange("p t b -> p (t b)").bitcast(I32))
         nc.sync.dma_start(dst_list[:], offs2)
+        scale_rows = tab_scales.bitcast(I32).rearrange("a (q r) t -> r q a t", r=4)
+        for r in range(4):
+            nc.sync.dma_start(out=tab_s[r:P:SHIFT, :].bitcast(I32), in_=scale_rows[r])
 
         rounded = [
             keep.tile([P, R * PACK], BF16, name="rounded", tag="rounded%d" % u, align_bytes=64) for u in range(2 * PASSES)
         ]
 
-        def load_weight(u, first, width):
-            w = (ws, wt)[u // PASSES]
-            a = u % PASSES
-            raw = keep.tile([P, PACK, width], F32, name="raw", tag="raw%d_%d" % (u, first), align_bytes=64)
+        def load_weight(u):
+            a, i = divmod(u, 2)
+            raw = keep.tile([P, PACK, R], F32, name="raw", tag="raw%d" % u, align_bytes=64)
             nc.sync.dma_start(
-                out=raw[:],
-                in_=w[a * K_PASS : (a + 1) * K_PASS, first : first + width].rearrange("(p i) r -> p i r", i=PACK),
+                out=raw[:], in_=(ws, wt)[i][a * K_PASS : (a + 1) * K_PASS, :].rearrange("(p i) r -> p i r", i=PACK)
             )
             nc.scalar.copy(
-                rounded[u][:].rearrange("p (t m i) -> p m t i", t=PACK, i=PACK)[
-                    :, first // PACK : (first + width) // PACK, :, :
-                ],
-                raw[:].rearrange("p i (m t) -> p m t i", t=PACK),
+                rounded[u][:].rearrange("p (t m i) -> p m i t", t=PACK, i=PACK),
+                raw[:].rearrange("p i (m t) -> p m i t", t=PACK),
             )
 
-        load_weight(0, 0, R)
-        load_weight(1, 0, R // 2)
-        nc.sync.dma_start(out=tab_w[:], in_=tab_words[0].rearrange("p t b -> p (t b)").bitcast(I32))
-        load_weight(1, R // 2, R // 2)
-        load_weight(2, 0, R // 2)
-        load_weight(2, R // 2, R // 2)
+        for u in range(2 * PASSES):
+            load_weight(u)
+
+        picked = {}
+        parted = {}
+
+        def pick(i, half, into):
+            picked[i, half] = into
+            nc.vector.tensor_copy(into, tab_w[:].bitcast(U32).indirect(part_of(both[i], half)))
+
+        picked_first = keep.tile([P, 2, HALF], U32, name="picked_first", align_bytes=64)
+        for i in range(2):
+            pick(i, 0, picked_first[:, i, :])
         for i in range(2):
             nc.vector.tensor_copy(plane0[:, i * J : (i + 1) * J], tab_s[:].indirect(both[i][:]))
         nc.sync.dma_start(out=plane1[0 : P - SHIFT, :].bitcast(I32), in_=plane0[SHIFT:P, :].bitcast(I32))
 
-        load_weight(3, 0, R // 2)
-        load_weight(3, R // 2, R // 2)
         sm_t = keep.tile([P, PACK], F32, name="sm_t")
         nc.sync.dma_start(out=sm_t[:], in_=sm.rearrange("(p t) -> p t", t=PACK))
 
-        res = [keep.tile([P, T], F32, name="res", tag="res%d" % nt, align_bytes=64) for nt in range(N_TILES)]
+        res = [keep.tile([P, T], F32, name="res", tag="res%d" % nt, align_bytes=64) for nt in (0, 1, 3)]
+        res = res[:2] + [shared.tile([P, T], F32, name="res2", offset=0, align_bytes=64)] + res[2:]
         wd4 = keep.tile([P, 2 * N], U8, name="wd4", align_bytes=64)
         wd8 = keep.tile([P, N], I32, name="wd8", align_bytes=64)
         edge_w = keep.tile([P, J], F32, name="edge_w")
-        for nt in range(2):
+
+        def load_wd_scales(i, scales):
+            rows = scales[0].bitcast(I32).rearrange("(q r) n -> r q n", r=4)
+            for r in range(4):
+                nc.sync.dma_start(out=wd_s[r:P:32, i, :].bitcast(I32), in_=rows[r])
+
+        def load_state(nt):
             nc.sync.dma_start(out=res[nt][:], in_=rT[nt * P : (nt + 1) * P, :])
+
+        load_wd_scales(0, wd4_scales)
+        load_state(0)
         nc.sync.dma_start(out=wd4[:].bitcast(I32), in_=wd4_words[0].bitcast(I32))
         nc.sync.dma_start(out=wd8[:], in_=wd8_words[0].rearrange("p n b -> p (n b)").bitcast(I32))
-        for i, scales in enumerate((wd4_scales, wd8_scales)):
-            rows = scales[0].bitcast(I32)
-            nc.sync.dma_start(
-                out=wd_s[0:98, i, :].bitcast(I32), in_=rows[0:14, :].unsqueeze(0).broadcast_to([7, 14, N // 4])
-            )
-            nc.sync.dma_start(
-                out=wd_s[98:P, i, :].bitcast(I32), in_=rows[14:16, :].unsqueeze(0).broadcast_to([15, 2, N // 4])
-            )
+        load_wd_scales(1, wd8_scales)
+        load_state(1)
         nc.sync.dma_start(out=edge_w[:], in_=wgo)
-        for nt in range(2, N_TILES):
-            nc.sync.dma_start(out=res[nt][:], in_=rT[nt * P : (nt + 1) * P, :])
+        load_state(2)
+        load_state(3)
 
         w_codes = keep.tile([P, 2 * PASSES, R], U32, name="w_codes", align_bytes=64)
         w_scales = keep.tile([P, 2 * PASSES, R], U8, name="w_scales", align_bytes=64)
@@ -131,45 +132,37 @@ def tile_list_msg_gelu_res_resL_kernel(
         def quantise_weight(u):
             nc.vector.quantize_mx(out=w_codes[:, u, :].bitcast(FP8X4), scales=w_scales[:, u, :], in_=rounded[u][:])
 
-        picked = {}
-        parted = {}
-
-        def pick(i, half, tag):
-            picked[i, half] = keep.tile([P, HALF], U32, name="picked", tag=tag, align_bytes=64)
-            nc.vector.tensor_copy(picked[i, half][:], tab_w[:].bitcast(U32).indirect(part_of(both[i], half)))
-
         def part(i, half, into):
             parted[i, half] = into[:, i * PASSES * 2 * HALF : (i + 1) * PASSES * 2 * HALF]
             nc.vector.tensor_copy(
                 parted[i, half].bitcast(U16).rearrange("p (d j) -> p d j", d=PASSES),
-                picked[i, half][:].bitcast(U16).rearrange("p (j d) -> p d j", d=PASSES),
+                picked[i, half].bitcast(U16).rearrange("p (j d) -> p d j", d=PASSES),
             )
 
         quantise_weight(0)
-        for i in range(2):
-            pick(i, 0, "picked%d" % i)
-        parted_first = keep.tile([P, 2 * PASSES * 2 * HALF], U8, name="parted_first", align_bytes=64)
+        parted_first = keep.tile([P, 2 * PASSES * 2 * HALF], U8, name="parted_first", tag="raw0", align_bytes=64)
         for i in range(2):
             part(i, 0, parted_first)
         quantise_weight(1)
-        pick(0, 1, "raw1_%d" % (R // 2))
+        picked_second = keep.tile([P, 2, HALF], U32, name="picked_second", tag="raw1", align_bytes=64)
+        for i in range(2):
+            pick(i, 1, picked_second[:, i, :])
         quantise_weight(2)
-        pick(1, 1, "raw2_%d" % (R // 2))
         quantise_weight(3)
-        parted_second = keep.tile([P, 2 * PASSES * 2 * HALF], U8, name="parted_second", tag="raw3_%d" % (R // 2), align_bytes=64)
+        parted_second = keep.tile([P, 2 * PASSES * 2 * HALF], U8, name="parted_second", tag="raw3", align_bytes=64)
         for i in range(2):
             part(i, 1, parted_second)
 
         h_scales = keep.tile([P, J], U8, name="h_scales", align_bytes=64)
 
         def project(half):
-            banks = [psum_a.tile([P, HALF], F32, name="a_ps") for t in range(PACK)]
+            banks = [psum.tile([P, HALF], F32, name="a_ps", tag="bank") for t in range(PACK)]
             first = half * HALF
             steps = [(u, t) for u in range(2 * PASSES) for t in range(PACK)]
             if half == 1:
                 steps = [(u, t) for t in range(PACK) for u in range(2 * PASSES)]
             for u, t in steps:
-                i, a = divmod(u, PASSES)
+                a, i = divmod(u, 2)
                 start = a * HALF * 2
                 nc.tensor.matmul_mx(
                     out=banks[t][:],
@@ -182,37 +175,38 @@ def tile_list_msg_gelu_res_resL_kernel(
                 )
             return banks
 
-        def hidden(banks, first, width, label):
+        def hidden(banks, first, width, label, make_act, h):
             planar = keep.tile([P, PACK, width], BF16, name="planar", tag="planar" + label, align_bytes=64)
             acts = []
             for t in range(PACK + 1):
                 if t < PACK:
-                    act = keep.tile([P, width], F32, name="act", tag="act%d" % t, align_bytes=64)
+                    act = make_act(t, width)
                     nc.scalar.activation(act[:], banks[t][:, first : first + width], GELU)
                     acts.append(act)
                 if t > 0:
                     nc.scalar.activation(planar[:, t - 1, :], acts[t - 1][:], COPY, scale=sm_t[:, t - 1 : t])
-            h = keep.tile([P, width * PACK], BF16, name="h", tag="h" + label, align_bytes=64)
             nc.scalar.copy(
-                h[:].rearrange("p (c i t) -> p c t i", i=4, t=PACK),
+                h.rearrange("p (c i t) -> p c t i", i=4, t=PACK),
                 planar[:].rearrange("p t (c i) -> p c t i", i=4),
             )
-            return h
+
+        codes = {}
 
         def quantise_hidden(first, width, h):
-            cols = slice(first, first + width)
-            nc.vector.quantize_mx(out=h_codes[:, cols].bitcast(FP8X4), scales=h_scales[:, cols], in_=h[:])
+            nc.vector.quantize_mx(out=codes[first][:].bitcast(FP8X4), scales=h_scales[:, first : first + width], in_=h)
 
-        def message(into, nt, cols):
+        def message(into, nt, first, inside, width):
+            rhs = codes[first][:, inside : inside + width].bitcast(FP8X4)
+            rhs_scale = h_scales[:, first + inside : first + inside + width]
             nc.tensor.matmul_mx(
                 out=into, lhsT=wd4[:, 2 * nt * P : 2 * (nt + 1) * P].bitcast(FP4X4),
                 lhsT_scale=wd_s[:, 0, nt * P : (nt + 1) * P],
-                rhs=h_codes[:, cols].bitcast(FP8X4), rhs_scale=h_scales[:, cols], start=True, stop=False,
+                rhs=rhs, rhs_scale=rhs_scale, start=True, stop=False,
             )
             nc.tensor.matmul_mx(
                 out=into, lhsT=wd8[:, nt * P : (nt + 1) * P].bitcast(FP8X4),
                 lhsT_scale=wd_s[:, 1, nt * P : (nt + 1) * P],
-                rhs=h_codes[:, cols].bitcast(FP8X4), rhs_scale=h_scales[:, cols], start=False, stop=True,
+                rhs=rhs, rhs_scale=rhs_scale, start=False, stop=True,
             )
 
         def entries(first, width):
@@ -220,16 +214,18 @@ def tile_list_msg_gelu_res_resL_kernel(
 
         own = {}
 
-        def residuals(parts, tag):
-            held = keep.tile([P, len(parts), HALF], F32, name="own", tag=tag, align_bytes=64)
+        def residuals(parts, held):
             for slot, (nt, half) in enumerate(parts):
                 nc.vector.tensor_copy(held[:, slot, :], res[nt][:].indirect(part_of(dst_list, half)))
                 own[nt, half] = held[:, slot, :]
-            return held
 
         def copy_out(nt, half, tag):
-            y_ps = psum_y.tile([P, HALF], F32, name="y_ps")
-            message(y_ps[:], nt, slice(half * HALF, (half + 1) * HALF))
+            y_ps = psum.tile([P, HALF], F32, name="y_ps", tag="bank")
+            if half == 0:
+                for c in range(0, HALF, P):
+                    message(y_ps[:, c : c + P], nt, c // QUARTER * QUARTER, c % QUARTER, P)
+            else:
+                message(y_ps[:], nt, HALF, 0, HALF)
             y = keep.tile([P, HALF], F32, name="y", tag=tag, align_bytes=64)
             nc.scalar.copy(y[:], y_ps[:])
             return y
@@ -244,37 +240,62 @@ def tile_list_msg_gelu_res_resL_kernel(
         def place(nt, first, width, weighted):
             nc.vector.tensor_copy(windows[nt][:].indirect(entries(first, width)), weighted)
 
-        def early_quarter(q):
+        def add_early(q, summed):
             first = q * QUARTER
-            y_ps = psum_y.tile([P, QUARTER], F32, name="y_ps")
+            y_ps = psum.tile([P, QUARTER], F32, name="y_ps", tag="bank")
             for c in range(0, QUARTER, P):
-                message(y_ps[:, c : c + P], 0, slice(first + c, first + c + P))
-            summed = keep.tile([P, QUARTER], F32, name="early", tag="early%d" % q, align_bytes=64)
-            nc.vector.tensor_tensor(summed[:], y_ps[:], own[0, 0][:, first : first + QUARTER], ADD)
+                message(y_ps[:, c : c + P], 0, first, c, P)
+            nc.vector.tensor_tensor(summed, y_ps[:], own[0, 0][:, first : first + QUARTER], ADD)
+
+        def place_early(q, summed):
+            first = q * QUARTER
             nc.vector.tensor_tensor(
-                windows[0][:].indirect(entries(first, QUARTER)), summed[:], edge_w[:, first : first + QUARTER], MULT
+                windows[0][:].indirect(entries(first, QUARTER)), summed, edge_w[:, first : first + QUARTER], MULT
             )
 
         def piece(nt, half, y, tag):
             weighted = combine(y[:], own[nt, half], edge_w[:, half * HALF : (half + 1) * HALF], tag)
             place(nt, half * HALF, HALF, weighted[:])
 
+        def act_tile(t, width):
+            return keep.tile([P, width], F32, name="act", tag="act%d" % t, align_bytes=64)
+
         first_banks = project(0)
-        h_quarters = [hidden(first_banks, q * QUARTER, QUARTER, "q%d" % q) for q in range(2)]
+        h_first = keep.tile([P, QUARTER * PACK], BF16, name="h_first", align_bytes=64)
+        hidden(first_banks, 0, QUARTER, "q0", act_tile, h_first[:])
+        h_next = shared.tile([P, QUARTER * PACK], BF16, name="h_next", offset=9216, align_bytes=64)
+        hidden(first_banks, QUARTER, QUARTER, "q1", act_tile, h_next[:])
         second_banks = project(1)
-        residuals([(0, 0), (0, 1), (1, 0), (1, 1)], "own_first")
-        h_codes = keep.tile([P, J], U32, name="h_codes", tag="res1", align_bytes=64)
-        for q in range(2):
-            quantise_hidden(q * QUARTER, QUARTER, h_quarters[q])
-            residuals([(2, q)], "planarq%d" % q)
-            early_quarter(q)
-        residuals([(3, 0), (3, 1)], "early1")
+        residuals([(0, 0), (0, 1), (1, 0), (1, 1)], keep.tile([P, 4, HALF], F32, name="own_first"))
+        codes[0] = keep.tile([P, QUARTER], U32, name="codes0", tag="res1", align_bytes=64)
+        quantise_hidden(0, QUARTER, h_first[:])
+        residuals([(2, 0), (2, 1)], keep.tile([P, 2, HALF], F32, name="own_third"))
+        early0 = shared.tile([P, QUARTER], F32, name="early0", offset=0, align_bytes=64)
+        add_early(0, early0[:])
+        codes[QUARTER] = shared.tile([P, QUARTER], U32, name="codes1", offset=1024, align_bytes=64)
+        quantise_hidden(QUARTER, QUARTER, h_next[:])
+        place_early(0, early0[:])
+        residuals([(3, 0)], shared.tile([P, 1, HALF], F32, name="own_30", offset=8192, align_bytes=64))
+        residuals([(3, 1)], keep.tile([P, 1, HALF], F32, name="own_31"))
+        early1 = keep.tile([P, QUARTER], F32, name="early1")
+        add_early(1, early1[:])
+        place_early(1, early1[:])
         piece(1, 0, copy_out(1, 0, "y1"), "weighted10")
         third_y = copy_out(2, 0, "y0")
-        h_second = hidden(second_banks, 0, HALF, "second")
-        quantise_hidden(HALF, HALF, h_second)
+        h_second = keep.tile([P, HALF * PACK], BF16, name="h_second", align_bytes=64)
+
+        def gated_act(t, width):
+            if t == 2:
+                return shared.tile([P, width], F32, name="act_gated", offset=10240, align_bytes=64)
+            if t == 3:
+                return keep.tile([P, width], F32, name="act_last", tag="y1", align_bytes=64)
+            return act_tile(t, width)
+
+        hidden(second_banks, 0, HALF, "second", gated_act, h_second[:])
+        codes[HALF] = keep.tile([P, HALF], U32, name="codes2", align_bytes=64)
+        quantise_hidden(HALF, HALF, h_second[:])
         piece(2, 0, third_y, "planarsecond")
-        piece(3, 0, copy_out(3, 0, "act%d" % (PACK - 1)), "weighted30")
+        piece(3, 0, copy_out(3, 0, "y1"), "weighted30")
         for nt in range(N_TILES):
             piece(nt, 1, copy_out(nt, 1, "y%d" % (nt % 2)), "weighted%d1" % nt)
             nc.sync.dma_start(out=out[nt * P : (nt + 1) * P, :], in_=windows[nt][:])

@@ -1,6 +1,7 @@
 from contextlib import ExitStack
 
 import concourse.mybir as mybir
+from concourse.masks import make_identity
 
 K, R, N, T, J = 1024, 512, 512, 2048, 1024
 FLOPS = 2 * J * (2 * K * R + 2 * R * N)
@@ -37,7 +38,7 @@ def tile_list_msg_gelu_res_resL_kernel(
         lists = ctx.enter_context(tc.tile_pool(name="lists", bufs=1))
         keep = ctx.enter_context(tc.tile_pool(name="keep", bufs=1))
         shared = ctx.enter_context(tc.tile_pool(name="shared", bufs=1))
-        psum = ctx.enter_context(tc.psum_pool(name="psum", bufs=8))
+        psum = ctx.enter_context(tc.psum_pool(name="psum", bufs=1))
 
         src_list = lists.tile([P, J // 16], U16, name="src_list")
         dst_list = lists.tile([P, J // 16], U16, name="dst_list")
@@ -47,7 +48,7 @@ def tile_list_msg_gelu_res_resL_kernel(
             return one_list[:, half * HALF // 16 : (half + 1) * HALF // 16]
 
         tab_w = keep.tile([P, T], I32, name="tab_w", align_bytes=64)
-        tab_s = keep.tile([P, T], U8, name="tab_s", align_bytes=64)
+        tab_s = keep.tile([P, T], U8, name="tab_s", tag="tab_s", align_bytes=64)
         wd_s = keep.tile([P, 2, N], U8, name="wd_s", align_bytes=64)
         plane0 = keep.tile([P, 2 * J], U8, name="plane0", align_bytes=64)
         plane1 = keep.tile([P, 2 * J], U8, name="plane1", align_bytes=64)
@@ -57,15 +58,10 @@ def tile_list_msg_gelu_res_resL_kernel(
             nc.gpsimd.memset(plane.bitcast(I32), 0)
         for i in range(WINDOWS):
             (nc.vector if i < 2 else nc.gpsimd).memset(windows[i][:], 0.0)
+        identity = keep.tile([P, P], F32, name="identity")
+        make_identity(nc, identity[:])
         warm_out = keep.tile([P, 1], F32, name="warm_out")
         nc.scalar.activation(warm_out[:], windows[0][:, 0:1], GELU)
-
-        nc.sync.dma_start(src_list[:], offs)
-        nc.sync.dma_start(out=tab_w[:], in_=tab_words[0].rearrange("p t b -> p (t b)").bitcast(I32))
-        nc.sync.dma_start(dst_list[:], offs2)
-        scale_rows = tab_scales.bitcast(I32).rearrange("a (q r) t -> r q a t", r=4)
-        for r in range(4):
-            nc.sync.dma_start(out=tab_s[r:P:SHIFT, :].bitcast(I32), in_=scale_rows[r])
 
         rounded = [
             keep.tile([P, R * PACK], BF16, name="rounded", tag="rounded%d" % u, align_bytes=64) for u in range(2 * PASSES)
@@ -82,8 +78,25 @@ def tile_list_msg_gelu_res_resL_kernel(
                 raw[:].rearrange("p i (m t) -> p m i t", t=PACK),
             )
 
-        for u in range(2 * PASSES):
-            load_weight(u)
+        def load_wd_scales(i, scales):
+            rows = scales[0].bitcast(I32).rearrange("(q r) n -> r q n", r=4)
+            for r in range(4):
+                nc.sync.dma_start(out=wd_s[r:P:32, i, :].bitcast(I32), in_=rows[r])
+
+        nc.sync.dma_start(src_list[:], offs)
+        nc.sync.dma_start(out=tab_w[:], in_=tab_words[0].rearrange("p t b -> p (t b)").bitcast(I32))
+        nc.sync.dma_start(dst_list[:], offs2)
+        sm_t = keep.tile([P, PACK], F32, name="sm_t")
+        nc.sync.dma_start(out=sm_t[:], in_=sm.rearrange("(p t) -> p t", t=PACK))
+        scale_rows = tab_scales.bitcast(I32).rearrange("a (q r) t -> r q a t", r=4)
+        for r in range(4):
+            nc.sync.dma_start(out=tab_s[r:P:SHIFT, :].bitcast(I32), in_=scale_rows[r])
+        load_weight(0)
+        load_weight(1)
+        load_wd_scales(0, wd4_scales)
+        load_weight(2)
+        load_wd_scales(1, wd8_scales)
+        load_weight(3)
 
         picked = {}
         parted = {}
@@ -99,38 +112,31 @@ def tile_list_msg_gelu_res_resL_kernel(
             nc.vector.tensor_copy(plane0[:, i * J : (i + 1) * J], tab_s[:].indirect(both[i][:]))
         nc.sync.dma_start(out=plane1[0 : P - SHIFT, :].bitcast(I32), in_=plane0[SHIFT:P, :].bitcast(I32))
 
-        sm_t = keep.tile([P, PACK], F32, name="sm_t")
-        nc.sync.dma_start(out=sm_t[:], in_=sm.rearrange("(p t) -> p t", t=PACK))
-
-        res = [keep.tile([P, T], F32, name="res", tag="res%d" % nt, align_bytes=64) for nt in (0, 1, 3)]
-        res = res[:2] + [shared.tile([P, T], F32, name="res2", offset=0, align_bytes=64)] + res[2:]
+        res = [keep.tile([P, T], F32, name="res", tag="res%d" % nt, align_bytes=64) for nt in range(N_TILES)]
         wd4 = keep.tile([P, 2 * N], U8, name="wd4", align_bytes=64)
         wd8 = keep.tile([P, N], I32, name="wd8", align_bytes=64)
         edge_w = keep.tile([P, J], F32, name="edge_w")
 
-        def load_wd_scales(i, scales):
-            rows = scales[0].bitcast(I32).rearrange("(q r) n -> r q n", r=4)
-            for r in range(4):
-                nc.sync.dma_start(out=wd_s[r:P:32, i, :].bitcast(I32), in_=rows[r])
-
         def load_state(nt):
             nc.sync.dma_start(out=res[nt][:], in_=rT[nt * P : (nt + 1) * P, :])
 
-        load_wd_scales(0, wd4_scales)
+        edge_col = keep.tile([P, J // P], F32, name="edge_col")
+        nc.sync.dma_start(out=edge_w[:], in_=wgo)
         load_state(0)
+        with nc.allow_non_contiguous_dma(reason="one edge weight a partition"):
+            nc.sync.dma_start(out=edge_col[:], in_=wgo[0].rearrange("(c p) -> p c", p=P))
         nc.sync.dma_start(out=wd4[:].bitcast(I32), in_=wd4_words[0].bitcast(I32))
         nc.sync.dma_start(out=wd8[:], in_=wd8_words[0].rearrange("p n b -> p (n b)").bitcast(I32))
-        load_wd_scales(1, wd8_scales)
         load_state(1)
-        nc.sync.dma_start(out=edge_w[:], in_=wgo)
         load_state(2)
         load_state(3)
 
-        w_codes = keep.tile([P, 2 * PASSES, R], U32, name="w_codes", align_bytes=64)
+        w_codes = {}
         w_scales = keep.tile([P, 2 * PASSES, R], U8, name="w_scales", align_bytes=64)
 
         def quantise_weight(u):
-            nc.vector.quantize_mx(out=w_codes[:, u, :].bitcast(FP8X4), scales=w_scales[:, u, :], in_=rounded[u][:])
+            w_codes[u] = keep.tile([P, R], U32, name="w_codes", tag="w_codes%d" % u, align_bytes=64)
+            nc.vector.quantize_mx(out=w_codes[u][:].bitcast(FP8X4), scales=w_scales[:, u, :], in_=rounded[u][:])
 
         def part(i, half, into):
             parted[i, half] = into[:, i * PASSES * 2 * HALF : (i + 1) * PASSES * 2 * HALF]
@@ -155,8 +161,11 @@ def tile_list_msg_gelu_res_resL_kernel(
 
         h_scales = keep.tile([P, J], U8, name="h_scales", align_bytes=64)
 
+        def bank(k, shape):
+            return psum.tile(shape, F32, name="bank", tag="bank%d" % k)
+
         def project(half):
-            banks = [psum.tile([P, HALF], F32, name="a_ps", tag="bank") for t in range(PACK)]
+            banks = [bank(half * PACK + t, [P, HALF]) for t in range(PACK)]
             first = half * HALF
             steps = [(u, t) for u in range(2 * PASSES) for t in range(PACK)]
             if half == 1:
@@ -166,7 +175,7 @@ def tile_list_msg_gelu_res_resL_kernel(
                 start = a * HALF * 2
                 nc.tensor.matmul_mx(
                     out=banks[t][:],
-                    lhsT=w_codes[:, u, t * P : (t + 1) * P].bitcast(FP8X4),
+                    lhsT=w_codes[u][:, t * P : (t + 1) * P].bitcast(FP8X4),
                     lhsT_scale=w_scales[:, u, t * P : (t + 1) * P],
                     rhs=parted[i, half][:, start : start + 2 * HALF].bitcast(FP4X4),
                     rhs_scale=planes[a][:, i * J + first : i * J + first + HALF],
@@ -175,127 +184,123 @@ def tile_list_msg_gelu_res_resL_kernel(
                 )
             return banks
 
-        def hidden(banks, first, width, label, make_act, h):
-            planar = keep.tile([P, PACK, width], BF16, name="planar", tag="planar" + label, align_bytes=64)
-            acts = []
-            for t in range(PACK + 1):
-                if t < PACK:
-                    act = make_act(t, width)
-                    nc.scalar.activation(act[:], banks[t][:, first : first + width], GELU)
-                    acts.append(act)
-                if t > 0:
-                    nc.scalar.activation(planar[:, t - 1, :], acts[t - 1][:], COPY, scale=sm_t[:, t - 1 : t])
+        def smooth(planar, act, t, first, width):
+            nc.scalar.activation(planar[:, t, :], act[:, t, first : first + width], COPY, scale=sm_t[:, t : t + 1])
+
+        def interleave(planar, width, name):
+            h = keep.tile([P, width * PACK], BF16, name=name, tag=name, align_bytes=64)
             nc.scalar.copy(
-                h.rearrange("p (c i t) -> p c t i", i=4, t=PACK),
+                h[:].rearrange("p (c i t) -> p c t i", i=4, t=PACK),
                 planar[:].rearrange("p t (c i) -> p c t i", i=4),
             )
+            return h
 
-        codes = {}
+        def hidden(banks, planar, width, name, tag):
+            acts = keep.tile([P, PACK, HALF], F32, name="acts", tag=tag, align_bytes=64)
+            for t in range(PACK + 1):
+                if t < PACK:
+                    nc.scalar.activation(acts[:, t, :], banks[t][:], GELU)
+                if t > 0:
+                    smooth(planar, acts, t - 1, 0, width)
+            return acts, interleave(planar, width, name)
 
-        def quantise_hidden(first, width, h):
-            nc.vector.quantize_mx(out=codes[first][:].bitcast(FP8X4), scales=h_scales[:, first : first + width], in_=h)
+        def quantise_hidden(first, width, h, tag):
+            codes = keep.tile([P, width], U32, name="codes", tag=tag, align_bytes=64)
+            nc.vector.quantize_mx(out=codes[:].bitcast(FP8X4), scales=h_scales[:, first : first + width], in_=h[:])
+            return codes
 
-        def message(into, nt, first, inside, width):
-            rhs = codes[first][:, inside : inside + width].bitcast(FP8X4)
-            rhs_scale = h_scales[:, first + inside : first + inside + width]
+        scaled = {}
+
+        def message(codes, first, edge_tile, k):
+            inside = edge_tile * P - first
+            y_ps = bank(k, [P, N])
+            lhsT = codes[:, inside : inside + P].bitcast(FP8X4)
+            lhsT_scale = h_scales[:, edge_tile * P : (edge_tile + 1) * P]
             nc.tensor.matmul_mx(
-                out=into, lhsT=wd4[:, 2 * nt * P : 2 * (nt + 1) * P].bitcast(FP4X4),
-                lhsT_scale=wd_s[:, 0, nt * P : (nt + 1) * P],
-                rhs=rhs, rhs_scale=rhs_scale, start=True, stop=False,
+                out=y_ps[:], lhsT=lhsT, lhsT_scale=lhsT_scale,
+                rhs=wd4[:].bitcast(FP4X4), rhs_scale=wd_s[:, 0, :], start=True, stop=False,
             )
             nc.tensor.matmul_mx(
-                out=into, lhsT=wd8[:, nt * P : (nt + 1) * P].bitcast(FP8X4),
-                lhsT_scale=wd_s[:, 1, nt * P : (nt + 1) * P],
-                rhs=rhs, rhs_scale=rhs_scale, start=False, stop=True,
+                out=y_ps[:], lhsT=lhsT, lhsT_scale=lhsT_scale,
+                rhs=wd8[:].bitcast(FP8X4), rhs_scale=wd_s[:, 1, :], start=False, stop=True,
             )
+            scaled[edge_tile] = keep.tile([P, N], F32, name="scaled", tag="scaled%d" % edge_tile)
+            nc.scalar.activation(scaled[edge_tile][:], y_ps[:], COPY, scale=edge_col[:, edge_tile : edge_tile + 1])
 
-        def entries(first, width):
-            return dst_list[:, first // 16 : (first + width) // 16]
+        def turn(blocks, k, into):
+            t_ps = bank(k, [P, len(blocks) * P])
+            for slot, (nt, edge_tile) in enumerate(blocks):
+                nc.tensor.transpose(
+                    t_ps[:, slot * P : (slot + 1) * P], scaled[edge_tile][:, nt * P : (nt + 1) * P], identity[:]
+                )
+            nc.scalar.copy(into[:], t_ps[:])
+            return into
 
         own = {}
 
-        def residuals(parts, held):
-            for slot, (nt, half) in enumerate(parts):
-                nc.vector.tensor_copy(held[:, slot, :], res[nt][:].indirect(part_of(dst_list, half)))
-                own[nt, half] = held[:, slot, :]
-
-        def copy_out(nt, half, tag):
-            y_ps = psum.tile([P, HALF], F32, name="y_ps", tag="bank")
-            if half == 0:
-                for c in range(0, HALF, P):
-                    message(y_ps[:, c : c + P], nt, c // QUARTER * QUARTER, c % QUARTER, P)
-            else:
-                message(y_ps[:], nt, HALF, 0, HALF)
-            y = keep.tile([P, HALF], F32, name="y", tag=tag, align_bytes=64)
-            nc.scalar.copy(y[:], y_ps[:])
-            return y
-
-        def combine(y, state, weight, tag):
-            summed = keep.tile(list(y.shape), F32, name="summed")
-            weighted = keep.tile(list(y.shape), F32, name="weighted", tag=tag, align_bytes=64)
-            nc.gpsimd.tensor_tensor(summed[:], y, state, ADD)
-            nc.gpsimd.tensor_tensor(weighted[:], summed[:], weight, MULT)
-            return weighted
-
-        def place(nt, first, width, weighted):
-            nc.vector.tensor_copy(windows[nt][:].indirect(entries(first, width)), weighted)
-
-        def add_early(q, summed):
-            first = q * QUARTER
-            y_ps = psum.tile([P, QUARTER], F32, name="y_ps", tag="bank")
-            for c in range(0, QUARTER, P):
-                message(y_ps[:, c : c + P], 0, first, c, P)
-            nc.vector.tensor_tensor(summed, y_ps[:], own[0, 0][:, first : first + QUARTER], ADD)
-
-        def place_early(q, summed):
-            first = q * QUARTER
+        def residual(nt, half, into):
             nc.vector.tensor_tensor(
-                windows[0][:].indirect(entries(first, QUARTER)), summed, edge_w[:, first : first + QUARTER], MULT
+                into, res[nt][:].indirect(part_of(dst_list, half)), edge_w[:, half * HALF : (half + 1) * HALF], MULT
+            )
+            own[nt, half] = into
+
+        def place(nt, first, width, y):
+            inside = first % HALF
+            nc.vector.tensor_tensor(
+                windows[nt][:].indirect(dst_list[:, first // 16 : (first + width) // 16]),
+                y, own[nt, first // HALF][:, inside : inside + width], ADD,
             )
 
-        def piece(nt, half, y, tag):
-            weighted = combine(y[:], own[nt, half], edge_w[:, half * HALF : (half + 1) * HALF], tag)
-            place(nt, half * HALF, HALF, weighted[:])
+        def piece(name, width=HALF):
+            return keep.tile([P, width], F32, name=name)
 
-        def act_tile(t, width):
-            return keep.tile([P, width], F32, name="act", tag="act%d" % t, align_bytes=64)
+        def gated(name, shape, dtype, offset):
+            return shared.tile(shape, dtype, name=name, offset=offset, align_bytes=64)
 
+        def quarter_pieces(q, tiles, k, into):
+            y = turn([(nt, e) for nt in tiles for e in (2 * q, 2 * q + 1)], k, into)
+            for slot, nt in enumerate(tiles):
+                place(nt, q * QUARTER, QUARTER, y[:, slot * QUARTER : (slot + 1) * QUARTER])
+
+        planar_shape = [P, PACK, QUARTER]
         first_banks = project(0)
-        h_first = keep.tile([P, QUARTER * PACK], BF16, name="h_first", align_bytes=64)
-        hidden(first_banks, 0, QUARTER, "q0", act_tile, h_first[:])
-        h_next = shared.tile([P, QUARTER * PACK], BF16, name="h_next", offset=9216, align_bytes=64)
-        hidden(first_banks, QUARTER, QUARTER, "q1", act_tile, h_next[:])
+        acts, h0 = hidden(first_banks, gated("planar0", planar_shape, BF16, 3072), QUARTER, "h0", "acts0")
         second_banks = project(1)
-        residuals([(0, 0), (0, 1), (1, 0), (1, 1)], keep.tile([P, 4, HALF], F32, name="own_first"))
-        codes[0] = keep.tile([P, QUARTER], U32, name="codes0", tag="res1", align_bytes=64)
-        quantise_hidden(0, QUARTER, h_first[:])
-        residuals([(2, 0), (2, 1)], keep.tile([P, 2, HALF], F32, name="own_third"))
-        early0 = shared.tile([P, QUARTER], F32, name="early0", offset=0, align_bytes=64)
-        add_early(0, early0[:])
-        codes[QUARTER] = shared.tile([P, QUARTER], U32, name="codes1", offset=1024, align_bytes=64)
-        quantise_hidden(QUARTER, QUARTER, h_next[:])
-        place_early(0, early0[:])
-        residuals([(3, 0)], shared.tile([P, 1, HALF], F32, name="own_30", offset=8192, align_bytes=64))
-        residuals([(3, 1)], keep.tile([P, 1, HALF], F32, name="own_31"))
-        early1 = keep.tile([P, QUARTER], F32, name="early1")
-        add_early(1, early1[:])
-        place_early(1, early1[:])
-        piece(1, 0, copy_out(1, 0, "y1"), "weighted10")
-        third_y = copy_out(2, 0, "y0")
-        h_second = keep.tile([P, HALF * PACK], BF16, name="h_second", align_bytes=64)
-
-        def gated_act(t, width):
-            if t == 2:
-                return shared.tile([P, width], F32, name="act_gated", offset=10240, align_bytes=64)
-            if t == 3:
-                return keep.tile([P, width], F32, name="act_last", tag="y1", align_bytes=64)
-            return act_tile(t, width)
-
-        hidden(second_banks, 0, HALF, "second", gated_act, h_second[:])
-        codes[HALF] = keep.tile([P, HALF], U32, name="codes2", align_bytes=64)
-        quantise_hidden(HALF, HALF, h_second[:])
-        piece(2, 0, third_y, "planarsecond")
-        piece(3, 0, copy_out(3, 0, "y1"), "weighted30")
+        own_first = keep.tile([P, 4, HALF], F32, name="own_first")
+        for slot in range(4):
+            residual(slot // 2, slot % 2, own_first[:, slot, :])
+        codes = quantise_hidden(0, QUARTER, h0, "res1")
+        own_third = gated("own_third", [P, 2, HALF], F32, 0)
+        for half in range(2):
+            residual(2, half, own_third[:, half, :])
+        message(codes, 0, 0, 0)
+        message(codes, 0, 1, 1)
+        planar1 = gated("planar1", planar_shape, BF16, 4096)
+        for t in range(PACK):
+            smooth(planar1, acts, t, QUARTER, QUARTER)
+        codes = quantise_hidden(QUARTER, QUARTER, interleave(planar1, QUARTER, "h1"), "res2")
+        own_fourth = gated("own_fourth", [P, 2, HALF], F32, 5120)
+        for half in range(2):
+            residual(3, half, own_fourth[:, half, :])
+        quarter_pieces(0, (0, 1), 2, piece("y_00"))
+        quarter_pieces(0, (2, 3), 3, piece("y_02"))
+        message(codes, QUARTER, 2, 0)
+        message(codes, QUARTER, 3, 1)
+        quarter_pieces(1, (0,), 2, piece("y_10", QUARTER))
+        planar2 = keep.tile(planar_shape, BF16, name="planar2", tag="planar2", align_bytes=64)
+        acts, h2 = hidden(second_banks, planar2, QUARTER, "h2", "h1")
+        codes = quantise_hidden(HALF, QUARTER, h2, "codes2")
+        quarter_pieces(1, (1, 2), 3, keep.tile([P, HALF], F32, name="y_11", tag="planar2", align_bytes=64))
+        planar3 = keep.tile(planar_shape, BF16, name="planar3", tag="planar3", align_bytes=64)
+        for t in range(PACK):
+            smooth(planar3, acts, t, QUARTER, QUARTER)
+        last_codes = quantise_hidden(HALF + QUARTER, QUARTER, interleave(planar3, QUARTER, "h3"), "codes3")
+        quarter_pieces(1, (3,), 0, keep.tile([P, QUARTER], F32, name="y_13", tag="planar3", align_bytes=64))
+        for q, made in ((2, codes), (3, last_codes)):
+            for e in (2 * q, 2 * q + 1):
+                message(made, q * QUARTER, e, e)
+            quarter_pieces(q, (0, 1), q - 1, piece("y_q%d" % q))
         for nt in range(N_TILES):
-            piece(nt, 1, copy_out(nt, 1, "y%d" % (nt % 2)), "weighted%d1" % nt)
+            if nt >= 2:
+                place(nt, HALF, HALF, turn([(nt, e) for e in range(4, 8)], (nt + 1) % 4, piece("y_%d1" % nt))[:])
             nc.sync.dma_start(out=out[nt * P : (nt + 1) * P, :], in_=windows[nt][:])

@@ -26,7 +26,6 @@ PASSES = K // K_PASS
 N_TILES = N // P
 HALF = J // 2
 QUARTER = J // 4
-WINDOWS = 4
 SHIFT = 16
 
 
@@ -53,11 +52,16 @@ def tile_list_msg_gelu_res_resL_kernel(
         plane0 = keep.tile([P, 2 * J], U8, name="plane0", align_bytes=64)
         plane1 = keep.tile([P, 2 * J], U8, name="plane1", align_bytes=64)
         planes = (plane0, plane1)
-        windows = [keep.tile([P, T], F32, name="window%d" % i) for i in range(WINDOWS)]
+        windows = {nt: keep.tile([P, T], F32, name="window%d" % nt) for nt in range(2)}
         for plane in (tab_s[:], plane1[:], wd_s[:].rearrange("p i n -> p (i n)")):
-            nc.gpsimd.memset(plane.bitcast(I32), 0)
-        for i in range(WINDOWS):
-            (nc.vector if i < 2 else nc.gpsimd).memset(windows[i][:], 0.0)
+            nc.vector.memset(plane.bitcast(I32), 0)
+        for nt in range(2):
+            nc.vector.memset(windows[nt][:], 0.0)
+
+        def late_window(nt, tag):
+            windows[nt] = keep.tile([P, T], F32, name="late_window", tag=tag, align_bytes=64)
+            nc.gpsimd.memset(windows[nt][:], 0.0)
+
         identity = keep.tile([P, P], F32, name="identity")
         make_identity(nc, identity[:])
         warm_out = keep.tile([P, 1], F32, name="warm_out")
@@ -158,6 +162,7 @@ def tile_list_msg_gelu_res_resL_kernel(
         parted_second = keep.tile([P, 2 * PASSES * 2 * HALF], U8, name="parted_second", tag="raw3", align_bytes=64)
         for i in range(2):
             part(i, 1, parted_second)
+        late_window(2, "raw1")
 
         h_scales = keep.tile([P, J], U8, name="h_scales", align_bytes=64)
 
@@ -282,6 +287,7 @@ def tile_list_msg_gelu_res_resL_kernel(
         own_fourth = gated("own_fourth", [P, 2, HALF], F32, 5120)
         for half in range(2):
             residual(3, half, own_fourth[:, half, :])
+        late_window(3, "res3")
         quarter_pieces(0, (0, 1), 2, piece("y_00"))
         quarter_pieces(0, (2, 3), 3, piece("y_02"))
         message(codes, QUARTER, 2, 0)

@@ -78,8 +78,8 @@ def tile_list_msg_gelu_res_resL_kernel(
                 out=raw[:], in_=(ws, wt)[i][a * K_PASS : (a + 1) * K_PASS, :].rearrange("(p i) r -> p i r", i=PACK)
             )
             nc.scalar.copy(
-                rounded[u][:].rearrange("p (t m i) -> p m i t", t=PACK, i=PACK),
-                raw[:].rearrange("p i (m t) -> p m i t", t=PACK),
+                rounded[u][:].rearrange("p (t m i) -> p m t i", t=PACK, i=PACK),
+                raw[:].rearrange("p i (m t) -> p m t i", t=PACK),
             )
 
         def load_wd_scales(i, scales):

@@ -27,6 +27,7 @@ N_TILES = N // P
 HALF = J // 2
 QUARTER = J // 4
 SHIFT = 16
+SCALAR_SHARE = 64
 
 
 def tile_list_msg_gelu_res_resL_kernel(
@@ -71,16 +72,20 @@ def tile_list_msg_gelu_res_resL_kernel(
             keep.tile([P, R * PACK], BF16, name="rounded", tag="rounded%d" % u, align_bytes=64) for u in range(2 * PASSES)
         ]
 
+        late_round = []
+
         def load_weight(u):
             a, i = divmod(u, 2)
             raw = keep.tile([P, PACK, R], F32, name="raw", tag="raw%d" % u, align_bytes=64)
             nc.sync.dma_start(
                 out=raw[:], in_=(ws, wt)[i][a * K_PASS : (a + 1) * K_PASS, :].rearrange("(p i) r -> p i r", i=PACK)
             )
-            nc.scalar.copy(
-                rounded[u][:].rearrange("p (t m i) -> p m t i", t=PACK, i=PACK),
-                raw[:].rearrange("p i (m t) -> p m t i", t=PACK),
-            )
+            into = rounded[u][:].rearrange("p (t m i) -> p m t i", t=PACK, i=PACK)
+            source = raw[:].rearrange("p i (m t) -> p m t i", t=PACK)
+            cut = SCALAR_SHARE if u == 2 * PASSES - 1 else P
+            nc.scalar.copy(into[:, 0:cut, :, :], source[:, 0:cut, :, :])
+            if cut < P:
+                late_round.append((into[:, cut:P, :, :], source[:, cut:P, :, :]))
 
         def load_wd_scales(i, scales):
             rows = scales[0].bitcast(I32).rearrange("(q r) n -> r q n", r=4)
@@ -157,6 +162,7 @@ def tile_list_msg_gelu_res_resL_kernel(
         picked_second = keep.tile([P, 2, HALF], U32, name="picked_second", tag="raw1", align_bytes=64)
         for i in range(2):
             pick(i, 1, picked_second[:, i, :])
+        nc.vector.tensor_copy(*late_round[0])
         quantise_weight(2)
         quantise_weight(3)
         parted_second = keep.tile([P, 2 * PASSES * 2 * HALF], U8, name="parted_second", tag="raw3", align_bytes=64)

@@ -27,7 +27,21 @@ N_TILES = N // P
 HALF = J // 2
 QUARTER = J // 4
 SHIFT = 16
-SCALAR_SHARE = 64
+KIB = 1024
+LAP = 64
+TAB_S = 0
+RAW0 = TAB_S + 4 * KIB
+RES2 = RAW0 + 8 * KIB
+RAW1 = RES2 + 8 * KIB - LAP
+RES1 = RAW1 + 8 * KIB - LAP
+WINDOW1 = RES1 + 8 * KIB
+RAW2 = WINDOW1 + 6 * KIB
+RES3 = RAW2 + 8 * KIB - LAP
+WINDOW2 = RES3 + LAP + KIB
+RAW3 = WINDOW2 + 8 * KIB
+PICKED_SRC = RAW3 + 8 * KIB
+PICKED_DST = PICKED_SRC + 3 * KIB
+RES0 = PICKED_DST + 2 * KIB - LAP
 
 
 def tile_list_msg_gelu_res_resL_kernel(
@@ -38,7 +52,14 @@ def tile_list_msg_gelu_res_resL_kernel(
         lists = ctx.enter_context(tc.tile_pool(name="lists", bufs=1))
         keep = ctx.enter_context(tc.tile_pool(name="keep", bufs=1))
         shared = ctx.enter_context(tc.tile_pool(name="shared", bufs=1))
+        laid = ctx.enter_context(tc.tile_pool(name="laid", bufs=1))
         psum = ctx.enter_context(tc.psum_pool(name="psum", bufs=1))
+
+        def lay(name, shape, dtype, offset):
+            return laid.tile(shape, dtype, name=name, offset=offset, align_bytes=64)
+
+        def bank(k, shape):
+            return psum.tile(shape, F32, name="bank", tag="bank%d" % k)
 
         src_list = lists.tile([P, J // 16], U16, name="src_list")
         dst_list = lists.tile([P, J // 16], U16, name="dst_list")
@@ -48,44 +69,41 @@ def tile_list_msg_gelu_res_resL_kernel(
             return one_list[:, half * HALF // 16 : (half + 1) * HALF // 16]
 
         tab_w = keep.tile([P, T], I32, name="tab_w", align_bytes=64)
-        tab_s = keep.tile([P, T], U8, name="tab_s", tag="tab_s", align_bytes=64)
+        tab_s = lay("tab_s", [P, T], U8, TAB_S)
         wd_s = keep.tile([P, 2, N], U8, name="wd_s", align_bytes=64)
-        plane0 = keep.tile([P, 2 * J], U8, name="plane0", align_bytes=64)
-        plane1 = keep.tile([P, 2 * J], U8, name="plane1", align_bytes=64)
-        planes = (plane0, plane1)
-        windows = {nt: keep.tile([P, T], F32, name="window%d" % nt) for nt in range(2)}
-        for plane in (tab_s[:], plane1[:], wd_s[:].rearrange("p i n -> p (i n)")):
-            nc.vector.memset(plane.bitcast(I32), 0)
-        for nt in range(2):
-            nc.vector.memset(windows[nt][:], 0.0)
-
-        def late_window(nt, tag):
-            windows[nt] = keep.tile([P, T], F32, name="late_window", tag=tag, align_bytes=64)
-            nc.gpsimd.memset(windows[nt][:], 0.0)
-
+        shifted = keep.tile([P, 2, J], U8, name="shifted", align_bytes=64)
+        planes = {(1, half): shifted[:, half, :] for half in range(2)}
+        edge_rows = keep.tile([P, P], F32, name="edge_rows")
+        nc.gpsimd.memset(edge_rows[:], 0.0)
         identity = keep.tile([P, P], F32, name="identity")
         make_identity(nc, identity[:])
-        warm_out = keep.tile([P, 1], F32, name="warm_out")
-        nc.scalar.activation(warm_out[:], windows[0][:, 0:1], GELU)
+        windows = {nt: keep.tile([P, T], F32, name="window%d" % nt) for nt in (3, 0)}
+        for plane in (tab_s[:], wd_s[:].rearrange("p i n -> p (i n)"), shifted[:].rearrange("p h j -> p (h j)")):
+            nc.vector.memset(plane.bitcast(I32), 0)
+        for nt in (3, 0):
+            nc.vector.memset(windows[nt][:], 0.0)
+
+        def late_window(nt, offset):
+            windows[nt] = lay("window%d" % nt, [P, T], F32, offset)
+            nc.gpsimd.memset(windows[nt][:], 0.0)
 
         rounded = [
             keep.tile([P, R * PACK], BF16, name="rounded", tag="rounded%d" % u, align_bytes=64) for u in range(2 * PASSES)
         ]
 
-        late_round = []
-
         def load_weight(u):
             a, i = divmod(u, 2)
-            raw = keep.tile([P, PACK, R], F32, name="raw", tag="raw%d" % u, align_bytes=64)
+            raw = lay("raw%d" % u, [P, PACK, R], F32, (RAW0, RAW1, RAW2, RAW3)[u])
             nc.sync.dma_start(
                 out=raw[:], in_=(ws, wt)[i][a * K_PASS : (a + 1) * K_PASS, :].rearrange("(p i) r -> p i r", i=PACK)
             )
-            into = rounded[u][:].rearrange("p (t m i) -> p m t i", t=PACK, i=PACK)
-            source = raw[:].rearrange("p i (m t) -> p m t i", t=PACK)
-            cut = SCALAR_SHARE if u == 2 * PASSES - 1 else P
-            nc.scalar.copy(into[:, 0:cut, :, :], source[:, 0:cut, :, :])
-            if cut < P:
-                late_round.append((into[:, cut:P, :, :], source[:, cut:P, :, :]))
+            return raw
+
+        def round_weight(u, raw):
+            nc.scalar.copy(
+                rounded[u][:].rearrange("p (t m i) -> p m t i", t=PACK, i=PACK),
+                raw[:].rearrange("p i (m t) -> p m t i", t=PACK),
+            )
 
         def load_wd_scales(i, scales):
             rows = scales[0].bitcast(I32).rearrange("(q r) n -> r q n", r=4)
@@ -93,19 +111,35 @@ def tile_list_msg_gelu_res_resL_kernel(
                 nc.sync.dma_start(out=wd_s[r:P:32, i, :].bitcast(I32), in_=rows[r])
 
         nc.sync.dma_start(src_list[:], offs)
-        nc.sync.dma_start(out=tab_w[:], in_=tab_words[0].rearrange("p t b -> p (t b)").bitcast(I32))
+        round_weight(0, load_weight(0))
         nc.sync.dma_start(dst_list[:], offs2)
-        sm_t = keep.tile([P, PACK], F32, name="sm_t")
-        nc.sync.dma_start(out=sm_t[:], in_=sm.rearrange("(p t) -> p t", t=PACK))
+        nc.sync.dma_start(out=edge_rows[0 : J // P, :], in_=wgo[0].rearrange("(c p) -> c p", p=P))
         scale_rows = tab_scales.bitcast(I32).rearrange("a (q r) t -> r q a t", r=4)
         for r in range(4):
             nc.sync.dma_start(out=tab_s[r:P:SHIFT, :].bitcast(I32), in_=scale_rows[r])
-        load_weight(0)
-        load_weight(1)
+        nc.sync.dma_start(out=tab_w[:], in_=tab_words[0].rearrange("p t b -> p (t b)").bitcast(I32))
+
+        edge_col = keep.tile([P, J // P], F32, name="edge_col")
+        col_ps = bank(4, [P, P])
+        nc.tensor.transpose(col_ps[:], edge_rows[:], identity[:])
+        nc.scalar.copy(edge_col[:], col_ps[:, 0 : J // P])
+        spread_ps = [bank(5 + half, [P, HALF]) for half in range(2)]
+        for c in range(J // P):
+            half, slot = divmod(c, PACK)
+            nc.tensor.transpose(
+                spread_ps[half][:, slot * P : (slot + 1) * P], edge_col[:, c : c + 1].to_broadcast([P, P]), identity[:]
+            )
+        edge_w = keep.tile([P, J], F32, name="edge_w")
+        for half in range(2):
+            nc.scalar.copy(edge_w[:, half * HALF : (half + 1) * HALF], spread_ps[half][:])
+
+        round_weight(1, load_weight(1))
         load_wd_scales(0, wd4_scales)
-        load_weight(2)
+        round_weight(2, load_weight(2))
+        sm_t = keep.tile([P, PACK], F32, name="sm_t")
+        nc.sync.dma_start(out=sm_t[:], in_=sm.rearrange("(p t) -> p t", t=PACK))
+        round_weight(3, load_weight(3))
         load_wd_scales(1, wd8_scales)
-        load_weight(3)
 
         picked = {}
         parted = {}
@@ -114,38 +148,30 @@ def tile_list_msg_gelu_res_resL_kernel(
             picked[i, half] = into
             nc.vector.tensor_copy(into, tab_w[:].bitcast(U32).indirect(part_of(both[i], half)))
 
-        picked_first = keep.tile([P, 2, HALF], U32, name="picked_first", align_bytes=64)
-        for i in range(2):
-            pick(i, 0, picked_first[:, i, :])
-        for i in range(2):
-            nc.vector.tensor_copy(plane0[:, i * J : (i + 1) * J], tab_s[:].indirect(both[i][:]))
-        nc.sync.dma_start(out=plane1[0 : P - SHIFT, :].bitcast(I32), in_=plane0[SHIFT:P, :].bitcast(I32))
+        def pick_scales(half, into):
+            planes[0, half] = into
+            for i in range(2):
+                nc.vector.tensor_copy(into[:, i * HALF : (i + 1) * HALF], tab_s[:].indirect(part_of(both[i], half)))
+            nc.sync.dma_start(out=shifted[0 : P - SHIFT, half, :].bitcast(I32), in_=into[SHIFT:P, :].bitcast(I32))
 
-        res = [keep.tile([P, T], F32, name="res", tag="res%d" % nt, align_bytes=64) for nt in range(N_TILES)]
-        wd4 = keep.tile([P, 2 * N], U8, name="wd4", align_bytes=64)
-        wd8 = keep.tile([P, N], I32, name="wd8", align_bytes=64)
-        edge_w = keep.tile([P, J], F32, name="edge_w")
+        wd4 = lay("wd4", [P, 2 * N], U8, TAB_S)
+        wd8 = lay("wd8", [P, N], I32, TAB_S + KIB)
+        res = {}
 
         def load_state(nt):
+            res[nt] = lay("res%d" % nt, [P, T], F32, (RES0, RES1, RES2, RES3)[nt])
             nc.sync.dma_start(out=res[nt][:], in_=rT[nt * P : (nt + 1) * P, :])
 
-        edge_col = keep.tile([P, J // P], F32, name="edge_col")
-        nc.sync.dma_start(out=edge_w[:], in_=wgo)
-        load_state(0)
-        with nc.allow_non_contiguous_dma(reason="one edge weight a partition"):
-            nc.sync.dma_start(out=edge_col[:], in_=wgo[0].rearrange("(c p) -> p c", p=P))
-        nc.sync.dma_start(out=wd4[:].bitcast(I32), in_=wd4_words[0].bitcast(I32))
-        nc.sync.dma_start(out=wd8[:], in_=wd8_words[0].rearrange("p n b -> p (n b)").bitcast(I32))
-        load_state(1)
-        load_state(2)
-        load_state(3)
-
         w_codes = {}
-        w_scales = keep.tile([P, 2 * PASSES, R], U8, name="w_scales", align_bytes=64)
+        w_scales = {}
 
         def quantise_weight(u):
             w_codes[u] = keep.tile([P, R], U32, name="w_codes", tag="w_codes%d" % u, align_bytes=64)
-            nc.vector.quantize_mx(out=w_codes[u][:].bitcast(FP8X4), scales=w_scales[:, u, :], in_=rounded[u][:])
+            if u == 0:
+                w_scales[u] = lay("w_scales0", [P, R], U8, PICKED_SRC)
+            else:
+                w_scales[u] = keep.tile([P, R], U8, name="w_scales", tag="w_scales%d" % u, align_bytes=64)
+            nc.vector.quantize_mx(out=w_codes[u][:].bitcast(FP8X4), scales=w_scales[u][:], in_=rounded[u][:])
 
         def part(i, half, into):
             parted[i, half] = into[:, i * PASSES * 2 * HALF : (i + 1) * PASSES * 2 * HALF]
@@ -154,30 +180,34 @@ def tile_list_msg_gelu_res_resL_kernel(
                 picked[i, half].bitcast(U16).rearrange("p (j d) -> p d j", d=PASSES),
             )
 
-        quantise_weight(0)
-        parted_first = keep.tile([P, 2 * PASSES * 2 * HALF], U8, name="parted_first", tag="raw0", align_bytes=64)
+        pick_scales(0, keep.tile([P, J], U8, name="first_plane", align_bytes=64)[:])
+        pick(0, 0, lay("picked_src0", [P, HALF], U32, PICKED_SRC)[:])
+        pick(1, 0, lay("picked_dst0", [P, HALF], U32, PICKED_DST)[:])
+        parted_first = keep.tile([P, 2 * PASSES * 2 * HALF], U8, name="parted_first", align_bytes=64)
         for i in range(2):
             part(i, 0, parted_first)
+        load_state(0)
+        quantise_weight(0)
+        pick(0, 1, lay("picked_src1", [P, HALF], U32, PICKED_SRC + KIB)[:])
         quantise_weight(1)
-        picked_second = keep.tile([P, 2, HALF], U32, name="picked_second", tag="raw1", align_bytes=64)
-        for i in range(2):
-            pick(i, 1, picked_second[:, i, :])
-        nc.vector.tensor_copy(*late_round[0])
+        load_state(1)
+        pick_scales(1, lay("second_plane", [P, J], U8, RAW1 + LAP)[:])
+        nc.sync.dma_start(out=wd4[:].bitcast(I32), in_=wd4_words[0].bitcast(I32))
+        nc.sync.dma_start(out=wd8[:], in_=wd8_words[0].rearrange("p n b -> p (n b)").bitcast(I32))
+        load_state(2)
+        load_state(3)
         quantise_weight(2)
+        pick(1, 1, lay("picked_dst1", [P, HALF], U32, RAW2)[:])
         quantise_weight(3)
-        parted_second = keep.tile([P, 2 * PASSES * 2 * HALF], U8, name="parted_second", tag="raw3", align_bytes=64)
+        parted_second = lay("parted_second", [P, 2 * PASSES * 2 * HALF], U8, RAW3)
         for i in range(2):
             part(i, 1, parted_second)
-        late_window(2, "raw1")
+        late_window(1, WINDOW1)
 
         h_scales = keep.tile([P, J], U8, name="h_scales", align_bytes=64)
 
-        def bank(k, shape):
-            return psum.tile(shape, F32, name="bank", tag="bank%d" % k)
-
         def project(half):
             banks = [bank(half * PACK + t, [P, HALF]) for t in range(PACK)]
-            first = half * HALF
             steps = [(u, t) for u in range(2 * PASSES) for t in range(PACK)]
             if half == 1:
                 steps = [(u, t) for t in range(PACK) for u in range(2 * PASSES)]
@@ -187,9 +217,9 @@ def tile_list_msg_gelu_res_resL_kernel(
                 nc.tensor.matmul_mx(
                     out=banks[t][:],
                     lhsT=w_codes[u][:, t * P : (t + 1) * P].bitcast(FP8X4),
-                    lhsT_scale=w_scales[:, u, t * P : (t + 1) * P],
+                    lhsT_scale=w_scales[u][:, t * P : (t + 1) * P],
                     rhs=parted[i, half][:, start : start + 2 * HALF].bitcast(FP4X4),
-                    rhs_scale=planes[a][:, i * J + first : i * J + first + HALF],
+                    rhs_scale=planes[a, half][:, i * HALF : (i + 1) * HALF],
                     start=(u == 0),
                     stop=(u == 2 * PASSES - 1),
                 )
@@ -206,17 +236,19 @@ def tile_list_msg_gelu_res_resL_kernel(
             )
             return h
 
-        def hidden(banks, planar, width, name, tag):
+        def gelu(acts, banks, t, first, last):
+            nc.scalar.activation(acts[:, t, first:last], banks[t][:, first:last], GELU)
+
+        def hidden(banks, planar, width, name, tag, last):
             acts = keep.tile([P, PACK, HALF], F32, name="acts", tag=tag, align_bytes=64)
             for t in range(PACK + 1):
                 if t < PACK:
-                    nc.scalar.activation(acts[:, t, :], banks[t][:], GELU)
+                    gelu(acts, banks, t, 0, last)
                 if t > 0:
                     smooth(planar, acts, t - 1, 0, width)
             return acts, interleave(planar, width, name)
 
-        def quantise_hidden(first, width, h, tag):
-            codes = keep.tile([P, width], U32, name="codes", tag=tag, align_bytes=64)
+        def quantise_hidden(first, width, h, codes):
             nc.vector.quantize_mx(out=codes[:].bitcast(FP8X4), scales=h_scales[:, first : first + width], in_=h[:])
             return codes
 
@@ -275,12 +307,14 @@ def tile_list_msg_gelu_res_resL_kernel(
 
         planar_shape = [P, PACK, QUARTER]
         first_banks = project(0)
-        acts, h0 = hidden(first_banks, gated("planar0", planar_shape, BF16, 3072), QUARTER, "h0", "acts0")
+        acts, h0 = hidden(first_banks, gated("planar0", planar_shape, BF16, 3072), QUARTER, "h0", "acts0", QUARTER)
+        for t in range(PACK):
+            gelu(acts, first_banks, t, QUARTER, HALF)
         second_banks = project(1)
         own_first = keep.tile([P, 4, HALF], F32, name="own_first")
         for slot in range(4):
             residual(slot // 2, slot % 2, own_first[:, slot, :])
-        codes = quantise_hidden(0, QUARTER, h0, "res1")
+        codes = quantise_hidden(0, QUARTER, h0, lay("codes0", [P, QUARTER], U32, RES1 + LAP))
         own_third = gated("own_third", [P, 2, HALF], F32, 0)
         for half in range(2):
             residual(2, half, own_third[:, half, :])
@@ -289,24 +323,25 @@ def tile_list_msg_gelu_res_resL_kernel(
         planar1 = gated("planar1", planar_shape, BF16, 4096)
         for t in range(PACK):
             smooth(planar1, acts, t, QUARTER, QUARTER)
-        codes = quantise_hidden(QUARTER, QUARTER, interleave(planar1, QUARTER, "h1"), "res2")
+        codes = quantise_hidden(QUARTER, QUARTER, interleave(planar1, QUARTER, "h1"), lay("codes1", [P, QUARTER], U32, RES2))
         own_fourth = gated("own_fourth", [P, 2, HALF], F32, 5120)
         for half in range(2):
             residual(3, half, own_fourth[:, half, :])
-        late_window(3, "res3")
-        quarter_pieces(0, (0, 1), 2, piece("y_00"))
-        quarter_pieces(0, (2, 3), 3, piece("y_02"))
+        late_window(2, WINDOW2)
+        quarter_pieces(0, (3,), 2, piece("y_03", QUARTER))
+        quarter_pieces(0, (0, 1), 3, lay("y_00", [P, HALF], F32, RES3 + LAP - 2 * KIB))
+        quarter_pieces(0, (2,), 2, lay("y_02", [P, QUARTER], F32, RES3 + LAP))
         message(codes, QUARTER, 2, 0)
         message(codes, QUARTER, 3, 1)
         quarter_pieces(1, (0,), 2, piece("y_10", QUARTER))
         planar2 = keep.tile(planar_shape, BF16, name="planar2", tag="planar2", align_bytes=64)
-        acts, h2 = hidden(second_banks, planar2, QUARTER, "h2", "h1")
-        codes = quantise_hidden(HALF, QUARTER, h2, "codes2")
+        acts, h2 = hidden(second_banks, planar2, QUARTER, "h2", "h1", HALF)
+        codes = quantise_hidden(HALF, QUARTER, h2, keep.tile([P, QUARTER], U32, name="codes2", align_bytes=64))
         quarter_pieces(1, (1, 2), 3, keep.tile([P, HALF], F32, name="y_11", tag="planar2", align_bytes=64))
         planar3 = keep.tile(planar_shape, BF16, name="planar3", tag="planar3", align_bytes=64)
         for t in range(PACK):
             smooth(planar3, acts, t, QUARTER, QUARTER)
-        last_codes = quantise_hidden(HALF + QUARTER, QUARTER, interleave(planar3, QUARTER, "h3"), "codes3")
+        last_codes = quantise_hidden(HALF + QUARTER, QUARTER, interleave(planar3, QUARTER, "h3"), keep.tile([P, QUARTER], U32, name="codes3", align_bytes=64))
         quarter_pieces(1, (3,), 0, keep.tile([P, QUARTER], F32, name="y_13", tag="planar3", align_bytes=64))
         for q, made in ((2, codes), (3, last_codes)):
             for e in (2 * q, 2 * q + 1):

@@ -34,11 +34,9 @@ RAW0 = TAB_S + 4 * KIB
 RES2 = RAW0 + 8 * KIB
 RAW1 = RES2 + 8 * KIB - LAP
 RES1 = RAW1 + 8 * KIB - LAP
-WINDOW1 = RES1 + 8 * KIB
-RAW2 = WINDOW1 + 6 * KIB
+RAW2 = RES1 + 8 * KIB
 RES3 = RAW2 + 8 * KIB - LAP
-WINDOW2 = RES3 + LAP + KIB
-RAW3 = WINDOW2 + 8 * KIB
+RAW3 = RES3 + 8 * KIB
 PICKED_SRC = RAW3 + 8 * KIB
 PICKED_DST = PICKED_SRC + 3 * KIB
 RES0 = PICKED_DST + 2 * KIB - LAP
@@ -77,15 +75,11 @@ def tile_list_msg_gelu_res_resL_kernel(
         nc.gpsimd.memset(edge_rows[:], 0.0)
         identity = keep.tile([P, P], F32, name="identity")
         make_identity(nc, identity[:])
-        windows = {nt: keep.tile([P, T], F32, name="window%d" % nt) for nt in (3, 0)}
+        windows = {nt: keep.tile([P, T], F32, name="window%d" % nt) for nt in range(N_TILES)}
         for plane in (tab_s[:], wd_s[:].rearrange("p i n -> p (i n)"), shifted[:].rearrange("p h j -> p (h j)")):
             nc.vector.memset(plane.bitcast(I32), 0)
-        for nt in (3, 0):
+        for nt in range(N_TILES):
             nc.vector.memset(windows[nt][:], 0.0)
-
-        def late_window(nt, offset):
-            windows[nt] = lay("window%d" % nt, [P, T], F32, offset)
-            nc.gpsimd.memset(windows[nt][:], 0.0)
 
         rounded = [
             keep.tile([P, R * PACK], BF16, name="rounded", tag="rounded%d" % u, align_bytes=64) for u in range(2 * PASSES)
@@ -202,7 +196,6 @@ def tile_list_msg_gelu_res_resL_kernel(
         parted_second = lay("parted_second", [P, 2 * PASSES * 2 * HALF], U8, RAW3)
         for i in range(2):
             part(i, 1, parted_second)
-        late_window(1, WINDOW1)
 
         h_scales = keep.tile([P, J], U8, name="h_scales", align_bytes=64)
 
@@ -327,7 +320,6 @@ def tile_list_msg_gelu_res_resL_kernel(
         own_fourth = gated("own_fourth", [P, 2, HALF], F32, 5120)
         for half in range(2):
             residual(3, half, own_fourth[:, half, :])
-        late_window(2, WINDOW2)
         quarter_pieces(0, (3,), 2, piece("y_03", QUARTER))
         quarter_pieces(0, (0, 1), 3, lay("y_00", [P, HALF], F32, RES3 + LAP - 2 * KIB))
         quarter_pieces(0, (2,), 2, lay("y_02", [P, QUARTER], F32, RES3 + LAP))

@@ -76,10 +76,19 @@ def tile_list_msg_gelu_res_resL_kernel(
         identity = keep.tile([P, P], F32, name="identity")
         make_identity(nc, identity[:])
         windows = {nt: keep.tile([P, T], F32, name="window%d" % nt) for nt in range(N_TILES)}
-        for plane in (tab_s[:], wd_s[:].rearrange("p i n -> p (i n)"), shifted[:].rearrange("p h j -> p (h j)")):
-            nc.vector.memset(plane.bitcast(I32), 0)
-        for nt in range(N_TILES):
-            nc.vector.memset(windows[nt][:], 0.0)
+
+        def zero_in_odd_pieces(words):
+            cut = words.shape[1] // 2 - 1
+            nc.vector.memset(words[:, 0:cut], 0)
+            nc.vector.memset(words[:, cut : words.shape[1]], 0)
+
+        zero_in_odd_pieces(tab_s[:].bitcast(I32))
+        zero_in_odd_pieces(shifted[:].rearrange("p h j -> p (h j)").bitcast(I32))
+        for nt in (3, 0):
+            zero_in_odd_pieces(windows[nt][:])
+        nc.gpsimd.memset(wd_s[:].rearrange("p i n -> p (i n)").bitcast(I32), 0)
+        for nt in (1, 2):
+            nc.gpsimd.memset(windows[nt][:], 0.0)
 
         rounded = [
             keep.tile([P, R * PACK], BF16, name="rounded", tag="rounded%d" % u, align_bytes=64) for u in range(2 * PASSES)

@@ -23,6 +23,7 @@ P = 128
 PACK = 4
 K_PASS = P * PACK
 PASSES = K // K_PASS
+WEIGHTS = 2 * PASSES
 N_TILES = N // P
 HALF = J // 2
 QUARTER = J // 4
@@ -30,16 +31,19 @@ SHIFT = 16
 KIB = 1024
 LAP = 64
 TAB_S = 0
-RAW0 = TAB_S + 4 * KIB
-RES2 = RAW0 + 8 * KIB
-RAW1 = RES2 + 8 * KIB - LAP
-RES1 = RAW1 + 8 * KIB - LAP
-RAW2 = RES1 + 8 * KIB
-RES3 = RAW2 + 8 * KIB - LAP
-RAW3 = RES3 + 8 * KIB
-PICKED_SRC = RAW3 + 8 * KIB
-PICKED_DST = PICKED_SRC + 3 * KIB
-RES0 = PICKED_DST + 2 * KIB - LAP
+RAW0 = TAB_S + 3 * KIB
+PICKED_LAST = RAW0 + 8 * KIB
+RAW1 = PICKED_LAST + 2 * KIB - LAP
+PARTED_SECOND = RAW1 + 8 * KIB + LAP
+RAW2 = PARTED_SECOND + 4 * KIB - LAP
+RAW3 = RAW2 + 8 * KIB + LAP
+WINDOW1 = RAW3 + 8 * KIB
+ROUNDED3 = WINDOW1 + 8 * KIB - LAP
+WINDOW2 = ROUNDED3 + 4 * KIB - LAP
+H0 = WINDOW2 + 8 * KIB
+WINDOW3 = H0 + 2 * KIB - LAP
+PLANAR0 = WINDOW3 + 8 * KIB
+OWN2 = PLANAR0 + 2 * KIB - LAP
 
 
 def tile_list_msg_gelu_res_resL_kernel(
@@ -49,12 +53,14 @@ def tile_list_msg_gelu_res_resL_kernel(
     with ExitStack() as ctx:
         lists = ctx.enter_context(tc.tile_pool(name="lists", bufs=1))
         keep = ctx.enter_context(tc.tile_pool(name="keep", bufs=1))
-        shared = ctx.enter_context(tc.tile_pool(name="shared", bufs=1))
         laid = ctx.enter_context(tc.tile_pool(name="laid", bufs=1))
         psum = ctx.enter_context(tc.psum_pool(name="psum", bufs=1))
 
         def lay(name, shape, dtype, offset):
             return laid.tile(shape, dtype, name=name, offset=offset, align_bytes=64)
+
+        def fresh(name, shape, dtype):
+            return keep.tile(shape, dtype, name=name, align_bytes=64)
 
         def bank(k, shape):
             return psum.tile(shape, F32, name="bank", tag="bank%d" % k)
@@ -63,36 +69,31 @@ def tile_list_msg_gelu_res_resL_kernel(
         dst_list = lists.tile([P, J // 16], U16, name="dst_list")
         both = (src_list, dst_list)
 
-        def part_of(one_list, half):
-            return one_list[:, half * HALF // 16 : (half + 1) * HALF // 16]
+        def entries(one_list, first, count):
+            return one_list[:, first // 16 : (first + count) // 16]
 
-        tab_w = keep.tile([P, T], I32, name="tab_w", align_bytes=64)
         tab_s = lay("tab_s", [P, T], U8, TAB_S)
-        wd_s = keep.tile([P, 2, N], U8, name="wd_s", align_bytes=64)
-        shifted = keep.tile([P, 2, J], U8, name="shifted", align_bytes=64)
-        planes = {(1, half): shifted[:, half, :] for half in range(2)}
-        edge_rows = keep.tile([P, P], F32, name="edge_rows")
+        nc.gpsimd.memset(tab_s[:].bitcast(I32), 0)
+        edge_rows = fresh("edge_rows", [P, P], F32)
         nc.gpsimd.memset(edge_rows[:], 0.0)
-        identity = keep.tile([P, P], F32, name="identity")
+        identity = fresh("identity", [P, P], F32)
         make_identity(nc, identity[:])
-        windows = {nt: keep.tile([P, T], F32, name="window%d" % nt) for nt in range(N_TILES)}
-
-        def zero_in_odd_pieces(words):
-            cut = words.shape[1] // 2 - 1
-            nc.vector.memset(words[:, 0:cut], 0)
-            nc.vector.memset(words[:, cut : words.shape[1]], 0)
-
-        zero_in_odd_pieces(tab_s[:].bitcast(I32))
-        zero_in_odd_pieces(shifted[:].rearrange("p h j -> p (h j)").bitcast(I32))
-        for nt in (3, 0):
-            zero_in_odd_pieces(windows[nt][:])
+        wd_s = fresh("wd_s", [P, 2, N], U8)
         nc.gpsimd.memset(wd_s[:].rearrange("p i n -> p (i n)").bitcast(I32), 0)
-        for nt in (1, 2):
-            nc.gpsimd.memset(windows[nt][:], 0.0)
+        shifted = fresh("shifted", [P, 2 * J], U8)
+        nc.gpsimd.memset(shifted[:].bitcast(I32), 0)
+        windows = {0: fresh("window0", [P, T], F32)}
+        nc.vector.memset(windows[0][:, 0 : T // 2 - 1], 0.0)
+        nc.vector.memset(windows[0][:, T // 2 - 1 : T], 0.0)
 
-        rounded = [
-            keep.tile([P, R * PACK], BF16, name="rounded", tag="rounded%d" % u, align_bytes=64) for u in range(2 * PASSES)
-        ]
+        nc.sync.dma_start(src_list[:], offs)
+        nc.sync.dma_start(dst_list[:], offs2)
+        scale_rows = tab_scales.bitcast(I32).rearrange("a (q r) t -> r q a t", r=4)
+        for r in range(4):
+            nc.sync.dma_start(out=tab_s[r:P:SHIFT, :].bitcast(I32), in_=scale_rows[r])
+        nc.sync.dma_start(out=edge_rows[0 : J // P, :], in_=wgo[0].rearrange("(c p) -> c p", p=P))
+
+        rounded = {}
 
         def load_weight(u):
             a, i = divmod(u, 2)
@@ -100,9 +101,10 @@ def tile_list_msg_gelu_res_resL_kernel(
             nc.sync.dma_start(
                 out=raw[:], in_=(ws, wt)[i][a * K_PASS : (a + 1) * K_PASS, :].rearrange("(p i) r -> p i r", i=PACK)
             )
-            return raw
-
-        def round_weight(u, raw):
+            if u == WEIGHTS - 1:
+                rounded[u] = lay("rounded%d" % u, [P, R * PACK], BF16, ROUNDED3)
+            else:
+                rounded[u] = fresh("rounded%d" % u, [P, R * PACK], BF16)
             nc.scalar.copy(
                 rounded[u][:].rearrange("p (t m i) -> p m t i", t=PACK, i=PACK),
                 raw[:].rearrange("p i (m t) -> p m t i", t=PACK),
@@ -113,154 +115,159 @@ def tile_list_msg_gelu_res_resL_kernel(
             for r in range(4):
                 nc.sync.dma_start(out=wd_s[r:P:32, i, :].bitcast(I32), in_=rows[r])
 
-        nc.sync.dma_start(src_list[:], offs)
-        round_weight(0, load_weight(0))
-        nc.sync.dma_start(dst_list[:], offs2)
-        nc.sync.dma_start(out=edge_rows[0 : J // P, :], in_=wgo[0].rearrange("(c p) -> c p", p=P))
-        scale_rows = tab_scales.bitcast(I32).rearrange("a (q r) t -> r q a t", r=4)
-        for r in range(4):
-            nc.sync.dma_start(out=tab_s[r:P:SHIFT, :].bitcast(I32), in_=scale_rows[r])
-        nc.sync.dma_start(out=tab_w[:], in_=tab_words[0].rearrange("p t b -> p (t b)").bitcast(I32))
-
-        edge_col = keep.tile([P, J // P], F32, name="edge_col")
+        edge_col = fresh("edge_col", [P, J // P], F32)
         col_ps = bank(4, [P, P])
         nc.tensor.transpose(col_ps[:], edge_rows[:], identity[:])
         nc.scalar.copy(edge_col[:], col_ps[:, 0 : J // P])
+
+        load_weight(0)
+        tab_w = fresh("tab_w", [P, T], I32)
+        nc.sync.dma_start(out=tab_w[:], in_=tab_words[0].rearrange("p t b -> p (t b)").bitcast(I32))
+
         spread_ps = [bank(5 + half, [P, HALF]) for half in range(2)]
         for c in range(J // P):
             half, slot = divmod(c, PACK)
             nc.tensor.transpose(
                 spread_ps[half][:, slot * P : (slot + 1) * P], edge_col[:, c : c + 1].to_broadcast([P, P]), identity[:]
             )
-        edge_w = keep.tile([P, J], F32, name="edge_w")
+        edge_w = fresh("edge_w", [P, J], F32)
         for half in range(2):
             nc.scalar.copy(edge_w[:, half * HALF : (half + 1) * HALF], spread_ps[half][:])
 
-        round_weight(1, load_weight(1))
+        load_weight(1)
         load_wd_scales(0, wd4_scales)
-        round_weight(2, load_weight(2))
-        sm_t = keep.tile([P, PACK], F32, name="sm_t")
-        nc.sync.dma_start(out=sm_t[:], in_=sm.rearrange("(p t) -> p t", t=PACK))
-        round_weight(3, load_weight(3))
+        load_weight(2)
         load_wd_scales(1, wd8_scales)
+        load_weight(3)
+        sm_t = fresh("sm_t", [P, PACK], F32)
+        nc.sync.dma_start(out=sm_t[:], in_=sm.rearrange("(p t) -> p t", t=PACK))
+
+        first_plane = fresh("first_plane", [P, 2 * J], U8)
+        for i in range(2):
+            nc.vector.tensor_copy(first_plane[:, i * J : (i + 1) * J], tab_s[:].indirect(both[i][:]))
+        nc.sync.dma_start(out=shifted[0 : P - SHIFT, :].bitcast(I32), in_=first_plane[SHIFT:P, :].bitcast(I32))
+        planes = (first_plane, shifted)
+
+        res = {}
+
+        def load_state(nt):
+            res[nt] = lay("res%d" % nt, [P, T], F32, (RAW0, RAW1 + LAP, RAW2 + LAP, RAW3)[nt])
+            nc.sync.dma_start(out=res[nt][:], in_=rT[nt * P : (nt + 1) * P, :])
+
+        load_state(0)
+        wd4 = lay("wd4", [P, 2 * N], U8, TAB_S)
+        wd8 = lay("wd8", [P, N], I32, TAB_S + KIB)
+        nc.sync.dma_start(out=wd4[:].bitcast(I32), in_=wd4_words[0].bitcast(I32))
+        nc.sync.dma_start(out=wd8[:], in_=wd8_words[0].rearrange("p n b -> p (n b)").bitcast(I32))
+        for nt in range(1, N_TILES):
+            load_state(nt)
+
+        w_codes = {}
+        w_scales = {}
+
+        def quantise_weight(u):
+            w_codes[u] = fresh("w_codes%d" % u, [P, R], U32)
+            w_scales[u] = fresh("w_scales%d" % u, [P, R], U8)
+            nc.vector.quantize_mx(out=w_codes[u][:].bitcast(FP8X4), scales=w_scales[u][:], in_=rounded[u][:])
 
         picked = {}
         parted = {}
 
         def pick(i, half, into):
             picked[i, half] = into
-            nc.vector.tensor_copy(into, tab_w[:].bitcast(U32).indirect(part_of(both[i], half)))
+            nc.vector.tensor_copy(into[:], tab_w[:].bitcast(U32).indirect(entries(both[i], half * HALF, HALF)))
 
-        def pick_scales(half, into):
-            planes[0, half] = into
+        def part(half, into):
             for i in range(2):
-                nc.vector.tensor_copy(into[:, i * HALF : (i + 1) * HALF], tab_s[:].indirect(part_of(both[i], half)))
-            nc.sync.dma_start(out=shifted[0 : P - SHIFT, half, :].bitcast(I32), in_=into[SHIFT:P, :].bitcast(I32))
+                parted[i, half] = into[:, i * PASSES * 2 * HALF : (i + 1) * PASSES * 2 * HALF]
+                nc.vector.tensor_copy(
+                    parted[i, half].bitcast(U16).rearrange("p (d j) -> p d j", d=PASSES),
+                    picked[i, half][:].bitcast(U16).rearrange("p (j d) -> p d j", d=PASSES),
+                )
 
-        wd4 = lay("wd4", [P, 2 * N], U8, TAB_S)
-        wd8 = lay("wd8", [P, N], I32, TAB_S + KIB)
-        res = {}
-
-        def load_state(nt):
-            res[nt] = lay("res%d" % nt, [P, T], F32, (RES0, RES1, RES2, RES3)[nt])
-            nc.sync.dma_start(out=res[nt][:], in_=rT[nt * P : (nt + 1) * P, :])
-
-        w_codes = {}
-        w_scales = {}
-
-        def quantise_weight(u):
-            w_codes[u] = keep.tile([P, R], U32, name="w_codes", tag="w_codes%d" % u, align_bytes=64)
-            if u == 0:
-                w_scales[u] = lay("w_scales0", [P, R], U8, PICKED_SRC)
-            else:
-                w_scales[u] = keep.tile([P, R], U8, name="w_scales", tag="w_scales%d" % u, align_bytes=64)
-            nc.vector.quantize_mx(out=w_codes[u][:].bitcast(FP8X4), scales=w_scales[u][:], in_=rounded[u][:])
-
-        def part(i, half, into):
-            parted[i, half] = into[:, i * PASSES * 2 * HALF : (i + 1) * PASSES * 2 * HALF]
-            nc.vector.tensor_copy(
-                parted[i, half].bitcast(U16).rearrange("p (d j) -> p d j", d=PASSES),
-                picked[i, half].bitcast(U16).rearrange("p (j d) -> p d j", d=PASSES),
-            )
-
-        pick_scales(0, keep.tile([P, J], U8, name="first_plane", align_bytes=64)[:])
-        pick(0, 0, lay("picked_src0", [P, HALF], U32, PICKED_SRC)[:])
-        pick(1, 0, lay("picked_dst0", [P, HALF], U32, PICKED_DST)[:])
-        parted_first = keep.tile([P, 2 * PASSES * 2 * HALF], U8, name="parted_first", align_bytes=64)
-        for i in range(2):
-            part(i, 0, parted_first)
-        load_state(0)
         quantise_weight(0)
-        pick(0, 1, lay("picked_src1", [P, HALF], U32, PICKED_SRC + KIB)[:])
-        quantise_weight(1)
-        load_state(1)
-        pick_scales(1, lay("second_plane", [P, J], U8, RAW1 + LAP)[:])
-        nc.sync.dma_start(out=wd4[:].bitcast(I32), in_=wd4_words[0].bitcast(I32))
-        nc.sync.dma_start(out=wd8[:], in_=wd8_words[0].rearrange("p n b -> p (n b)").bitcast(I32))
-        load_state(2)
-        load_state(3)
-        quantise_weight(2)
-        pick(1, 1, lay("picked_dst1", [P, HALF], U32, RAW2)[:])
-        quantise_weight(3)
-        parted_second = lay("parted_second", [P, 2 * PASSES * 2 * HALF], U8, RAW3)
         for i in range(2):
-            part(i, 1, parted_second)
+            pick(i, 0, fresh("picked%d0" % i, [P, HALF], U32))
+        part(0, fresh("parted_first", [P, 2 * PASSES * 2 * HALF], U8))
+        pick(0, 1, fresh("picked01", [P, HALF], U32))
+        quantise_weight(1)
+        pick(1, 1, lay("picked11", [P, HALF], U32, PICKED_LAST))
+        quantise_weight(2)
+        part(1, lay("parted_second", [P, 2 * PASSES * 2 * HALF], U8, PARTED_SECOND))
+        quantise_weight(3)
+        for nt, offset in ((1, WINDOW1), (2, WINDOW2)):
+            windows[nt] = lay("window%d" % nt, [P, T], F32, offset)
+            nc.gpsimd.memset(windows[nt][:], 0.0)
 
-        h_scales = keep.tile([P, J], U8, name="h_scales", align_bytes=64)
-
-        def project(half):
+        def project(half, steps):
             banks = [bank(half * PACK + t, [P, HALF]) for t in range(PACK)]
-            steps = [(u, t) for u in range(2 * PASSES) for t in range(PACK)]
-            if half == 1:
-                steps = [(u, t) for t in range(PACK) for u in range(2 * PASSES)]
-            for u, t in steps:
+            for n, (u, t) in enumerate(steps):
                 a, i = divmod(u, 2)
                 start = a * HALF * 2
+                mine = [v for v, s in steps if s == t]
                 nc.tensor.matmul_mx(
                     out=banks[t][:],
                     lhsT=w_codes[u][:, t * P : (t + 1) * P].bitcast(FP8X4),
                     lhsT_scale=w_scales[u][:, t * P : (t + 1) * P],
                     rhs=parted[i, half][:, start : start + 2 * HALF].bitcast(FP4X4),
-                    rhs_scale=planes[a, half][:, i * HALF : (i + 1) * HALF],
-                    start=(u == 0),
-                    stop=(u == 2 * PASSES - 1),
+                    rhs_scale=planes[a][:, i * J + half * HALF : i * J + (half + 1) * HALF],
+                    start=(u == mine[0]),
+                    stop=(u == mine[-1]),
                 )
             return banks
 
-        def smooth(planar, act, t, first, width):
-            nc.scalar.activation(planar[:, t, :], act[:, t, first : first + width], COPY, scale=sm_t[:, t : t + 1])
+        first_banks = project(0, [(u, t) for u in range(WEIGHTS) for t in range(PACK)])
+        second_banks = project(1, [(u, t) for t in range(PACK) for u in reversed(range(WEIGHTS))])
 
-        def interleave(planar, width, name):
-            h = keep.tile([P, width * PACK], BF16, name=name, tag=name, align_bytes=64)
+        h_scales = fresh("h_scales", [P, J], U8)
+        acts = {}
+        planar = {}
+        h = {}
+        codes = {}
+
+        def gelu(q, t):
+            if q not in acts:
+                acts[q] = fresh("acts%d" % q, [P, PACK, QUARTER], F32)
+            inside = (q % 2) * QUARTER
+            nc.scalar.activation(acts[q][:, t, :], (first_banks, second_banks)[q // 2][t][:, inside : inside + QUARTER], GELU)
+
+        def smooth(q, t):
+            if q not in planar:
+                shape = [P, PACK, QUARTER]
+                planar[q] = lay("planar0", shape, BF16, PLANAR0) if q == 0 else fresh("planar%d" % q, shape, BF16)
+            nc.scalar.activation(planar[q][:, t, :], acts[q][:, t, :], COPY, scale=sm_t[:, t : t + 1])
+
+        def interleave(q):
+            shape = [P, QUARTER * PACK]
+            h[q] = lay("h0", shape, BF16, H0) if q == 0 else fresh("h%d" % q, shape, BF16)
             nc.scalar.copy(
-                h[:].rearrange("p (c i t) -> p c t i", i=4, t=PACK),
-                planar[:].rearrange("p t (c i) -> p c t i", i=4),
+                h[q][:].rearrange("p (c i t) -> p c t i", i=4, t=PACK),
+                planar[q][:].rearrange("p t (c i) -> p c t i", i=4),
             )
-            return h
 
-        def gelu(acts, banks, t, first, last):
-            nc.scalar.activation(acts[:, t, first:last], banks[t][:, first:last], GELU)
+        def quantise_hidden(q):
+            shape = [P, QUARTER]
+            codes[q] = lay("codes0", shape, U32, RAW1 + LAP) if q == 0 else fresh("codes%d" % q, shape, U32)
+            nc.vector.quantize_mx(
+                out=codes[q][:].bitcast(FP8X4), scales=h_scales[:, q * QUARTER : (q + 1) * QUARTER], in_=h[q][:]
+            )
 
-        def hidden(banks, planar, width, name, tag, last):
-            acts = keep.tile([P, PACK, HALF], F32, name="acts", tag=tag, align_bytes=64)
+        def hidden(q):
             for t in range(PACK + 1):
                 if t < PACK:
-                    gelu(acts, banks, t, 0, last)
+                    gelu(q, t)
                 if t > 0:
-                    smooth(planar, acts, t - 1, 0, width)
-            return acts, interleave(planar, width, name)
-
-        def quantise_hidden(first, width, h, codes):
-            nc.vector.quantize_mx(out=codes[:].bitcast(FP8X4), scales=h_scales[:, first : first + width], in_=h[:])
-            return codes
+                    smooth(q, t - 1)
+            interleave(q)
+            quantise_hidden(q)
 
         scaled = {}
 
-        def message(codes, first, edge_tile, k):
-            inside = edge_tile * P - first
+        def message(e, k):
+            inside = (e % 2) * P
             y_ps = bank(k, [P, N])
-            lhsT = codes[:, inside : inside + P].bitcast(FP8X4)
-            lhsT_scale = h_scales[:, edge_tile * P : (edge_tile + 1) * P]
+            lhsT = codes[e // 2][:, inside : inside + P].bitcast(FP8X4)
+            lhsT_scale = h_scales[:, e * P : (e + 1) * P]
             nc.tensor.matmul_mx(
                 out=y_ps[:], lhsT=lhsT, lhsT_scale=lhsT_scale,
                 rhs=wd4[:].bitcast(FP4X4), rhs_scale=wd_s[:, 0, :], start=True, stop=False,
@@ -269,86 +276,68 @@ def tile_list_msg_gelu_res_resL_kernel(
                 out=y_ps[:], lhsT=lhsT, lhsT_scale=lhsT_scale,
                 rhs=wd8[:].bitcast(FP8X4), rhs_scale=wd_s[:, 1, :], start=False, stop=True,
             )
-            scaled[edge_tile] = keep.tile([P, N], F32, name="scaled", tag="scaled%d" % edge_tile)
-            nc.scalar.activation(scaled[edge_tile][:], y_ps[:], COPY, scale=edge_col[:, edge_tile : edge_tile + 1])
-
-        def turn(blocks, k, into):
-            t_ps = bank(k, [P, len(blocks) * P])
-            for slot, (nt, edge_tile) in enumerate(blocks):
-                nc.tensor.transpose(
-                    t_ps[:, slot * P : (slot + 1) * P], scaled[edge_tile][:, nt * P : (nt + 1) * P], identity[:]
-                )
-            nc.scalar.copy(into[:], t_ps[:])
-            return into
+            scaled[e] = fresh("scaled%d" % e, [P, N], F32)
+            nc.scalar.activation(scaled[e][:], y_ps[:], COPY, scale=edge_col[:, e : e + 1])
 
         own = {}
 
-        def residual(nt, half, into):
-            nc.vector.tensor_tensor(
-                into, res[nt][:].indirect(part_of(dst_list, half)), edge_w[:, half * HALF : (half + 1) * HALF], MULT
-            )
-            own[nt, half] = into
+        def residual(nt, into):
+            own[nt] = into
+            for half in range(2):
+                cols = slice(half * HALF, (half + 1) * HALF)
+                nc.vector.tensor_tensor(
+                    into[:, cols], res[nt][:].indirect(entries(dst_list, half * HALF, HALF)), edge_w[:, cols], MULT
+                )
 
-        def place(nt, first, width, y):
-            inside = first % HALF
-            nc.vector.tensor_tensor(
-                windows[nt][:].indirect(dst_list[:, first // 16 : (first + width) // 16]),
-                y, own[nt, first // HALF][:, inside : inside + width], ADD,
-            )
-
-        def piece(name, width=HALF):
-            return keep.tile([P, width], F32, name=name)
-
-        def gated(name, shape, dtype, offset):
-            return shared.tile(shape, dtype, name=name, offset=offset, align_bytes=64)
-
-        def quarter_pieces(q, tiles, k, into):
-            y = turn([(nt, e) for nt in tiles for e in (2 * q, 2 * q + 1)], k, into)
+        def pieces(tiles, edge_tiles, k, tag=""):
+            width = len(edge_tiles) * P
+            first = edge_tiles[0] * P
+            t_ps = bank(k, [P, len(tiles) * width])
+            for slot, (nt, e) in enumerate([(nt, e) for nt in tiles for e in edge_tiles]):
+                nc.tensor.transpose(
+                    t_ps[:, slot * P : (slot + 1) * P], scaled[e][:, nt * P : (nt + 1) * P], identity[:]
+                )
+            name = "y_%d_%d" % (tiles[0], edge_tiles[0])
+            y = keep.tile([P, len(tiles) * width], F32, name=name, tag=tag or name, align_bytes=64)
+            nc.scalar.copy(y[:], t_ps[:])
             for slot, nt in enumerate(tiles):
-                place(nt, q * QUARTER, QUARTER, y[:, slot * QUARTER : (slot + 1) * QUARTER])
+                nc.vector.tensor_tensor(
+                    windows[nt][:].indirect(entries(dst_list, first, width)),
+                    y[:, slot * width : (slot + 1) * width], own[nt][:, first : first + width], ADD,
+                )
 
-        planar_shape = [P, PACK, QUARTER]
-        first_banks = project(0)
-        acts, h0 = hidden(first_banks, gated("planar0", planar_shape, BF16, 3072), QUARTER, "h0", "acts0", QUARTER)
+        for nt in range(2):
+            residual(nt, fresh("own%d" % nt, [P, J], F32))
+        hidden(0)
+        windows[3] = lay("window3", [P, T], F32, WINDOW3)
+        nc.gpsimd.memset(windows[3][:], 0.0)
+        residual(2, lay("own2", [P, J], F32, OWN2))
+        residual(3, fresh("own3", [P, J], F32))
         for t in range(PACK):
-            gelu(acts, first_banks, t, QUARTER, HALF)
-        second_banks = project(1)
-        own_first = keep.tile([P, 4, HALF], F32, name="own_first")
-        for slot in range(4):
-            residual(slot // 2, slot % 2, own_first[:, slot, :])
-        codes = quantise_hidden(0, QUARTER, h0, lay("codes0", [P, QUARTER], U32, RES1 + LAP))
-        own_third = gated("own_third", [P, 2, HALF], F32, 0)
-        for half in range(2):
-            residual(2, half, own_third[:, half, :])
-        message(codes, 0, 0, 0)
-        message(codes, 0, 1, 1)
-        planar1 = gated("planar1", planar_shape, BF16, 4096)
+            gelu(1, t)
+        message(0, 0)
         for t in range(PACK):
-            smooth(planar1, acts, t, QUARTER, QUARTER)
-        codes = quantise_hidden(QUARTER, QUARTER, interleave(planar1, QUARTER, "h1"), lay("codes1", [P, QUARTER], U32, RES2))
-        own_fourth = gated("own_fourth", [P, 2, HALF], F32, 5120)
-        for half in range(2):
-            residual(3, half, own_fourth[:, half, :])
-        quarter_pieces(0, (3,), 2, piece("y_03", QUARTER))
-        quarter_pieces(0, (0, 1), 3, lay("y_00", [P, HALF], F32, RES3 + LAP - 2 * KIB))
-        quarter_pieces(0, (2,), 2, lay("y_02", [P, QUARTER], F32, RES3 + LAP))
-        message(codes, QUARTER, 2, 0)
-        message(codes, QUARTER, 3, 1)
-        quarter_pieces(1, (0,), 2, piece("y_10", QUARTER))
-        planar2 = keep.tile(planar_shape, BF16, name="planar2", tag="planar2", align_bytes=64)
-        acts, h2 = hidden(second_banks, planar2, QUARTER, "h2", "h1", HALF)
-        codes = quantise_hidden(HALF, QUARTER, h2, keep.tile([P, QUARTER], U32, name="codes2", align_bytes=64))
-        quarter_pieces(1, (1, 2), 3, keep.tile([P, HALF], F32, name="y_11", tag="planar2", align_bytes=64))
-        planar3 = keep.tile(planar_shape, BF16, name="planar3", tag="planar3", align_bytes=64)
-        for t in range(PACK):
-            smooth(planar3, acts, t, QUARTER, QUARTER)
-        last_codes = quantise_hidden(HALF + QUARTER, QUARTER, interleave(planar3, QUARTER, "h3"), keep.tile([P, QUARTER], U32, name="codes3", align_bytes=64))
-        quarter_pieces(1, (3,), 0, keep.tile([P, QUARTER], F32, name="y_13", tag="planar3", align_bytes=64))
-        for q, made in ((2, codes), (3, last_codes)):
-            for e in (2 * q, 2 * q + 1):
-                message(made, q * QUARTER, e, e)
-            quarter_pieces(q, (0, 1), q - 1, piece("y_q%d" % q))
+            smooth(1, t)
+        pieces((0, 1, 2, 3), (0,), 2)
+        interleave(1)
+        quantise_hidden(1)
+        message(1, 1)
+        pieces((0, 1, 2, 3), (1,), 3)
+        message(2, 0)
+        message(3, 1)
+        pieces((0,), (2, 3), 2)
+        hidden(2)
+        pieces((1, 2), (2, 3), 3, "planar2")
+        hidden(3)
+        pieces((3,), (2, 3), 0, "planar3")
+        message(4, 4)
+        message(5, 5)
+        for nt in range(2):
+            pieces((nt,), (4, 5), 1 + nt)
+        message(6, 1)
+        message(7, 2)
+        pieces((0, 1), (6, 7), 6)
         for nt in range(N_TILES):
             if nt >= 2:
-                place(nt, HALF, HALF, turn([(nt, e) for e in range(4, 8)], (nt + 1) % 4, piece("y_%d1" % nt))[:])
+                pieces((nt,), (4, 5, 6, 7), nt + 1)
             nc.sync.dma_start(out=out[nt * P : (nt + 1) * P, :], in_=windows[nt][:])

@@ -37,8 +37,7 @@ RAW1 = PICKED_LAST + 2 * KIB - LAP
 PARTED_SECOND = RAW1 + 8 * KIB + LAP
 RAW2 = PARTED_SECOND + 4 * KIB - LAP
 RAW3 = RAW2 + 8 * KIB + LAP
-WINDOW1 = RAW3 + 8 * KIB
-ROUNDED3 = WINDOW1 + 8 * KIB - LAP
+ROUNDED3 = RAW3 + 8 * KIB
 WINDOW2 = ROUNDED3 + 4 * KIB - LAP
 H0 = WINDOW2 + 8 * KIB
 WINDOW3 = H0 + 2 * KIB - LAP
@@ -81,10 +80,12 @@ def tile_list_msg_gelu_res_resL_kernel(
         wd_s = fresh("wd_s", [P, 2, N], U8)
         nc.gpsimd.memset(wd_s[:].rearrange("p i n -> p (i n)").bitcast(I32), 0)
         shifted = fresh("shifted", [P, 2 * J], U8)
-        nc.gpsimd.memset(shifted[:].bitcast(I32), 0)
-        windows = {0: fresh("window0", [P, T], F32)}
-        nc.vector.memset(windows[0][:, 0 : T // 2 - 1], 0.0)
-        nc.vector.memset(windows[0][:, T // 2 - 1 : T], 0.0)
+        windows = {nt: fresh("window%d" % nt, [P, T], F32) for nt in (0, 3)}
+        nc.gpsimd.memset(windows[3][:], 0.0)
+        for words in (windows[0][:], shifted[:].bitcast(I32)):
+            cut = words.shape[1] // 2 - 1
+            nc.vector.memset(words[:, 0:cut], 0)
+            nc.vector.memset(words[:, cut : words.shape[1]], 0)
 
         nc.sync.dma_start(src_list[:], offs)
         nc.sync.dma_start(dst_list[:], offs2)
@@ -195,9 +196,8 @@ def tile_list_msg_gelu_res_resL_kernel(
         quantise_weight(2)
         part(1, lay("parted_second", [P, 2 * PASSES * 2 * HALF], U8, PARTED_SECOND))
         quantise_weight(3)
-        for nt, offset in ((1, WINDOW1), (2, WINDOW2)):
-            windows[nt] = lay("window%d" % nt, [P, T], F32, offset)
-            nc.gpsimd.memset(windows[nt][:], 0.0)
+        windows[1] = lay("window1", [P, T], F32, WINDOW2)
+        nc.gpsimd.memset(windows[1][:], 0.0)
 
         def project(half, steps):
             banks = [bank(half * PACK + t, [P, HALF]) for t in range(PACK)]
@@ -227,14 +227,18 @@ def tile_list_msg_gelu_res_resL_kernel(
 
         def gelu(q, t):
             if q not in acts:
-                acts[q] = fresh("acts%d" % q, [P, PACK, QUARTER], F32)
+                shape = [P, PACK, QUARTER]
+                acts[q] = lay("acts3", shape, F32, ROUNDED3 - LAP) if q == 3 else fresh("acts%d" % q, shape, F32)
             inside = (q % 2) * QUARTER
             nc.scalar.activation(acts[q][:, t, :], (first_banks, second_banks)[q // 2][t][:, inside : inside + QUARTER], GELU)
 
         def smooth(q, t):
             if q not in planar:
                 shape = [P, PACK, QUARTER]
-                planar[q] = lay("planar0", shape, BF16, PLANAR0) if q == 0 else fresh("planar%d" % q, shape, BF16)
+                if q % 2 == 0:
+                    planar[q] = lay("planar%d" % q, shape, BF16, (PLANAR0, RAW3 + 4 * KIB)[q // 2])
+                else:
+                    planar[q] = fresh("planar%d" % q, shape, BF16)
             nc.scalar.activation(planar[q][:, t, :], acts[q][:, t, :], COPY, scale=sm_t[:, t : t + 1])
 
         def interleave(q):
@@ -247,7 +251,10 @@ def tile_list_msg_gelu_res_resL_kernel(
 
         def quantise_hidden(q):
             shape = [P, QUARTER]
-            codes[q] = lay("codes0", shape, U32, RAW1 + LAP) if q == 0 else fresh("codes%d" % q, shape, U32)
+            if q < 2:
+                codes[q] = lay("codes%d" % q, shape, U32, (RAW1 + LAP, RAW3)[q])
+            else:
+                codes[q] = fresh("codes%d" % q, shape, U32)
             nc.vector.quantize_mx(
                 out=codes[q][:].bitcast(FP8X4), scales=h_scales[:, q * QUARTER : (q + 1) * QUARTER], in_=h[q][:]
             )
@@ -289,7 +296,7 @@ def tile_list_msg_gelu_res_resL_kernel(
                     into[:, cols], res[nt][:].indirect(entries(dst_list, half * HALF, HALF)), edge_w[:, cols], MULT
                 )
 
-        def pieces(tiles, edge_tiles, k, tag=""):
+        def pieces(tiles, edge_tiles, k, tag="", offset=None):
             width = len(edge_tiles) * P
             first = edge_tiles[0] * P
             t_ps = bank(k, [P, len(tiles) * width])
@@ -298,7 +305,10 @@ def tile_list_msg_gelu_res_resL_kernel(
                     t_ps[:, slot * P : (slot + 1) * P], scaled[e][:, nt * P : (nt + 1) * P], identity[:]
                 )
             name = "y_%d_%d" % (tiles[0], edge_tiles[0])
-            y = keep.tile([P, len(tiles) * width], F32, name=name, tag=tag or name, align_bytes=64)
+            if offset is None:
+                y = keep.tile([P, len(tiles) * width], F32, name=name, tag=tag or name, align_bytes=64)
+            else:
+                y = lay(name, [P, len(tiles) * width], F32, offset)
             nc.scalar.copy(y[:], t_ps[:])
             for slot, nt in enumerate(tiles):
                 nc.vector.tensor_tensor(
@@ -309,8 +319,8 @@ def tile_list_msg_gelu_res_resL_kernel(
         for nt in range(2):
             residual(nt, fresh("own%d" % nt, [P, J], F32))
         hidden(0)
-        windows[3] = lay("window3", [P, T], F32, WINDOW3)
-        nc.gpsimd.memset(windows[3][:], 0.0)
+        windows[2] = lay("window2", [P, T], F32, WINDOW3)
+        nc.gpsimd.memset(windows[2][:], 0.0)
         residual(2, lay("own2", [P, J], F32, OWN2))
         residual(3, fresh("own3", [P, J], F32))
         for t in range(PACK):
@@ -318,16 +328,17 @@ def tile_list_msg_gelu_res_resL_kernel(
         message(0, 0)
         for t in range(PACK):
             smooth(1, t)
-        pieces((0, 1, 2, 3), (0,), 2)
+        pieces((3,), (0,), 2)
         interleave(1)
         quantise_hidden(1)
+        pieces((0, 1, 2), (0,), 3, offset=RAW3 + 2 * KIB)
         message(1, 1)
-        pieces((0, 1, 2, 3), (1,), 3)
+        pieces((3, 0, 1, 2), (1,), 2)
         message(2, 0)
         message(3, 1)
-        pieces((0,), (2, 3), 2)
+        pieces((0,), (2, 3), 3)
         hidden(2)
-        pieces((1, 2), (2, 3), 3, "planar2")
+        pieces((1, 2), (2, 3), 2, offset=RAW3 + 4 * KIB)
         hidden(3)
         pieces((3,), (2, 3), 0, "planar3")
         message(4, 4)

@@ -107,8 +107,8 @@ def tile_list_msg_gelu_res_resL_kernel(
             else:
                 rounded[u] = fresh("rounded%d" % u, [P, R * PACK], BF16)
             nc.scalar.copy(
-                rounded[u][:].rearrange("p (t m i) -> p m t i", t=PACK, i=PACK),
-                raw[:].rearrange("p i (m t) -> p m t i", t=PACK),
+                rounded[u][:].rearrange("p (t m i) -> p m i t", t=PACK, i=PACK),
+                raw[:].rearrange("p i (m t) -> p m i t", t=PACK),
             )
 
         def load_wd_scales(i, scales):

@@ -336,19 +336,19 @@ def tile_list_msg_gelu_res_resL_kernel(
         pieces((3, 0, 1, 2), (1,), 2)
         message(2, 0)
         message(3, 1)
-        pieces((0,), (2, 3), 3)
         hidden(2)
-        pieces((1, 2), (2, 3), 2, offset=RAW3 + 4 * KIB)
+        pieces((0, 1), (2, 3), 3, offset=RAW3 + 4 * KIB)
+        pieces((2,), (2, 3), 2)
         hidden(3)
         pieces((3,), (2, 3), 0, "planar3")
         message(4, 4)
         message(5, 5)
-        for nt in range(2):
-            pieces((nt,), (4, 5), 1 + nt)
+        pieces((0, 1), (4, 5), 1)
+        pieces((2,), (4, 5), 2)
         message(6, 1)
         message(7, 2)
-        pieces((0, 1), (6, 7), 6)
+        pieces((0, 1), (6, 7), 3)
+        pieces((2,), (6, 7), 0)
+        pieces((3,), (4, 5, 6, 7), 4)
         for nt in range(N_TILES):
-            if nt >= 2:
-                pieces((nt,), (4, 5, 6, 7), nt + 1)
             nc.sync.dma_start(out=out[nt * P : (nt + 1) * P, :], in_=windows[nt][:])

@@ -38,11 +38,13 @@ PARTED_SECOND = RAW1 + 8 * KIB + LAP
 RAW2 = PARTED_SECOND + 4 * KIB - LAP
 RAW3 = RAW2 + 8 * KIB + LAP
 ROUNDED3 = RAW3 + 8 * KIB
-WINDOW2 = ROUNDED3 + 4 * KIB - LAP
-H0 = WINDOW2 + 8 * KIB
-WINDOW3 = H0 + 2 * KIB - LAP
-PLANAR0 = WINDOW3 + 8 * KIB
+WINDOW0 = ROUNDED3 + 4 * KIB - LAP
+H0 = WINDOW0 + 8 * KIB
+WINDOW1 = H0 + 2 * KIB - LAP
+PLANAR0 = WINDOW1 + 8 * KIB
 OWN2 = PLANAR0 + 2 * KIB - LAP
+H1 = OWN2 + 4 * KIB
+WINDOW2 = H1 + 2 * KIB - LAP
 
 
 def tile_list_msg_gelu_res_resL_kernel(
@@ -80,12 +82,14 @@ def tile_list_msg_gelu_res_resL_kernel(
         wd_s = fresh("wd_s", [P, 2, N], U8)
         nc.gpsimd.memset(wd_s[:].rearrange("p i n -> p (i n)").bitcast(I32), 0)
         shifted = fresh("shifted", [P, 2 * J], U8)
-        windows = {nt: fresh("window%d" % nt, [P, T], F32) for nt in (0, 3)}
-        nc.gpsimd.memset(windows[3][:], 0.0)
-        for words in (windows[0][:], shifted[:].bitcast(I32)):
-            cut = words.shape[1] // 2 - 1
-            nc.vector.memset(words[:, 0:cut], 0)
-            nc.vector.memset(words[:, cut : words.shape[1]], 0)
+        nc.gpsimd.memset(shifted[:].bitcast(I32), 0)
+        windows = {3: fresh("window3", [P, T], F32)}
+        nc.vector.memset(windows[3][:, 0 : T // 2 - 1], 0.0)
+        nc.vector.memset(windows[3][:, T // 2 - 1 : T], 0.0)
+
+        def late_window(nt, offset):
+            windows[nt] = lay("window%d" % nt, [P, T], F32, offset)
+            nc.gpsimd.memset(windows[nt][:], 0.0)
 
         nc.sync.dma_start(src_list[:], offs)
         nc.sync.dma_start(dst_list[:], offs2)
@@ -196,8 +200,7 @@ def tile_list_msg_gelu_res_resL_kernel(
         quantise_weight(2)
         part(1, lay("parted_second", [P, 2 * PASSES * 2 * HALF], U8, PARTED_SECOND))
         quantise_weight(3)
-        windows[1] = lay("window1", [P, T], F32, WINDOW2)
-        nc.gpsimd.memset(windows[1][:], 0.0)
+        late_window(0, WINDOW0)
 
         def project(half, steps):
             banks = [bank(half * PACK + t, [P, HALF]) for t in range(PACK)]
@@ -243,7 +246,7 @@ def tile_list_msg_gelu_res_resL_kernel(
 
         def interleave(q):
             shape = [P, QUARTER * PACK]
-            h[q] = lay("h0", shape, BF16, H0) if q == 0 else fresh("h%d" % q, shape, BF16)
+            h[q] = lay("h%d" % q, shape, BF16, (H0, H1)[q]) if q < 2 else fresh("h%d" % q, shape, BF16)
             nc.scalar.copy(
                 h[q][:].rearrange("p (c i t) -> p c t i", i=4, t=PACK),
                 planar[q][:].rearrange("p t (c i) -> p c t i", i=4),
@@ -319,8 +322,7 @@ def tile_list_msg_gelu_res_resL_kernel(
         for nt in range(2):
             residual(nt, fresh("own%d" % nt, [P, J], F32))
         hidden(0)
-        windows[2] = lay("window2", [P, T], F32, WINDOW3)
-        nc.gpsimd.memset(windows[2][:], 0.0)
+        late_window(1, WINDOW1)
         residual(2, lay("own2", [P, J], F32, OWN2))
         residual(3, fresh("own3", [P, J], F32))
         for t in range(PACK):
@@ -331,9 +333,11 @@ def tile_list_msg_gelu_res_resL_kernel(
         pieces((3,), (0,), 2)
         interleave(1)
         quantise_hidden(1)
-        pieces((0, 1, 2), (0,), 3, offset=RAW3 + 2 * KIB)
+        late_window(2, WINDOW2)
+        pieces((0, 1), (0,), 3, offset=RAW3 + 2 * KIB)
         message(1, 1)
-        pieces((3, 0, 1, 2), (1,), 2)
+        pieces((3, 0, 1), (1,), 2)
+        pieces((2,), (0, 1), 3)
         message(2, 0)
         message(3, 1)
         hidden(2)

@@ -32,7 +32,8 @@ KIB = 1024
 LAP = 64
 TAB_S = 0
 RAW0 = TAB_S + 3 * KIB
-PICKED_LAST = RAW0 + 8 * KIB
+RES0 = RAW0 + 6 * KIB
+PICKED_LAST = RES0 + 8 * KIB
 RAW1 = PICKED_LAST + 2 * KIB - LAP
 PARTED_SECOND = RAW1 + 8 * KIB + LAP
 RAW2 = PARTED_SECOND + 4 * KIB - LAP
@@ -45,6 +46,7 @@ PLANAR0 = WINDOW1 + 8 * KIB
 OWN2 = PLANAR0 + 2 * KIB - LAP
 H1 = OWN2 + 4 * KIB
 WINDOW2 = H1 + 2 * KIB - LAP
+ROUNDED0 = WINDOW2 + 8 * KIB
 
 
 def tile_list_msg_gelu_res_resL_kernel(
@@ -75,7 +77,7 @@ def tile_list_msg_gelu_res_resL_kernel(
 
         tab_s = lay("tab_s", [P, T], U8, TAB_S)
         nc.gpsimd.memset(tab_s[:].bitcast(I32), 0)
-        edge_rows = fresh("edge_rows", [P, P], F32)
+        edge_rows = lay("edge_rows", [P, P], F32, ROUNDED0)
         nc.gpsimd.memset(edge_rows[:], 0.0)
         identity = fresh("identity", [P, P], F32)
         make_identity(nc, identity[:])
@@ -106,8 +108,8 @@ def tile_list_msg_gelu_res_resL_kernel(
             nc.sync.dma_start(
                 out=raw[:], in_=(ws, wt)[i][a * K_PASS : (a + 1) * K_PASS, :].rearrange("(p i) r -> p i r", i=PACK)
             )
-            if u == WEIGHTS - 1:
-                rounded[u] = lay("rounded%d" % u, [P, R * PACK], BF16, ROUNDED3)
+            if u in (0, WEIGHTS - 1):
+                rounded[u] = lay("rounded%d" % u, [P, R * PACK], BF16, ROUNDED3 if u else ROUNDED0)
             else:
                 rounded[u] = fresh("rounded%d" % u, [P, R * PACK], BF16)
             nc.scalar.copy(
@@ -156,7 +158,7 @@ def tile_list_msg_gelu_res_resL_kernel(
         res = {}
 
         def load_state(nt):
-            res[nt] = lay("res%d" % nt, [P, T], F32, (RAW0, RAW1 + LAP, RAW2 + LAP, RAW3)[nt])
+            res[nt] = lay("res%d" % nt, [P, T], F32, (RES0, RAW1 + LAP, RAW2 + LAP, RAW3)[nt])
             nc.sync.dma_start(out=res[nt][:], in_=rT[nt * P : (nt + 1) * P, :])
 
         load_state(0)
@@ -192,9 +194,9 @@ def tile_list_msg_gelu_res_resL_kernel(
 
         quantise_weight(0)
         for i in range(2):
-            pick(i, 0, fresh("picked%d0" % i, [P, HALF], U32))
+            pick(i, 0, lay("picked%d0" % i, [P, HALF], U32, RAW0 + 2 * i * KIB))
         part(0, fresh("parted_first", [P, 2 * PASSES * 2 * HALF], U8))
-        pick(0, 1, fresh("picked01", [P, HALF], U32))
+        pick(0, 1, lay("picked01", [P, HALF], U32, RAW0 + 4 * KIB))
         quantise_weight(1)
         pick(1, 1, lay("picked11", [P, HALF], U32, PICKED_LAST))
         quantise_weight(2)

@@ -97,7 +97,7 @@ def tile_list_msg_gelu_res_resL_kernel(
         nc.sync.dma_start(dst_list[:], offs2)
         scale_rows = tab_scales.bitcast(I32).rearrange("a (q r) t -> r q a t", r=4)
         for r in range(4):
-            nc.sync.dma_start(out=tab_s[r:P:SHIFT, :].bitcast(I32), in_=scale_rows[r])
+            (nc.sync, nc.scalar)[r % 2].dma_start(out=tab_s[r:P:SHIFT, :].bitcast(I32), in_=scale_rows[r])
         nc.sync.dma_start(out=edge_rows[0 : J // P, :], in_=wgo[0].rearrange("(c p) -> c p", p=P))
 
         rounded = {}
@@ -188,8 +188,8 @@ def tile_list_msg_gelu_res_resL_kernel(
             for i in range(2):
                 parted[i, half] = into[:, i * PASSES * 2 * HALF : (i + 1) * PASSES * 2 * HALF]
                 nc.vector.tensor_copy(
-                    parted[i, half].bitcast(U16).rearrange("p (d j) -> p d j", d=PASSES),
-                    picked[i, half][:].bitcast(U16).rearrange("p (j d) -> p d j", d=PASSES),
+                    parted[i, half].bitcast(U16).rearrange("p (d c j) -> p c d j", d=PASSES, j=8),
+                    picked[i, half][:].bitcast(U16).rearrange("p (c j d) -> p c d j", d=PASSES, j=8),
                 )
 
         quantise_weight(0)
@@ -256,10 +256,7 @@ def tile_list_msg_gelu_res_resL_kernel(
 
         def quantise_hidden(q):
             shape = [P, QUARTER]
-            if q < 2:
-                codes[q] = lay("codes%d" % q, shape, U32, (RAW1 + LAP, RAW3)[q])
-            else:
-                codes[q] = fresh("codes%d" % q, shape, U32)
+            codes[q] = lay("codes1", shape, U32, RAW3) if q == 1 else fresh("codes%d" % q, shape, U32)
             nc.vector.quantize_mx(
                 out=codes[q][:].bitcast(FP8X4), scales=h_scales[:, q * QUARTER : (q + 1) * QUARTER], in_=h[q][:]
             )
@@ -293,12 +290,12 @@ def tile_list_msg_gelu_res_resL_kernel(
 
         own = {}
 
-        def residual(nt, into):
+        def residual(nt, into, width=J):
             own[nt] = into
-            for half in range(2):
-                cols = slice(half * HALF, (half + 1) * HALF)
+            for first in range(0, J, width):
+                cols = slice(first, first + width)
                 nc.vector.tensor_tensor(
-                    into[:, cols], res[nt][:].indirect(entries(dst_list, half * HALF, HALF)), edge_w[:, cols], MULT
+                    into[:, cols], res[nt][:].indirect(entries(dst_list, first, width)), edge_w[:, cols], MULT
                 )
 
         def pieces(tiles, edge_tiles, k, tag="", offset=None):
@@ -326,7 +323,7 @@ def tile_list_msg_gelu_res_resL_kernel(
         hidden(0)
         late_window(1, WINDOW1)
         residual(2, lay("own2", [P, J], F32, OWN2))
-        residual(3, fresh("own3", [P, J], F32))
+        residual(3, fresh("own3", [P, J], F32), HALF)
         for t in range(PACK):
             gelu(1, t)
         message(0, 0)

@@ -31,7 +31,7 @@ SHIFT = 16
 KIB = 1024
 LAP = 64
 TAB_S = 0
-RAW0 = TAB_S + 3 * KIB
+RAW0 = TAB_S + 2 * KIB
 RES0 = RAW0 + 6 * KIB
 PICKED_LAST = RES0 + 8 * KIB
 RAW1 = PICKED_LAST + 2 * KIB - LAP
@@ -163,11 +163,9 @@ def tile_list_msg_gelu_res_resL_kernel(
 
         load_state(0)
         wd4 = lay("wd4", [P, 2 * N], U8, TAB_S)
-        wd8 = lay("wd8", [P, N], I32, TAB_S + KIB)
         nc.sync.dma_start(out=wd4[:].bitcast(I32), in_=wd4_words[0].bitcast(I32))
-        nc.sync.dma_start(out=wd8[:], in_=wd8_words[0].rearrange("p n b -> p (n b)").bitcast(I32))
-        for nt in range(1, N_TILES):
-            load_state(nt)
+        load_state(1)
+        load_state(2)
 
         w_codes = {}
         w_scales = {}
@@ -201,6 +199,9 @@ def tile_list_msg_gelu_res_resL_kernel(
         pick(1, 1, lay("picked11", [P, HALF], U32, PICKED_LAST))
         quantise_weight(2)
         part(1, lay("parted_second", [P, 2 * PASSES * 2 * HALF], U8, PARTED_SECOND))
+        wd8 = lay("wd8", [P, N], I32, PICKED_LAST)
+        nc.sync.dma_start(out=wd8[:], in_=wd8_words[0].rearrange("p n b -> p (n b)").bitcast(I32))
+        load_state(3)
         quantise_weight(3)
         late_window(0, WINDOW0)
 

@@ -251,8 +251,8 @@ def tile_list_msg_gelu_res_resL_kernel(
             shape = [P, QUARTER * PACK]
             h[q] = lay("h%d" % q, shape, BF16, (H0, H1)[q]) if q < 2 else fresh("h%d" % q, shape, BF16)
             nc.scalar.copy(
-                h[q][:].rearrange("p (c i t) -> p c t i", i=4, t=PACK),
-                planar[q][:].rearrange("p t (c i) -> p c t i", i=4),
+                h[q][:].rearrange("p (c i t) -> p c t i", i=8, t=PACK),
+                planar[q][:].rearrange("p t (c i) -> p c t i", i=8),
             )
 
         def quantise_hidden(q):

from contextlib import ExitStack

import concourse.mybir as mybir
from concourse.masks import make_identity

K, R, N, T, J = 1024, 512, 512, 2048, 1024
FLOPS = 2 * J * (2 * K * R + 2 * R * N)

F32 = mybir.dt.float32
BF16 = mybir.dt.bfloat16
I32 = mybir.dt.int32
U32 = mybir.dt.uint32
U16 = mybir.dt.uint16
U8 = mybir.dt.uint8
FP8X4 = mybir.dt.float8_e4m3fn_x4
FP4X4 = mybir.dt.float4_e2m1fn_x4
GELU = mybir.ActivationFunctionType.Gelu_apprx_tanh
COPY = mybir.ActivationFunctionType.Copy
MULT = mybir.AluOpType.mult
ADD = mybir.AluOpType.add

P = 128
PACK = 4
K_PASS = P * PACK
PASSES = K // K_PASS
WEIGHTS = 2 * PASSES
N_TILES = N // P
HALF = J // 2
QUARTER = J // 4
SHIFT = 16
KIB = 1024
LAP = 64
TAB_S = 0
RAW0 = TAB_S + 2 * KIB
RES0 = RAW0 + 6 * KIB
PICKED_LAST = RES0 + 8 * KIB
RAW1 = PICKED_LAST + 2 * KIB - LAP
PARTED_SECOND = RAW1 + 8 * KIB + LAP
RAW2 = PARTED_SECOND + 4 * KIB - LAP
RAW3 = RAW2 + 8 * KIB + LAP
ROUNDED3 = RAW3 + 8 * KIB
WINDOW0 = ROUNDED3 + 4 * KIB - LAP
H0 = WINDOW0 + 8 * KIB
WINDOW1 = H0 + 2 * KIB - LAP
PLANAR0 = WINDOW1 + 8 * KIB
OWN2 = PLANAR0 + 2 * KIB - LAP
H1 = OWN2 + 4 * KIB
WINDOW2 = H1 + 2 * KIB - LAP
ROUNDED0 = WINDOW2 + 8 * KIB


def tile_list_msg_gelu_res_resL_kernel(
    tc, tab_words, tab_scales, ws, wt, sm, wd4_words, wd4_scales, wd8_words, wd8_scales, rT, wgo, offs, offs2, out
):
    nc = tc.nc
    with ExitStack() as ctx:
        lists = ctx.enter_context(tc.tile_pool(name="lists", bufs=1))
        keep = ctx.enter_context(tc.tile_pool(name="keep", bufs=1))
        laid = ctx.enter_context(tc.tile_pool(name="laid", bufs=1))
        psum = ctx.enter_context(tc.psum_pool(name="psum", bufs=1))

        def lay(name, shape, dtype, offset):
            return laid.tile(shape, dtype, name=name, offset=offset, align_bytes=64)

        def fresh(name, shape, dtype):
            return keep.tile(shape, dtype, name=name, align_bytes=64)

        def bank(k, shape):
            return psum.tile(shape, F32, name="bank", tag="bank%d" % k)

        src_list = lists.tile([P, J // 16], U16, name="src_list")
        dst_list = lists.tile([P, J // 16], U16, name="dst_list")
        both = (src_list, dst_list)

        def entries(one_list, first, count):
            return one_list[:, first // 16 : (first + count) // 16]

        tab_s = lay("tab_s", [P, T], U8, TAB_S)
        nc.gpsimd.memset(tab_s[:].bitcast(I32), 0)
        edge_rows = lay("edge_rows", [P, P], F32, ROUNDED0)
        nc.gpsimd.memset(edge_rows[:], 0.0)
        identity = fresh("identity", [P, P], F32)
        make_identity(nc, identity[:])
        wd_s = fresh("wd_s", [P, 2, N], U8)
        nc.gpsimd.memset(wd_s[:].rearrange("p i n -> p (i n)").bitcast(I32), 0)
        shifted = fresh("shifted", [P, 2 * J], U8)
        nc.gpsimd.memset(shifted[:].bitcast(I32), 0)
        windows = {3: fresh("window3", [P, T], F32)}
        nc.vector.memset(windows[3][:, 0 : T // 2 - 1], 0.0)
        nc.vector.memset(windows[3][:, T // 2 - 1 : T], 0.0)

        def late_window(nt, offset):
            windows[nt] = lay("window%d" % nt, [P, T], F32, offset)
            nc.gpsimd.memset(windows[nt][:], 0.0)

        nc.sync.dma_start(src_list[:], offs)
        nc.sync.dma_start(dst_list[:], offs2)
        scale_rows = tab_scales.bitcast(I32).rearrange("a (q r) t -> r q a t", r=4)
        for r in range(4):
            (nc.sync, nc.scalar)[r % 2].dma_start(out=tab_s[r:P:SHIFT, :].bitcast(I32), in_=scale_rows[r])
        nc.sync.dma_start(out=edge_rows[0 : J // P, :], in_=wgo[0].rearrange("(c p) -> c p", p=P))

        rounded = {}

        def load_weight(u):
            a, i = divmod(u, 2)
            raw = lay("raw%d" % u, [P, PACK, R], F32, (RAW0, RAW1, RAW2, RAW3)[u])
            nc.sync.dma_start(
                out=raw[:], in_=(ws, wt)[i][a * K_PASS : (a + 1) * K_PASS, :].rearrange("(p i) r -> p i r", i=PACK)
            )
            if u in (0, WEIGHTS - 1):
                rounded[u] = lay("rounded%d" % u, [P, R * PACK], BF16, ROUNDED3 if u else ROUNDED0)
            else:
                rounded[u] = fresh("rounded%d" % u, [P, R * PACK], BF16)
            nc.scalar.copy(
                rounded[u][:].rearrange("p (t m i) -> p m i t", t=PACK, i=PACK),
                raw[:].rearrange("p i (m t) -> p m i t", t=PACK),
            )

        def load_wd_scales(i, scales):
            rows = scales[0].bitcast(I32).rearrange("(q r) n -> r q n", r=4)
            for r in range(4):
                nc.sync.dma_start(out=wd_s[r:P:32, i, :].bitcast(I32), in_=rows[r])

        edge_col = fresh("edge_col", [P, J // P], F32)
        col_ps = bank(4, [P, P])
        nc.tensor.transpose(col_ps[:], edge_rows[:], identity[:])
        nc.scalar.copy(edge_col[:], col_ps[:, 0 : J // P])

        load_weight(0)
        tab_w = fresh("tab_w", [P, T], I32)
        nc.sync.dma_start(out=tab_w[:], in_=tab_words[0].rearrange("p t b -> p (t b)").bitcast(I32))

        spread_ps = [bank(5 + half, [P, HALF]) for half in range(2)]
        for c in range(J // P):
            half, slot = divmod(c, PACK)
            nc.tensor.transpose(
                spread_ps[half][:, slot * P : (slot + 1) * P], edge_col[:, c : c + 1].to_broadcast([P, P]), identity[:]
            )
        edge_w = fresh("edge_w", [P, J], F32)
        for half in range(2):
            nc.scalar.copy(edge_w[:, half * HALF : (half + 1) * HALF], spread_ps[half][:])

        load_weight(1)
        load_wd_scales(0, wd4_scales)
        load_weight(2)
        load_wd_scales(1, wd8_scales)
        load_weight(3)
        sm_t = fresh("sm_t", [P, PACK], F32)
        nc.sync.dma_start(out=sm_t[:], in_=sm.rearrange("(p t) -> p t", t=PACK))

        first_plane = fresh("first_plane", [P, 2 * J], U8)
        for i in range(2):
            nc.vector.tensor_copy(first_plane[:, i * J : (i + 1) * J], tab_s[:].indirect(both[i][:]))
        nc.sync.dma_start(out=shifted[0 : P - SHIFT, :].bitcast(I32), in_=first_plane[SHIFT:P, :].bitcast(I32))
        planes = (first_plane, shifted)

        res = {}

        def load_state(nt):
            res[nt] = lay("res%d" % nt, [P, T], F32, (RES0, RAW1 + LAP, RAW2 + LAP, RAW3)[nt])
            nc.sync.dma_start(out=res[nt][:], in_=rT[nt * P : (nt + 1) * P, :])

        load_state(0)
        wd4 = lay("wd4", [P, 2 * N], U8, TAB_S)
        nc.sync.dma_start(out=wd4[:].bitcast(I32), in_=wd4_words[0].bitcast(I32))
        load_state(1)
        load_state(2)

        w_codes = {}
        w_scales = {}

        def quantise_weight(u):
            w_codes[u] = fresh("w_codes%d" % u, [P, R], U32)
            w_scales[u] = fresh("w_scales%d" % u, [P, R], U8)
            nc.vector.quantize_mx(out=w_codes[u][:].bitcast(FP8X4), scales=w_scales[u][:], in_=rounded[u][:])

        picked = {}
        parted = {}

        def pick(i, half, into):
            picked[i, half] = into
            nc.vector.tensor_copy(into[:], tab_w[:].bitcast(U32).indirect(entries(both[i], half * HALF, HALF)))

        def part(half, into):
            for i in range(2):
                parted[i, half] = into[:, i * PASSES * 2 * HALF : (i + 1) * PASSES * 2 * HALF]
                nc.vector.tensor_copy(
                    parted[i, half].bitcast(U16).rearrange("p (d c j) -> p c d j", d=PASSES, j=8),
                    picked[i, half][:].bitcast(U16).rearrange("p (c j d) -> p c d j", d=PASSES, j=8),
                )

        quantise_weight(0)
        for i in range(2):
            pick(i, 0, lay("picked%d0" % i, [P, HALF], U32, RAW0 + 2 * i * KIB))
        part(0, fresh("parted_first", [P, 2 * PASSES * 2 * HALF], U8))
        pick(0, 1, lay("picked01", [P, HALF], U32, RAW0 + 4 * KIB))
        quantise_weight(1)
        pick(1, 1, lay("picked11", [P, HALF], U32, PICKED_LAST))
        quantise_weight(2)
        part(1, lay("parted_second", [P, 2 * PASSES * 2 * HALF], U8, PARTED_SECOND))
        wd8 = lay("wd8", [P, N], I32, PICKED_LAST)
        nc.sync.dma_start(out=wd8[:], in_=wd8_words[0].rearrange("p n b -> p (n b)").bitcast(I32))
        load_state(3)
        quantise_weight(3)
        late_window(0, WINDOW0)

        def project(half, steps):
            banks = [bank(half * PACK + t, [P, HALF]) for t in range(PACK)]
            for n, (u, t) in enumerate(steps):
                a, i = divmod(u, 2)
                start = a * HALF * 2
                mine = [v for v, s in steps if s == t]
                nc.tensor.matmul_mx(
                    out=banks[t][:],
                    lhsT=w_codes[u][:, t * P : (t + 1) * P].bitcast(FP8X4),
                    lhsT_scale=w_scales[u][:, t * P : (t + 1) * P],
                    rhs=parted[i, half][:, start : start + 2 * HALF].bitcast(FP4X4),
                    rhs_scale=planes[a][:, i * J + half * HALF : i * J + (half + 1) * HALF],
                    start=(u == mine[0]),
                    stop=(u == mine[-1]),
                )
            return banks

        first_banks = project(0, [(u, t) for u in range(WEIGHTS) for t in range(PACK)])
        second_banks = project(1, [(u, t) for t in range(PACK) for u in reversed(range(WEIGHTS))])

        h_scales = fresh("h_scales", [P, J], U8)
        acts = {}
        planar = {}
        h = {}
        codes = {}

        def gelu(q, t):
            if q not in acts:
                shape = [P, PACK, QUARTER]
                acts[q] = lay("acts3", shape, F32, ROUNDED3 - LAP) if q == 3 else fresh("acts%d" % q, shape, F32)
            inside = (q % 2) * QUARTER
            nc.scalar.activation(acts[q][:, t, :], (first_banks, second_banks)[q // 2][t][:, inside : inside + QUARTER], GELU)

        def smooth(q, t):
            if q not in planar:
                shape = [P, PACK, QUARTER]
                if q % 2 == 0:
                    planar[q] = lay("planar%d" % q, shape, BF16, (PLANAR0, RAW3 + 4 * KIB)[q // 2])
                else:
                    planar[q] = fresh("planar%d" % q, shape, BF16)
            nc.scalar.activation(planar[q][:, t, :], acts[q][:, t, :], COPY, scale=sm_t[:, t : t + 1])

        def interleave(q):
            shape = [P, QUARTER * PACK]
            h[q] = lay("h%d" % q, shape, BF16, (H0, H1)[q]) if q < 2 else fresh("h%d" % q, shape, BF16)
            nc.scalar.copy(
                h[q][:].rearrange("p (c i t) -> p c t i", i=8, t=PACK),
                planar[q][:].rearrange("p t (c i) -> p c t i", i=8),
            )

        def quantise_hidden(q):
            shape = [P, QUARTER]
            codes[q] = lay("codes1", shape, U32, RAW3) if q == 1 else fresh("codes%d" % q, shape, U32)
            nc.vector.quantize_mx(
                out=codes[q][:].bitcast(FP8X4), scales=h_scales[:, q * QUARTER : (q + 1) * QUARTER], in_=h[q][:]
            )

        def hidden(q):
            for t in range(PACK + 1):
                if t < PACK:
                    gelu(q, t)
                if t > 0:
                    smooth(q, t - 1)
            interleave(q)
            quantise_hidden(q)

        scaled = {}

        def message(e, k):
            inside = (e % 2) * P
            y_ps = bank(k, [P, N])
            lhsT = codes[e // 2][:, inside : inside + P].bitcast(FP8X4)
            lhsT_scale = h_scales[:, e * P : (e + 1) * P]
            nc.tensor.matmul_mx(
                out=y_ps[:], lhsT=lhsT, lhsT_scale=lhsT_scale,
                rhs=wd4[:].bitcast(FP4X4), rhs_scale=wd_s[:, 0, :], start=True, stop=False,
            )
            nc.tensor.matmul_mx(
                out=y_ps[:], lhsT=lhsT, lhsT_scale=lhsT_scale,
                rhs=wd8[:].bitcast(FP8X4), rhs_scale=wd_s[:, 1, :], start=False, stop=True,
            )
            scaled[e] = fresh("scaled%d" % e, [P, N], F32)
            nc.scalar.activation(scaled[e][:], y_ps[:], COPY, scale=edge_col[:, e : e + 1])

        own = {}

        def residual(nt, into, width=J):
            own[nt] = into
            for first in range(0, J, width):
                cols = slice(first, first + width)
                nc.vector.tensor_tensor(
                    into[:, cols], res[nt][:].indirect(entries(dst_list, first, width)), edge_w[:, cols], MULT
                )

        def pieces(tiles, edge_tiles, k, tag="", offset=None):
            width = len(edge_tiles) * P
            first = edge_tiles[0] * P
            t_ps = bank(k, [P, len(tiles) * width])
            for slot, (nt, e) in enumerate([(nt, e) for nt in tiles for e in edge_tiles]):
                nc.tensor.transpose(
                    t_ps[:, slot * P : (slot + 1) * P], scaled[e][:, nt * P : (nt + 1) * P], identity[:]
                )
            name = "y_%d_%d" % (tiles[0], edge_tiles[0])
            if offset is None:
                y = keep.tile([P, len(tiles) * width], F32, name=name, tag=tag or name, align_bytes=64)
            else:
                y = lay(name, [P, len(tiles) * width], F32, offset)
            nc.scalar.copy(y[:], t_ps[:])
            for slot, nt in enumerate(tiles):
                nc.vector.tensor_tensor(
                    windows[nt][:].indirect(entries(dst_list, first, width)),
                    y[:, slot * width : (slot + 1) * width], own[nt][:, first : first + width], ADD,
                )

        for nt in range(2):
            residual(nt, fresh("own%d" % nt, [P, J], F32))
        hidden(0)
        late_window(1, WINDOW1)
        residual(2, lay("own2", [P, J], F32, OWN2))
        residual(3, fresh("own3", [P, J], F32), HALF)
        for t in range(PACK):
            gelu(1, t)
        message(0, 0)
        for t in range(PACK):
            smooth(1, t)
        pieces((3,), (0,), 2)
        interleave(1)
        quantise_hidden(1)
        late_window(2, WINDOW2)
        pieces((0, 1), (0,), 3, offset=RAW3 + 2 * KIB)
        message(1, 1)
        pieces((3, 0, 1), (1,), 2)
        pieces((2,), (0, 1), 3)
        message(2, 0)
        message(3, 1)
        hidden(2)
        pieces((0, 1), (2, 3), 3, offset=RAW3 + 4 * KIB)
        pieces((2,), (2, 3), 2)
        hidden(3)
        pieces((3,), (2, 3), 0, "planar3")
        message(4, 4)
        message(5, 5)
        pieces((0, 1), (4, 5), 1)
        pieces((2,), (4, 5), 2)
        message(6, 1)
        message(7, 2)
        pieces((0, 1), (6, 7), 3)
        pieces((2,), (6, 7), 0)
        pieces((3,), (4, 5, 6, 7), 4)
        for nt in range(N_TILES):
            nc.sync.dma_start(out=out[nt * P : (nt + 1) * P, :], in_=windows[nt][:])
